import numpy as np, ml_dtypes
CORES = [6,15,38,47]
N = 4
BF = ml_dtypes.bfloat16
def gentries(a):
    return np.ascontiguousarray(a.reshape(8, 16, -1).transpose(0, 2, 1)).reshape(8, -1)
def gtable(e):
    e = np.asarray(e); return np.ascontiguousarray(e.reshape(8, -1, 16).transpose(0, 2, 1)).reshape(128, -1).astype(np.int32)
W, C, T, S = 4096, 256, 4, 1
K = 16 * C; H = 8 * C
EX = np.exp(-0.015625 * np.arange(256))
def pack(Y, R, L, D, F):
    return {"wl": np.ascontiguousarray(Y.reshape(N, 128, W)).astype(np.float32).astype(BF), "rc": np.ascontiguousarray(R.reshape(N, 128, K)).astype(np.float32).astype(BF),
            "nm": np.stack([gtable(a) for a in L]), "dn": np.ascontiguousarray(D).astype(np.int32), "pl": np.ascontiguousarray(F).astype(np.int32)}
def names(rng):
    return np.ascontiguousarray(np.argsort(rng.random((N, 8, 2, W)), axis=-1)[..., :H]).reshape(N, 8, K)
def flows(rng):
    return np.argsort(rng.random((N, 8, W)), axis=-1)
def records(rng, k):
    v = rng.integers(0, 256, (N, 8, 16, k)); v[:, :, :15] = v[:, :, :15] >> rng.integers(0, 2, (N, 8, 1, k)); v[:, :, 15] = rng.integers(0, 160, (N, 8, k))
    return v * (rng.random((N, 8, 1, k)) > 0.125)
def thin(rng, R):
    share = rng.choice(np.array([0.0, 0.0, 0.25, 0.5]), (N, 8, 1, C, 1))
    return (R.reshape(N, 8, 16, C, 16) * (rng.random((N, 8, 1, C, 16)) >= share)).reshape(N, 8, 16, K)
def steady(rng, size, lo, hi):
    v = np.zeros((N, 8, 16, K), np.int64); v[:, :, :15] = size * (1 + np.argsort(rng.random((N, 8, 15, K)), axis=2)); v[:, :, 15] = rng.integers(lo, hi, (N, 8, K))
    return v
def alive(rng, m):
    return (np.argsort(rng.random((N, 8, C, 16)), axis=3) < m[..., None]).reshape(N, 8, 1, K)
def lanes(a):
    return np.repeat(a, 16, axis=2)[:, :, None, :]
def mixed(rng, k):
    v = 255 * rng.integers(0, 2, (N, 8, 16, k)); t = rng.integers(0, 5, (N, 8, 1, k))
    v = np.where(t == 0, 0, np.where((t == 1) | (t == 2), 255, v)); t = t[:, :, 0]
    v[:, :, 15] = np.where(t == 2, 0, np.where(t == 4, 255, v[:, :, 15]))
    return v
def strong(rng):
    a = rng.integers(130, 231, (N, 8, C)); c = np.repeat(a, 16, axis=2) + (rng.random((N, 8, K)) < 0.25).astype(np.int64)
    b = (16 * c + rng.integers(0, 9, (N, 8, K)))[:, :, None, :]; e = rng.integers(0, 4, (N, 8, 15, K)); o = np.argsort(rng.random((N, 8, 15, K)), axis=2)
    v = np.zeros((N, 8, 16, K), np.int64); v[:, :, :15] = b // 15 + (o < b % 15).astype(np.int64) + e - np.roll(e, 1, axis=2); v[:, :, 15] = c
    F = 256 * a + rng.integers(-1, 2, (N, 8, C)); F[..., C - 1] = 256 * a[..., C - 1] + 1
    return v, F
def setup_inputs(rng):
    return pack(records(rng, W), thin(rng, records(rng, K)), names(rng), flows(rng), rng.integers(0, 14001, (N, 8, C)))
def setup_inputs_spread(rng):
    def uneven(k):
        v = np.exp2(2 + 6 * rng.random((N, 8, 1, k))) * rng.random((N, 8, 16, k)); v[:, :, 15] = np.exp2(3 + 5 * rng.random((N, 8, k))) * rng.random((N, 8, k))
        return np.minimum(np.floor(v), 255)
    F = np.minimum(np.floor(np.exp2(16 * rng.random((N, 8, C)))), 61200)
    return pack(uneven(W), uneven(K), names(rng), flows(rng), F)
def setup_inputs_ends(rng):
    mid = 1 + rng.permutation(W - 2); P = np.concatenate([np.array([0, W - 1]), mid[:W // 2 - 2]]); Q = mid[W // 2 - 2:]
    fc = np.zeros(C, bool)
    fc[np.concatenate([np.array([0]), 1 + rng.permutation(C // 2 - 1)])[:C // 4]] = True
    fc[C - 1 - np.concatenate([np.array([0]), 1 + rng.permutation(C // 2 - 1)])[:C // 4]] = True
    fl = np.repeat(fc, 16); L = np.zeros((N, 8, K), np.int64); D = np.zeros((N, 8, W), np.int64)
    for q in range(N):
        for g in range(8):
            D[q, g, P] = rng.permutation(P); D[q, g, Q] = rng.permutation(Q)
            for h in range(2):
                a = np.flatnonzero(fl[h * H:(h + 1) * H]) + h * H; b = np.flatnonzero(~fl[h * H:(h + 1) * H]) + h * H
                p = np.concatenate([P[:2], rng.permutation(P[2:])])[:len(a)]
                L[q, g, a] = p if h == 0 else p[::-1]
                if h == 1:
                    L[q, g, a[-1]] = W - 1; L[q, g, a[-2]] = 0
                L[q, g, b] = rng.permutation(Q)[:len(b)]
    Y = mixed(rng, W); Y[..., P] = 255
    R = np.where(fl[None, None, None, :], 255, mixed(rng, K))
    short = (rng.random((N, 8, C)) < 0.3) & fc[None, None, :]; short[..., 0] = False; short[..., C - 1] = False
    hole = (np.arange(16) == rng.integers(0, 16, (N, 8, C, 1))) & short[..., None]
    R = np.where(hole.reshape(N, 8, 1, K), 0, R)
    near = (rng.random((N, 8, C)) < 0.25) & fc[None, None, :] & ~short; near[..., 0] = False; near[..., C - 1] = False
    R = np.where(lanes(near), 255 - (rng.random((N, 8, 16, K)) < 0.3).astype(np.int64), R)
    F = np.where(fc[None, None, :], np.where(near, 0, 61200), 61200 * rng.integers(0, 2, (N, 8, C)))
    far = int(rng.integers(1, N - 1)); m = rng.integers(1, 17, (8, C)); m[:, 0] = 3; m[:, C - 1] = 16
    live = (np.argsort(rng.random((8, C, 16)), axis=2) < m[..., None]).reshape(8, 1, K)
    z = ((np.arange(16)[None, :, None] == rng.integers(0, 15, (8, 1, K))) & live).astype(np.int64)
    R[far] = np.where(fl[None, None, :], z, R[far]); F[far] = np.where(fc[None, :], 0, 61200)
    return pack(Y, R, L, D, F)
def setup_inputs_corners(rng):
    s = np.arange(W); L = np.zeros((N, 8, K), np.int64); D = np.zeros((N, 8, W), np.int64)
    for q in range(N):
        for g in range(8):
            o = rng.permutation(W); cyc = np.zeros(W, np.int64); cyc[o] = np.roll(o, -1)
            D[q, g] = (s, (s + 1) % W, W - 1 - s, (s - 1) % W, cyc)[(q + g) % 5]
            A, B = ((s[:H], s[W - H:]), (s[0:2 * H:2], s[1:2 * H:2]), (s[W - H:], s[W - H:]), (rng.permutation(W)[:H], rng.permutation(W)[:H]))[(q + 3 * g) % 4]
            L[q, g, :H] = rng.permutation(A); L[q, g, H:] = rng.permutation(B)
    Y = rng.integers(30, 256, (N, 8, 16, W))
    Y[:, :, 15] = np.where(rng.random((N, 8, W)) < 0.7, rng.integers(14, 17, (N, 8, W)), rng.integers(0, 256, (N, 8, W)))
    Y = Y * (rng.random((N, 8, 1, W)) > 0.03125)
    kc = rng.integers(0, 4, (N, 8, C)); m = rng.choice(np.array([0, 1, 2, 15, 16, 16]), (N, 8, C))
    R = np.where(lanes(kc) < 2, steady(rng, 2, 14, 17) * alive(rng, m), records(rng, K))
    F = m * rng.choice(np.array([224, 240]), (N, 8, C)) + rng.integers(0, 2, (N, 8, C))
    F = np.where(kc < 2, F, np.where(kc == 2, rng.integers(0, 14001, (N, 8, C)), 61200 * rng.integers(0, 2, (N, 8, C))))
    return pack(Y, R, L, D, F)
def setup_inputs_crowd(rng):
    o = rng.permutation(W); L = np.zeros((N, 8, K), np.int64)
    for q in range(N):
        for g in range(8):
            L[q, g, :H] = rng.permutation(o[:H]); j = H + rng.integers(0, H)
            if q % 2 == 0:
                L[q, g, H:] = rng.permutation(o[:H])
                if g % 2 == 1: L[q, g, j] = o[rng.integers(H, W)]
            else:
                L[q, g, H:] = rng.permutation(o[H:])[:H]
                if g % 2 == 1: L[q, g, j] = o[rng.integers(0, H)]
    Y = records(rng, W); R = thin(rng, records(rng, K)); F = rng.integers(0, 14001, (N, 8, C))
    high = rng.integers(250, 256, (N, 8, 16, W - H)); high[:, :, 15] = rng.integers(232, 256, (N, 8, W - H)); Y[..., o[H:]] = high
    v, u = strong(rng); R[1::2, :, :, H:] = v[1::2, :, :, H:]; F[1::2, :, C // 2:] = u[1::2, :, C // 2:]
    return pack(Y, R, L, flows(rng), F)
def setup_inputs_calm(rng):
    Y = rng.integers(64, 256, (N, 8, 16, W)); Y[:, :, 15] = rng.integers(60, 256, (N, 8, W))
    m = rng.integers(0, 4, (N, 8, C)); pc = rng.random((N, 8, C)) < 0.25
    R = np.where(lanes(pc), records(rng, K), steady(rng, 4, 60, 256) * alive(rng, m))
    F = np.where(pc, rng.integers(0, 14001, (N, 8, C)), 480 * m + rng.integers(0, 2, (N, 8, C)))
    return pack(Y, R, names(rng), flows(rng), F)
def check_ranges(d):
    bad = []
    for k, lo, hi in (("wl", 0, 255), ("rc", 0, 255), ("nm", 0, W - 1), ("dn", 0, W - 1), ("pl", 0, 61200)):
        v = np.asarray(d[k]).astype(np.float64)
        if not (np.min(v) >= lo and np.max(v) <= hi): bad.append("range of " + k)
        elif np.any(v != np.floor(v)): bad.append("whole numbers of " + k)
    if not bad:
        if np.any(np.sort(d["dn"], axis=-1) != np.arange(W)): bad.append("a row of dn doesn't hold every site once")
        s = np.sort(np.stack([gentries(a) for a in d["nm"]]).reshape(N, 8, 2, H), axis=-1)
        if np.any(s[..., 1:] == s[..., :-1]): bad.append("names of a half in nm repeat")
    return bad
def turn(a, t):
    b = np.roll(a, t, axis=0); h = b.shape[-1] // 2
    b[..., h:] = np.roll(b[..., h:], S * t, axis=1)
    return b
def reference(wl, rc, nm, dn, pl):
    Y = wl.astype(np.float32).astype(np.int32).reshape(N, 8, 16, W); R = rc.astype(np.float32).astype(np.int32).reshape(N, 8, 16, K)
    L = np.stack([gentries(a) for a in nm]).astype(np.int64); D = dn.astype(np.int64); F = np.repeat(pl.astype(np.int64), 16, axis=2)
    E = np.zeros((N, 8, 16, C))
    for t in range(1, T + 1):
        R = turn(R, t); L = turn(L, t); pull = turn(F, t)
        ca = np.zeros((N, 8, W), np.int32); cb = np.zeros((N, 8, W), np.int32)
        np.put_along_axis(ca, L[..., :H], 1, 2); np.put_along_axis(cb, L[..., H:], 1, 2); cnt = ca + cb
        y = np.take_along_axis(Y, L[:, :, None, :], 3)
        b = np.add.reduce(np.minimum(R, y)[:, :, :15], axis=2).astype(np.int64); bond = b > 0
        n = np.repeat(np.add.reduce(bond.reshape(N, 8, C, 16).astype(np.int64), axis=3), 16, axis=2)
        ly = 16 * y[:, :, 15].astype(np.int64); lr = 16 * R[:, :, 15].astype(np.int64); la = np.minimum(ly, lr)
        fail = bond & (n * np.minimum(b, la) < pull); hold = bond & ~fail
        x = np.where(hold[:, :, None, :], EX[np.abs(R - y)], 0.0)
        E = E + turn(np.add.reduce(x.reshape(N, 8, 16, C, 16), axis=4), -t)
        swap = fail & (np.take_along_axis(cnt, L, 2) == 1) & (b > la)
        lig = (swap & (ly <= lr))[:, :, None, :]; rec = (swap & (ly > lr))[:, :, None, :]
        v = np.where(lig, 0, np.where(rec, R, y)); R = np.where(lig, y, np.where(rec, 0, R))
        np.put_along_axis(Y, L[:, :, None, :], v, 3)
        if t < T:
            d = np.take_along_axis(D, L, 2)
            L = np.where(~hold & (np.take_along_axis(cnt, d, 2) == 0), d, L)
        R = turn(R, -t); L = turn(L, -t)
    a = Y.reshape(N, 128, 4, W // 4); r = R.reshape(N, 128, 4, K // 4)
    return {"ye": E.reshape(N, 128, C).astype(np.float32),
            "yw": (a[:, :, 0] - a[:, :, 1] + 2 * a[:, :, 2] - 2 * a[:, :, 3]).astype(np.float32),
            "yr": (r[:, :, 0] - r[:, :, 1] + 2 * r[:, :, 2] - 2 * r[:, :, 3]).astype(np.float32)}

def check_inputs(d):
    bad = list(check_ranges(d))
    if not bad:
        for name, y in reference(**d).items():
            for q in range(N):
                v = np.abs(np.asarray(y[q], np.float64)); s = np.sqrt(np.mean(v * v))
                if v.max() > 10 * s or s < 2.0 ** -3: bad.append('%s of rank %d is uneven or too small' % (name, q))
    return bad

@@ -1,0 +1,573 @@
+from concourse.bass import DstId, RemoteDMATransfer
+from concourse.mybir import AluOpType as OP, ActivationFunctionType as AF
+
+K = 4096
+H = 2048
+C = 256
+STEPS = 4
+PV, PZ, PRA, PY, PZ2, PRB, PZ3, PEND = 0, 4096, 4224, 8320, 12416, 12544, 16640, 16656
+YOFF = PY - PZ
+QO = (2, 3, 0, 1)
+
+SCRATCH = {
+    "P0": ("sbuf", [128, PEND], "bfloat16"), "P1": ("sbuf", [128, PEND], "bfloat16"),
+    "SB": ("sbuf", [128, 3 * H], "bfloat16"), "RS": ("sbuf", [128, K], "bfloat16"),
+    "W0": ("sbuf", [128, K], "bfloat16"), "W1": ("sbuf", [128, K], "bfloat16"), "WT": ("sbuf", [128, K], "bfloat16"),
+    "CS": ("sbuf", [128, K], "bfloat16"), "DN": ("sbuf", [128, K], "bfloat16"),
+    "D": ("sbuf", [128, K], "bfloat16"), "NN": ("sbuf", [128, K], "bfloat16"),
+    "GC": ("sbuf", [128, K], "bfloat16"), "GD": ("sbuf", [128, K], "bfloat16"),
+    "X": ("sbuf", [128, K], "float32"),
+    "YW": ("sbuf", [128, 1024], "float32"), "YR": ("sbuf", [128, 1024], "float32"), "YE": ("sbuf", [128, C], "float32"),
+    "SEL": ("sbuf", [128, 16 * 128], "bfloat16"), "EX": ("sbuf", [128, 8 * 144], "bfloat16"),
+    "BM": ("sbuf", [128, 144], "bfloat16"), "BD": ("sbuf", [128, 128], "bfloat16"),
+    "PBF": ("sbuf", [128, 256], "float32"), "PB1": ("sbuf", [128, 128], "bfloat16"), "PBM": ("sbuf", [128, 128], "bfloat16"),
+    "PB2": ("sbuf", [128, 256], "bfloat16"), "PBN": ("sbuf", [128, 256], "bfloat16"),
+    "KC": ("sbuf", [128, C], "bfloat16"), "RB": ("sbuf", [128, 256], "float32"),
+    "L": ("sbuf", [128, 256], "float32"), "XG": ("sbuf", [128, 256], "float32"),
+    "PI": ("sbuf", [128, 4], "int32"), "PF": ("sbuf", [128, 16], "float32"), "CB": ("sbuf", [128, 16], "bfloat16"),
+    "M16": ("sbuf", [128, 16], "float32"), "MS": ("sbuf", [128, 16], "bfloat16"),
+    "KD": ("sbuf", [128, C], "bfloat16"), "RL": ("sbuf", [128, C], "float32"), "E3": ("sbuf", [128, C], "float32"),
+    "JA": ("sbuf", [128, C], "float32"), "JB": ("sbuf", [128, C], "float32"),
+    "NI": ("sbuf", [128, C], "int32"), "DI": ("sbuf", [128, C], "int32"), "DJ": ("sbuf", [128, 2 * C], "int32"),
+    "DB": ("sbuf", [128, 2 * C], "bfloat16"), "PL": ("sbuf", [128, C], "int32"), "PLF": ("sbuf", [128, C], "float32"),
+    "FS": ("sbuf", [128, 4 * C], "float32"), "FL": ("sbuf", [128, 3 * C], "float32"), "EL": ("sbuf", [128, 3 * C], "float32"),
+    "NU": ("sbuf", [128, 4 * C], "uint16"), "NS": ("sbuf", [128, C], "uint16"),
+    "OU": ("sbuf", [128, C], "uint16"), "DU": ("sbuf", [128, C], "uint16"),
+    "RU": ("sbuf", [128, C], "uint16"), "VU": ("sbuf", [128, C], "uint16"),
+    "NF": ("sbuf", [128, C], "float32"), "DM": ("sbuf", [128, C], "float32"), "LA": ("sbuf", [128, C], "float32"),
+    "WM": ("sbuf", [128, C], "float32"), "G1": ("sbuf", [128, C], "float32"), "G2": ("sbuf", [128, C], "float32"),
+    "SN": ("sbuf", [128, C], "float32"), "Y1": ("sbuf", [128, C], "float32"), "Y2": ("sbuf", [128, C], "float32"),
+    "BO": ("sbuf", [128, C], "bfloat16"), "NH": ("sbuf", [128, C], "bfloat16"),
+}
+for _b in range(8):
+    SCRATCH["B%d" % _b] = ("psum", [128, 512], "float32")
+
+SEMAPHORES = (["qv", "qa", "qp", "qg"] + ["d%d" % i for i in range(40)] + ["l%d" % i for i in range(24)]
+              + ["rn%d" % t for t in range(1, 5)] + ["ra%d" % t for t in range(1, 5)] + ["rb%d" % t for t in range(1, 5)]
+              + ["rf%d" % t for t in range(1, 4)] + ["re%d" % t for t in range(1, 4)])
+
+
+def rank_program(g, core, T, topo):
+    rank = T.rank_of(core)
+    cores = list(T.cores)
+    n_ranks = len(cores)
+
+    def helper(c):
+        return [h for h in topo.cores_of(c) if h not in cores and topo.die(h) != topo.die(c)
+                and all(topo.may_write(h, d) for d in cores)][0]
+
+    def inner(c):
+        far = set(e for d in cores if d != c for e in topo.engines(c, d))
+        return [e for e in topo.engines(c, helper(c)) if e not in far]
+
+    if rank is None:
+        for r, c in enumerate(cores):
+            if helper(c) == core:
+                jobs = []
+                for t in range(1, STEPS + 1):
+                    r0 = PRA if t <= 2 else PRB
+                    jobs.append(("ra%d" % t, (T.P0, T.P1)[(t - 1) % 2][:, r0:r0 + H], T.P0[:, (t - 1) * H:t * H], r + 1))
+                    if t > 1:
+                        e = T.EL[:, (t - 2) * C:(t - 1) * C]
+                        jobs.append(("re%d" % (t - 1), e, e, r - t + 1))
+                total = 0
+                for sem, out, in_, to in jobs:
+                    dst = cores[to % n_ranks]
+                    rid, pid, _ = topo.addr(dst)
+                    g.wait_ge(T.sem[sem], len(inner(c)))
+                    g.remote_dma(out, in_, T.sem[sem], T.sem.l0, pid, rid, topo.mask(core, dst))
+                    total += len(topo.engines(core, dst))
+                g.wait_ge(T.sem.l0, total)
+        return
+    aide = helper(core)
+    aide_mask = sum(1 << e for e in inner(core))
+    Q = {"v": g.vector, "a": g.scalar, "p": g.tensor, "g": g, "s": g.sync}
+    cnt = {"v": 0, "a": 0, "p": 0, "g": 0, "d": 0, "l": 0}
+    seen = {q: {} for q in Q}
+    wr, rd, bank, final = {}, {}, {}, {}
+
+    def need(q, reads, writes, banks=()):
+        want = {}
+
+        def add(tok):
+            if tok is not None and not (q == "p" and tok[2] == "p"):
+                want[tok[0]] = max(want.get(tok[0], 0), tok[1])
+        for k in reads:
+            add(wr.get(k))
+        for k in writes:
+            add(wr.get(k))
+            for tok in rd.get(k, {}).values():
+                add(tok)
+        for b in banks:
+            for e, tok in bank.get(b, {}).items():
+                if e != q:
+                    add(tok)
+        for s, v in want.items():
+            if seen[q].get(s, 0) < v:
+                Q[q].wait_ge(T.sem[s], v)
+                seen[q][s] = v
+
+    def done(tok, reads, writes, banks=()):
+        for k in reads:
+            rd.setdefault(k, {})[tok[0]] = tok
+        for k in writes:
+            wr[k] = tok
+            rd[k] = {}
+        for b in banks:
+            bank.setdefault(b, {})[tok[2]] = tok
+        final[tok[0]] = tok[1]
+
+    def op(q, fn, reads, writes, banks=()):
+        need(q, reads, writes, banks)
+        ins = fn()
+        cnt[q] += 1
+        ins.then_inc(T.sem["q" + q], 1)
+        done(("q" + q, cnt[q], q), reads, writes, banks)
+
+    def dma(q, out, in_, reads, writes):
+        need(q, reads, writes)
+        s = "d%d" % cnt["d"]
+        cnt["d"] += 1
+        Q[q].dma_start(out, in_).then_inc(T.sem[s], 16)
+        done((s, 16, "d"), reads, writes)
+
+    def peer(t):
+        return cores[(rank + t) % n_ranks]
+
+    def lsem():
+        cnt["l"] += 1
+        return "l%d" % (cnt["l"] - 1)
+
+    def send(out, in_, dst, sem, reads):
+        need("g", reads, [])
+        s = lsem()
+        rid, pid, _ = topo.addr(dst)
+        g.remote_dma(out, in_, T.sem[sem], T.sem[s], pid, rid, aide_mask if dst == aide else topo.mask(core, dst))
+        done((s, len(inner(core) if dst == aide else topo.engines(core, dst)), "r"), reads, [])
+
+    def lands(sem, n, keys):
+        done((sem, n, "r"), [], keys)
+
+    def tt(out, a, b, o, reads, writes, banks=()):
+        op("v", lambda: g.vector.tensor_tensor(out, a, b, o), reads, writes, banks)
+
+    def ts(out, a, s1, s2, o0, o1, reads, writes, banks=()):
+        if o1 is None:
+            op("v", lambda: g.vector.tensor_scalar(out, a, s1, None, o0), reads, writes, banks)
+        else:
+            op("v", lambda: g.vector.tensor_scalar(out, a, s1, s2, o0, o1), reads, writes, banks)
+
+    def cp(q, out, a, reads, writes, banks=()):
+        if q == "v":
+            op("v", lambda: g.vector.tensor_copy(out, a), reads, writes, banks)
+        else:
+            op("a", lambda: g.scalar.activation(out, a, AF.Copy), reads, writes, banks)
+
+    def act(out, a, f, reads, writes, banks=(), **kw):
+        op("a", lambda: g.scalar.activation(out, a, f, **kw), reads, writes, banks)
+
+    def mm(items, reads, writes, banks):
+        def run():
+            ins = None
+            for it in items:
+                ins = g.tensor.matmul(*it)
+            return ins
+        op("p", run, reads, writes, banks)
+
+    def to_list(out, b, key, e, src, skeys, c0, c1, start, stop):
+        x = 144 * e + 15
+        mm([(out[:, c0:c1], T.EX[:, x - k:x - k + 128], src[:, 16 * c0 + k:16 * c1:16], start and k == 0, stop and k == 15)
+            for k in range(16)], skeys + ["EX%d" % e], [key], [b])
+    E_B, E_LA, E_SG, E_ID, E_FA, E_FB, E_OC, E_DN = range(8)
+
+    B = [T["B%d" % b] for b in range(8)]
+    p_b, p_nm = B[0][:, 0:C], B[0][:, C:C + 128]
+    p_la, t2 = B[1][:, 0:C], B[1][:, C:2 * C]
+    p_sg, p_n = B[2][:, 0:C], B[2][:, C:2 * C]
+    p_co, p_own = B[3][:, 0:C], B[3][:, C:2 * C]
+    p_d, p_oc = B[4][:, 0:C], B[4][:, C:2 * C]
+    t0, t1 = B[5][:, 0:C], B[5][:, C:2 * C]
+
+    src_n = len(topo.engines(peer(-1), core))
+    for t in range(1, STEPS + 1):
+        lands("rn%d" % t, src_n, ["NU%d" % t])
+        lands("ra%d" % t, len(topo.engines(helper(peer(-1)), core)), ["R%dq0" % t, "R%dq1" % t])
+        lands("rb%d" % t, src_n, ["R1q2", "R1q3"] if t == 1 else ["SB%d" % t])
+    for t in range(1, STEPS):
+        lands("rf%d" % t, 2, ["F%d" % t])
+        lands("re%d" % t, len(topo.engines(helper(peer(t)), core)), ["EL%d" % t])
+
+    dma("s", T.NI[:, 0:128], T.nm[:, 0:128], [], ["NIa"])
+    dma("a", T.NI[16:128, 128:256], T.nm[0:112, 128:256], [], ["NIb"])
+    dma("s", T.NI[0:16, 128:256], T.nm[112:128, 128:256], [], ["NIc"])
+    dma("a", T.RS[16:128, H:K], T.rc[0:112, H:K], [], ["RS2"])
+    dma("s", T.RS[0:16, H:K], T.rc[112:128, H:K], [], ["RS3"])
+    dma("s", T.RS[:, 0:H], T.rc[:, 0:H], [], ["RS0", "RS1"])
+    dma("s", T.DI[:], T.dn[:], [], ["DI"])
+    dma("s", T.PL[0:8, :], T.pl[:], [], ["PL"])
+    dma("s", T.P0[:, PY:PY + K], T.wl[:], [], ["Y0"])
+
+    op("g", lambda: g.iota(T.PI[:, 0:1], [[0, 1]], 0, 1), [], ["PI0"])
+    op("g", lambda: g.iota(T.L[:], [[1, 256]], 0, 0, allow_small_or_imprecise_dtypes=True), [], ["L"])
+    op("g", lambda: g.iota(T.XG[:], [[0, 2], [1, 8], [0, 16]], 0, 0, allow_small_or_imprecise_dtypes=True), [], ["XG"])
+
+    op("v", lambda: g.vector.memset(T.KC[:], 1024.0), [], ["KC"])
+    op("v", lambda: g.vector.memset(T.KD[:], 1.0 / 512), [], ["KD"])
+    for i, P in enumerate((T.P0, T.P1)):
+        op("v", lambda: g.vector.memset(P[:, PZ:PRA], 0.0), [], ["Za%d" % i])
+        op("v", lambda: g.vector.memset(P[:, PZ2:PRB], 0.0), [], ["Zb%d" % i])
+        op("v", lambda: g.vector.memset(P[:, PZ3:PEND], 0.0), [], ["Zc%d" % i])
+    ts(T.PI[:, 1:2], T.PI[:, 0:1], 15, None, OP.bitwise_and, None, ["PI0"], ["PI1"])
+    ts(T.PI[:, 2:3], T.PI[:, 0:1], 4, None, OP.arith_shift_right, None, ["PI0"], ["PI2"])
+    cp("v", T.PF[:, 0:3], T.PI[:, 0:3], ["PI0", "PI1", "PI2"], ["PF"])
+    ts(T.M16[:], T.L[:, 0:16], T.PF[:, 1:2], None, OP.is_equal, None, ["L", "PF"], ["M16"])
+    m = [T.M16[:, k:k + 1] for k in range(16)]
+    for i in range(4):
+        ts(T.CB[:, i:i + 1], m[2], float(1 << i), None, OP.mult, None, ["M16"], ["CB%d" % i])
+    ts(T.PF[:, 3:4], m[2], 16.0, m[1], OP.mult, OP.add, ["M16"], ["PF3"])
+    ts(T.CS[:, 0:128], T.L[:, 0:128], m[3], m[0], OP.mult, OP.add, ["L", "M16"], ["CS"])
+    ts(T.CB[:, 4:5], T.PF[:, 3:4], m[0], None, OP.subtract, None, ["PF3", "M16"], ["CB4"])
+    ts(T.CB[:, 5:6], m[2], m[3], None, OP.add, None, ["M16"], ["CB5"])
+    ts(T.CB[:, 6:7], m[2], float(PY // 128), None, OP.mult, None, ["M16"], ["CB6"])
+    ts(T.CB[:, 7:8], m[2], float(PY // 128 + 16), None, OP.mult, None, ["M16"], ["CB7"])
+    ts(T.PF[:, 4:5], m[2], m[3], None, OP.add, None, ["M16"], ["PF4"])
+    ts(T.PF[:, 5:6], T.PF[:, 2:3], 16.0, 15.0, OP.mult, OP.add, ["PF"], ["PF5"])
+    ts(T.MS[:], T.M16[:], 8192.0, None, OP.mult, None, ["M16"], ["MS"])
+    cp("v", T.NS[:], T.NI[:], ["NIa", "NIb", "NIc"], ["NSa", "NSb"])
+    send(T.NU[:, 0:C], T.NS[:], peer(1), "rn1", ["NSa", "NSb"])
+    send(T.P0[:, PRA + H:PRA + K], T.RS[:, H:K], peer(1), "rb1", ["RS2", "RS3"])
+    send(T.P0[:, 0:H], T.RS[:, 0:H], aide, "ra1", ["RS0", "RS1"])
+    for i in range(4):
+        w = 128 << i
+        ts(T.CS[:, w:2 * w], T.CS[:, 0:w], T.CB[:, i:i + 1], None, OP.add, None, ["CS", "CB%d" % i], ["CS"])
+    ts(T.W0[:, 0:H], T.CS[:, 0:H], T.CB[:, 5:6], T.CB[:, 6:7], OP.mult, OP.add, ["CS", "CB5", "CB6"], ["W0"])
+    ts(T.W0[:, H:K], T.CS[:, 0:H], T.CB[:, 5:6], T.CB[:, 7:8], OP.mult, OP.add, ["CS", "CB5", "CB7"], ["W0h"])
+    ts(T.BM[:], T.L[:, 0:144], T.PF[:, 5:6], None, OP.is_equal, None, ["L", "PF5"], ["BM"])
+    ts(T.PBF[:, 0:128], T.L[:, 0:128], T.PF[:, 0:1], None, OP.is_equal, None, ["L", "PF"], ["PBFa"])
+    ts(T.PBF[:, 128:256], T.L[:, 0:128], T.PF[:, 0:1], None, OP.is_equal, None, ["L", "PF"], ["PBFb"])
+    op("g", lambda: g.iota(T.DN[:], [[0, K]], 0, 0, allow_small_or_imprecise_dtypes=True), [], ["DN"])
+    idn = AF.Identity
+    act(T.PF[:, 12:13], m[8], idn, ["M16"], ["W7c"], scale=128.0, bias=m[12])
+    act(T.PF[:, 6:7], m[15], idn, ["M16"], ["W0c"], scale=-1.0, bias=1.0)
+    act(T.PF[:, 7:8], m[15], idn, ["M16"], ["W1c"], scale=16.0)
+    act(T.PF[:, 8:9], m[15], idn, ["M16"], ["W2c"], scale=-32768.0)
+    act(T.PF[:, 9:10], m[2], idn, ["M16"], ["W3c"], scale=128.0, bias=m[3])
+    act(T.PF[:, 10:11], m[0], idn, ["M16"], ["W6c"], bias=m[1])
+    act(T.PF[:, 11:12], T.PF[:, 1:2], idn, ["PF"], ["PF11"], bias=float(PRA - PZ))
+    act(T.JA[:], T.L[:], idn, ["L", "PF11"], ["JA"], scale=16.0, bias=T.PF[:, 11:12])
+    act(T.JB[:], T.JA[:], idn, ["JA"], ["JB"], bias=float(PRB - PRA))
+    act(T.CS[:, H:K], T.CS[:, 0:H], idn, ["CS", "CB4"], ["CSb"], bias=T.CB[:, 4:5])
+    act(T.WT[:], T.CS[:], idn, ["CS", "CSb", "PF4", "CB6"], ["WT"], scale=T.PF[:, 4:5], bias=T.CB[:, 6:7])
+    cols = [T.PF[:, 6:7], T.PF[:, 7:8], T.PF[:, 8:9], T.PF[:, 9:10], m[0], m[1], T.PF[:, 10:11], T.PF[:, 12:13]]
+    for e in range(8):
+        act(T.EX[:, 144 * e:144 * e + 144], T.BM[:], idn, ["BM", "M16", "W%dc" % e], ["EX%d" % e], scale=cols[e])
+    act(T.PB1[:], T.PBF[:, 0:128], idn, ["PBFa"], ["PB1"])
+    act(T.PBM[:], T.PBF[:, 0:128], idn, ["PBFa"], ["PBM"], scale=-1.0)
+    act(T.PBN[:], T.PBF[:], idn, ["PBFa", "PBFb"], ["PBN"], scale=-2.0)
+    act(T.PB2[:], T.PBF[:], idn, ["PBFa", "PBFb"], ["PB2"], scale=2.0)
+
+    def setup_rest():
+        ts(T.DJ[:, 0:C], T.DI[:], 7, None, OP.arith_shift_right, None, ["DI"], ["DJa"])
+        ts(T.DJ[:, C:2 * C], T.DI[:], 127, None, OP.bitwise_and, None, ["DI"], ["DJb"])
+        ts(T.DB[:, 0:C], T.DJ[:, 0:C], float(YOFF // 128), None, OP.add, None, ["DJa"], ["DBa"])
+        cp("v", T.DB[:, C:2 * C], T.DJ[:, C:2 * C], ["DJb"], ["DBb"])
+        dma("s", T.DN[8:128:16, :], T.DB[:, 0:C], ["DBa", "DN"], ["DNa"])
+        dma("s", T.DN[12:128:16, :], T.DB[:, C:2 * C], ["DBb", "DN"], ["DNb"])
+        dma("s", T.WT[8:128:16, :], T.DB[:, 0:C], ["DBa", "WT"], ["WTa"])
+        dma("s", T.WT[12:128:16, :], T.DB[:, C:2 * C], ["DBb", "WT"], ["WTb"])
+        dma("s", T.W1[:], T.WT[:], ["WT", "WTa", "WTb"], ["W1"])
+        ts(T.BD[:], T.XG[:, 0:128], T.PF[:, 2:3], None, OP.is_equal, None, ["XG", "PF"], ["BD"])
+        ts(T.RB[0:8, :], T.XG[0:8, :], T.PF[0:8, 0:1], None, OP.is_equal, None, ["XG", "PF"], ["RB"])
+        ts(T.PLF[0:8, :], T.PL[0:8, :], -0.25, 0.0, OP.add, OP.max, ["PL"], ["PLF"])
+        for k in range(16):
+            ts(T.SEL[:, 128 * k:128 * k + 128], T.BD[:], T.MS[:, k:k + 1], None, OP.mult, None, ["BD", "MS"], ["SEL%d" % k])
+
+    def send_pulls():
+        for h in range(2):
+            it = []
+            for j in range(2):
+                t = 2 * h + j + 1
+                it.append((B[6 + h][:, j * C:j * C + 128], T.RB[0:8, 128:256], T.PLF[0:8, 0:128], True, True))
+                it.append((B[6 + h][:, j * C + 128:(j + 1) * C], T.RB[0:8, 128 - 16 * t:256 - 16 * t], T.PLF[0:8, 128:256], True, True))
+            mm(it, ["RB", "PLF"], ["x%d" % h], [6 + h])
+            cp("a", T.FS[:, 512 * h:512 * h + 512], B[6 + h][:], ["x%d" % h], ["FS%d" % h] + (["F4"] if h else []), [6 + h])
+        need("g", ["FS0", "FS1"], [])
+        tr = []
+        for t in range(1, STEPS):
+            rid, pid, _ = topo.addr(peer(t))
+            en = topo.engines(core, peer(t))
+            tr.append(RemoteDMATransfer(dst_ids=[DstId(rid=rid, pnc=pid)], dma_engine_mask=(1 << en[2 * t]) | (1 << en[2 * t + 1]),
+                                        remote_sem=T.sem["rf%d" % t], src=T.FS[:, (t - 1) * C:t * C], dst=T.FL[:, (t - 1) * C:t * C]))
+        s = lsem()
+        g.remote_dma_fused(tr, local_sem=T.sem[s])
+        done((s, 2 * (STEPS - 1), "r"), ["FS0", "FS1"], [])
+
+    def pool(t):
+        return (T.P0, T.P1)[(t - 1) % 2]
+
+    def rkeys(t):
+        return ["R%dq%d" % (t, q) for q in range(4)]
+
+    def rec_window(t):
+        i = (t - 1) % 2
+        keys = ["Za%d" % i, "Zb%d" % i, "Y%d" % i, "Y%db" % i] + rkeys(t)
+        if t > 2:
+            return pool(t)[:, PZ:PEND], keys + ["Zc%d" % i] + rkeys(t - 2)
+        return pool(t)[:, PZ:PZ2 + 16], keys
+
+    def gather_r(q, t, c0, c1, keys):
+        win, wk = rec_window(t)
+        cp(q, T.RS[:, 16 * c0:16 * c1], win.indirect(T.RU[:, c0:c1]), wk + ["RU"], keys)
+
+    def gather_v(q, t, h):
+        win, wk = rec_window(t)
+        cp(q, pool(t)[:, PV + h * H:PV + h * H + H], win.indirect(T.VU[:, 128 * h:128 * h + 128]), wk + ["VU"],
+           ["V%d%d" % ((t - 1) % 2, h)])
+
+    def gather_y(q, t, c0, c1, keys):
+        i = (t - 1) % 2
+        wk = ["V%d0" % i, "V%d1" % i, "Za%d" % i, "Y%d" % i, "Y%db" % i, "OU"] + rkeys(1 + i)
+        cp(q, pool(t + 1)[:, PY + 16 * c0:PY + 16 * c1], pool(t)[:, PV:PZ2].indirect(T.OU[:, c0:c1]), wk, keys)
+
+    dk = ["D%d" % q for q in range(4)]
+    nk = ["N%d" % q for q in range(4)]
+
+    def exp_mm(j):
+        b = 6 + j % 2
+        it = []
+        for kk in range(2):
+            k = 2 * j + kk
+            o = B[b][:, kk * C:(kk + 1) * C]
+            it += [(o, T.PB1[:], T.D[:, k:K:16], True, False), (o, T.PBN[:, 0:128], T.NN[:, k:K:16], False, False),
+                   (o, T.SEL[:, 128 * k:128 * k + 128], T.NH[:], False, True)]
+        mm(it, dk + nk + ["NH", "PB1", "PBN", "SEL%d" % (2 * j), "SEL%d" % (2 * j + 1)], ["x%d" % (j % 2)], [b])
+
+    def exp_act(j):
+        act(T.X[:, 512 * j:512 * j + 512], B[6 + j % 2][:], AF.Exp, ["x%d" % (j % 2)], ["X%d" % j], [6 + j % 2], scale=-1.0 / 64)
+
+    def exp_both(j):
+        exp_mm(j)
+        exp_act(j)
+
+    def owners(t):
+        W = (T.W0, T.W1)[(t - 1) % 2]
+        to_list(p_own, 3, "own", E_ID, W, ["W%d" % ((t - 1) % 2)], 0, C, True, True)
+
+    def fold_home(t):
+        xk = ["X%d" % j for j in range(8)]
+        need("g", xk, [])
+        rid, pid, _ = topo.addr(aide)
+        s = lsem()
+        g.remote_dma_fused([RemoteDMATransfer(dst_ids=[DstId(rid=rid, pnc=pid)], dma_engine_mask=aide_mask,
+                                              remote_sem=T.sem["re%d" % t], srcs=[T.X[:, k * C:(k + 1) * C] for k in range(16)],
+                                              dsts=[T.EL[:, (t - 1) * C:t * C]], alu_op=1)], local_sem=T.sem[s])
+        done((s, len(inner(core)), "r"), xk, [])
+
+    for t in range(1, STEPS + 1):
+        last = t == STEPS
+        i = (t - 1) % 2
+        P, W, wk = pool(t), (T.W0, T.W1)[i], "W%d" % i
+        r0 = PRA if t <= 2 else PRB
+        nu, nuk = T.NU, "NU%d" % t
+        n0 = (t - 1) * C
+        yk = ["Y%d" % i, "Y%db" % i]
+        if t > 1:
+            sb = T.SB[:, (t - 2) * H:(t - 1) * H]
+            dma("s", P[16:128, r0 + H:r0 + K], T.SB[0:112, (t - 2) * H:(t - 1) * H], ["SB%d" % t], ["R%dq2" % t])
+            dma("s", P[0:16, r0 + H:r0 + K], T.SB[112:128, (t - 2) * H:(t - 1) * H], ["SB%d" % t], ["R%dq3" % t])
+        dnk = [nuk, "DN", "DNa", "DNb"]
+        if t == 1 or last:
+            cp("v", W[:].indirect(nu[:, n0:n0 + 128]), T.CS[:, 0:H], [nuk, "CS"], [wk, "W0h"][:2 if t == 1 else 1])
+        else:
+            cp("v", T.GD[:, 0:1024], T.DN[:].indirect(nu[:, n0:n0 + 64]), dnk, ["GD0"])
+            cp("a", T.GD[:, 1024:H], T.DN[:].indirect(nu[:, n0 + 64:n0 + 128]), dnk, ["GD0b"])
+            tt(W[:].indirect(nu[:, n0:n0 + 128]), T.GD[:, 0:H], T.CS[:, 0:H], OP.add, [nuk, "CS", "GD0", "GD0b"], [wk])
+        if t > 1:
+            exp_both(4)
+            exp_both(5)
+            gather_v("a", t - 1, 1)
+            gather_v("a", t - 1, 0)
+        if t == 1:
+            setup_rest()
+            cp("a", T.GC[:, H:K], W[:].indirect(nu[:, n0 + 128:n0 + C]), [nuk, wk], ["GC2", "GC3"])
+        else:
+            cp("v", T.GC[:, H:H + 1024], W[:].indirect(nu[:, n0 + 128:n0 + 192]), [nuk, wk], ["GC2"])
+            cp("a", T.GC[:, H + 1024:K], W[:].indirect(nu[:, n0 + 192:n0 + C]), [nuk, wk], ["GC3"])
+        cp("v", W[:].indirect(nu[:, n0 + 128:n0 + C]), T.CS[:, H:K], [nuk, "CS", "CSb"], [wk])
+        if t > 1:
+            exp_both(6)
+            exp_both(7)
+            fold_home(t - 1)
+            gather_y("a", t - 1, 0, C, yk)
+        if t == 1:
+            send_pulls()
+            for h in range(2):
+                cp("a", T.GD[:, h * H:h * H + H], T.DN[:].indirect(nu[:, n0 + 128 * h:n0 + 128 * h + 128]), dnk, ["GD%d" % h])
+        if not last:
+            to_list(p_d, 4, "dA", E_DN, T.GD, ["GD0", "GD0b"], 0, 128, True, True)
+            if t == 1:
+                to_list(p_d, 4, "dB", E_DN, T.GD, ["GD1"], 128, C, True, True)
+            else:
+                to_list(p_d, 4, "dB", E_DN, T.GC, ["GC2", "GC3"], 128, C, True, True)
+        to_list(p_co, 3, "coB", E_FA, T.GC, ["GC2", "GC3"], 128, C, True, True)
+        R = P[:, r0:r0 + K]
+        to_list(p_b, 0, "b", E_B, R, rkeys(t), 0, C, True, False)
+        to_list(p_la, 1, "la", E_LA, R, rkeys(t), 0, C, True, False)
+        mm([(p_la, T.BD[:], T.KD[:], False, True)], ["BD", "KD"], ["la"], [1])
+        mm([(p_sg, T.BD[:], T.KC[:], True, False)], ["BD", "KC"], ["sg"], [2])
+        cp("a", T.GC[:, 0:H], W[:].indirect(nu[:, n0:n0 + 128]), [nuk, wk], ["GC0"])
+        if last:
+            it = []
+            for h in range(2):
+                for u in (1, 2):
+                    it.append((B[6][:, 128 * h:128 * h + 128], T.PBF[:, 16 * u * h:16 * u * h + 128],
+                               T.EL[:, (u - 1) * C + 128 * h:(u - 1) * C + 128 * h + 128], u == 1, u == 2))
+            mm(it, ["PBFa", "PBFb", "EL1", "EL2"], ["x0"], [6])
+            cp("a", T.E3[:], B[6][:, 0:C], ["x0"], ["E3"], [6])
+
+        def d_gather(q):
+            tt(T.D[:, 1024 * q:1024 * q + 1024], P[:, PY:PY + K].indirect(nu[:, n0 + 64 * q:n0 + 64 * q + 64]),
+               P[:, r0 + 1024 * q:r0 + 1024 * q + 1024], OP.subtract, yk + [nuk] + rkeys(t), ["D%d" % q])
+        d_gather(QO[0])
+        if not last:
+            ts(T.DU[:], p_d, float(-YOFF), None, OP.add, None, ["dA", "dB"], ["DU"], [4])
+            for h in range(2):
+                cp("a", T.GD[:, h * H:h * H + H], W[:].indirect(T.DU[:, 128 * h:128 * h + 128]), ["DU", wk], ["GD%d" % h, "GD0b"][:2 - h])
+        for a, q in enumerate(QO):
+            if a < 3:
+                d_gather(QO[a + 1])
+            ts(T.NN[:, 1024 * q:1024 * q + 1024], T.D[:, 1024 * q:1024 * q + 1024], 0.0, None, OP.min, None, ["D%d" % q], ["N%d" % q])
+            if a == 0:
+                to_list(p_sg, 2, "sg", E_SG, T.D, ["D%d" % q], 64 * q, 64 * q + 64, False, False)
+            if a < 3:
+                qn = QO[a + 1]
+                to_list(p_sg, 2, "sg", E_SG, T.D, ["D%d" % qn], 64 * qn, 64 * qn + 64, False, a == 2)
+            to_list(p_b, 0, "b", E_B, T.NN, ["N%d" % q], 64 * q, 64 * q + 64, False, a == 3)
+            if a == 0:
+                to_list(p_co, 3, "coA", E_FB, T.GC, ["GC0"], 0, 128, True, True)
+                ts(T.NF[:], nu[:, n0:n0 + C], float(YOFF), None, OP.add, None, [nuk], ["NF"])
+                if last:
+                    owners(t)
+                else:
+                    tt(T.DM[:], p_d, T.NF[:], OP.subtract, ["dA", "dB", "NF"], ["DM"], [4])
+            if a == 1 and not last:
+                to_list(p_oc, 4, "ocA", E_OC, T.GD, ["GD0"], 0, 128, True, True)
+        act(T.RL[:], p_sg, AF.Relu, ["sg"], ["RL"], [2], scale=1.0 / 2048, bias=-8.0)
+        act(T.BO[:], p_b, AF.Sign, ["b"], ["BO"], [0])
+        mm([(p_n, T.BD[:], T.BO[:], True, True)], ["BD", "BO"], ["n"], [2])
+        if last:
+            cp("v", T.OU[:], p_own, ["own"], ["OU"], [3])
+        else:
+            to_list(p_oc, 4, "ocB", E_OC, T.GD, ["GD1"], 128, C, True, True)
+        tt(T.LA[:], p_la, T.RL[:], OP.subtract, ["la", "RL"], ["LA"], [1])
+        F = T.FS[:, 3 * C:4 * C] if last else T.FL[:, n0:n0 + C]
+        J, jk = (T.JA, "JA") if t <= 2 else (T.JB, "JB")
+        tt(T.WM[:], p_b, T.LA[:], OP.min, ["b", "LA"], ["WM"], [0])
+        tt(T.G1[:], p_b, T.LA[:], OP.is_gt, ["b", "LA"], ["G1"], [0])
+        tt(t0, p_n, T.WM[:], OP.mult, ["n", "WM"], ["t0"], [2, 5])
+        tt(T.G2[:], T.G1[:], p_co, OP.is_gt, ["G1", "coA", "coB"], ["G2"], [3])
+        tt(T.NH[:], t0, F, OP.is_le, ["t0", "F%d" % t], ["NH"], [5])
+        tt(t1, p_sg, T.G2[:], OP.mult, ["sg", "G2"], ["t1"], [2, 5])
+        exp_both(0)
+        exp_both(1)
+        up, lo, hi = (OP.add, OP.min, OP.max) if t <= 2 else (OP.subtract, OP.max, OP.min)
+        top = float((PZ2 if t <= 2 else PZ3) - PZ)
+        if not last:
+            tt(t2, T.NH[:], p_oc, OP.is_gt, ["NH", "ocA", "ocB"], ["t2"], [4, 1])
+        tt(t0, t1, T.NH[:], OP.mult, ["t1", "NH"], ["t0"], [5])
+        if not last:
+            tt(t2, t2, T.DM[:], OP.mult, ["t2", "DM"], ["t2"], [1])
+            tt(t1, J[:], t0, up, [jk, "t0"], ["t1"], [5])
+            tt(T.SN[:], t2, T.NF[:], OP.add, ["t2", "NF"], ["SN"], [1])
+            mm([(p_nm, T.PBF[:, 112:240], T.SN[:, 128:C], True, True)], ["PBFa", "PBFb", "SN"], ["nm"], [0])
+            tt(T.Y1[:], t1, T.NF[:], lo, ["t1", "NF"], ["Y1"], [5])
+            ts(T.NS[:, 0:128], T.SN[:, 0:128], float(-YOFF), None, OP.add, None, ["SN"], ["NSa"])
+            ts(T.NS[:, 128:C], p_nm, float(-YOFF), None, OP.add, None, ["nm"], ["NSb"], [0])
+            send(T.NU[:, t * C:(t + 1) * C], T.NS[:], peer(1), "rn%d" % (t + 1), ["NSa", "NSb"])
+            ts(T.RU[:], T.Y1[:], 0.0, top, OP.max, OP.min, ["Y1"], ["RU"])
+            tt(t2, T.NF[:], t0, up, ["NF", "t0"], ["t2"], [5, 1])
+            exp_both(2)
+            exp_both(3)
+            owners(t)
+            gather_r("a", t, 0, 128, ["RS0", "RS1"])
+            tt(T.Y2[:], t2, J[:], hi, ["t2", jk], ["Y2"], [1])
+            gather_r("v", t, 128, C, ["RS2", "RS3"])
+            ts(T.VU[:], T.Y2[:], 0.0, top, OP.max, OP.min, ["Y2"], ["VU"])
+            cp("v", T.OU[:], p_own, ["own"], ["OU"], [3])
+            send(T.SB[:, (t - 1) * H:t * H], T.RS[:, H:K], peer(1), "rb%d" % (t + 1), ["RS2", "RS3"])
+            send(T.P0[:, t * H:(t + 1) * H], T.RS[:, 0:H], aide, "ra%d" % (t + 1), ["RS0", "RS1"])
+            if t <= 2:
+                dma("s", W[:], T.WT[:], ["WT", "WTa", "WTb"], [wk])
+            continue
+
+        tt(t2, T.NF[:], t0, up, ["NF", "t0"], ["t2"], [5, 1])
+        tt(t1, J[:], t0, up, [jk, "t0"], ["t1"], [5])
+        tt(T.Y2[:], t2, J[:], hi, ["t2", jk], ["Y2"], [1])
+        tt(T.Y1[:], t1, T.NF[:], lo, ["t1", "NF"], ["Y1"], [5])
+        ts(T.VU[:], T.Y2[:], 0.0, top, OP.max, OP.min, ["Y2"], ["VU"])
+        ts(T.RU[:], T.Y1[:], 0.0, top, OP.max, OP.min, ["Y1"], ["RU"])
+        pb = ["PBFa", "PBFb"]
+        ea, eb = B[4][:, 0:128], B[1][:, 0:128]
+
+        def totals(j):
+            it = []
+            for k in (2 * j, 2 * j + 1):
+                it += [(ea, T.PBF[:, 0:128], T.X[:, k * C:k * C + 128], k == 0, False),
+                       (eb, T.PBF[:, 64:192], T.X[:, k * C + 128:(k + 1) * C], k == 0, False)]
+            mm(it, pb + ["X%d" % j], ["ea", "eb"], [4, 1])
+
+        def mix(src, keys, h, b, turn, out, okey, dst, q):
+            x = 64 if turn else 0
+            mats = (T.PB1[:], T.PBM[:], T.PB2[:, x:x + 128], T.PBN[:, x:x + 128])
+            mm([(B[b][:], mats[e], src[:, 1024 * e + 512 * h:1024 * e + 512 * h + 512], e == 0, e == 3) for e in range(4)],
+               keys + ["PB1", "PBM", "PB2", "PBN"], ["o%d" % b], [b])
+
+            def store():
+                cp(q, out[:, 512 * h:512 * h + 512], B[b][:], ["o%d" % b], [okey], [b])
+                dma("s", dst[:, 512 * h:512 * h + 512], out[:, 512 * h:512 * h + 512], [okey], [])
+            return store
+        Yn = pool(t + 1)[:, PY:PY + K]
+        exp_both(2)
+        gather_v("v", t, 1)
+        gather_v("a", t, 0)
+        exp_both(3)
+        totals(0)
+        exp_both(4)
+        totals(1)
+        totals(2)
+        for e in range(4):
+            gather_r("v", t, 64 * e, 64 * e + 32, ["RS%d" % e])
+        for e in range(4):
+            gather_y("a", t, 64 * e, 64 * e + 32, ["Yf0%d" % e, "Y0", "Y0b"][:3 if e == 0 else 1])
+        for e in range(4):
+            gather_y("v", t, 64 * e + 32, 64 * e + 64, ["Yf1%d" % e])
+        exp_mm(5)
+        exp_mm(6)
+        st_r0 = mix(T.RS, ["RS%d" % e for e in range(4)], 0, 0, True, T.YR, "YR0", T.yr, "a")
+        totals(3)
+        exp_act(5)
+        exp_act(6)
+        st_r0()
+        st_w0 = mix(Yn, ["Yf0%d" % e for e in range(4)], 0, 2, False, T.YW, "YW0", T.yw, "a")
+        exp_both(7)
+        st_w0()
+        totals(4)
+        st_w1 = mix(Yn, ["Yf1%d" % e for e in range(4)], 1, 3, False, T.YW, "YW1", T.yw, "v")
+        for e in range(3):
+            gather_r("v", t, 64 * e + 32, 64 * e + 64, ["RT%d" % e])
+        gather_r("a", t, 64 * 3 + 32, 64 * 3 + 64, ["RT3"])
+        st_w1()
+        totals(5)
+        totals(6)
+        st_r1 = mix(T.RS, ["RT%d" % e for e in range(4)], 1, 5, True, T.YR, "YR1", T.yr, "a")
+        totals(7)
+        mm([(ea, T.PBF[:, 0:128], T.EL[:, 2 * C:2 * C + 128], False, True),
+            (eb, T.PBF[:, 48:176], T.EL[:, 2 * C + 128:3 * C], False, True)], pb + ["EL3"], ["ea", "eb"], [4, 1])
+        st_r1()
+        tt(T.YE[:, 0:128], ea, T.E3[:, 0:128], OP.add, ["ea", "E3"], ["YEa"], [4])
+        tt(T.YE[:, 128:C], eb, T.E3[:, 128:C], OP.add, ["eb", "E3"], ["YEb"], [1])
+        dma("a", T.ye[:], T.YE[:], ["YEa", "YEb"], [])
+
+    for s, v in final.items():
+        if all(seen[q].get(s, 0) < v for q in Q):
+            g.wait_ge(T.sem[s], v)

@@ -1,3 +1,4 @@
+import math
 from concourse.bass import DstId, RemoteDMATransfer
 from concourse.mybir import AluOpType as OP, ActivationFunctionType as AF
 
@@ -5,46 +6,55 @@ K = 4096
 H = 2048
 C = 256
 STEPS = 4
-PV, PZ, PRA, PY, PZ2, PRB, PZ3, PEND = 0, 4096, 4224, 8320, 12416, 12544, 16640, 16656
-YOFF = PY - PZ
-QO = (2, 3, 0, 1)
+U = K + 128
+Y0, PEND = 4 * U, 9 * U - 128
+X_, Y_ = 1, 0
+BIG = 8192.0
+LARGE = 131072.0
+FAR = 20.0
+R_ID, R_FX, R_PT, R_DN, R_FY = 0, 2, 4, 8, 12
 
 SCRATCH = {
-    "P0": ("sbuf", [128, PEND], "bfloat16"), "P1": ("sbuf", [128, PEND], "bfloat16"),
+    "P": ("sbuf", [128, PEND], "bfloat16"),
     "SB": ("sbuf", [128, 3 * H], "bfloat16"), "RS": ("sbuf", [128, K], "bfloat16"),
-    "W0": ("sbuf", [128, K], "bfloat16"), "W1": ("sbuf", [128, K], "bfloat16"), "WT": ("sbuf", [128, K], "bfloat16"),
-    "CS": ("sbuf", [128, K], "bfloat16"), "DN": ("sbuf", [128, K], "bfloat16"),
+    "W": ("sbuf", [128, K], "bfloat16"), "CX": ("sbuf", [128, H], "bfloat16"),
+    "WY": ("sbuf", [128, K], "float32"), "CY": ("sbuf", [128, H], "float32"),
     "D": ("sbuf", [128, K], "bfloat16"), "NN": ("sbuf", [128, K], "bfloat16"),
-    "GC": ("sbuf", [128, K], "bfloat16"), "GD": ("sbuf", [128, K], "bfloat16"),
+    "GL": ("sbuf", [128, K], "bfloat16"), "GX": ("sbuf", [128, H], "bfloat16"), "OC": ("sbuf", [128, K], "bfloat16"),
     "X": ("sbuf", [128, K], "float32"),
-    "YW": ("sbuf", [128, 1024], "float32"), "YR": ("sbuf", [128, 1024], "float32"), "YE": ("sbuf", [128, C], "float32"),
-    "SEL": ("sbuf", [128, 16 * 128], "bfloat16"), "EX": ("sbuf", [128, 8 * 144], "bfloat16"),
-    "BM": ("sbuf", [128, 144], "bfloat16"), "BD": ("sbuf", [128, 128], "bfloat16"),
-    "PBF": ("sbuf", [128, 256], "float32"), "PB1": ("sbuf", [128, 128], "bfloat16"), "PBM": ("sbuf", [128, 128], "bfloat16"),
+    "YW": ("sbuf", [128, 1024], "float32"), "YR": ("sbuf", [128, 1024], "float32"),
+    "SEL": ("sbuf", [128, 16 * 128], "bfloat16"), "EX": ("sbuf", [128, 3 * 144], "bfloat16"),
+    "TW": ("sbuf", [128, 120], "bfloat16"), "GM": ("sbuf", [128, 32], "bfloat16"), "BD": ("sbuf", [128, 128], "bfloat16"),
+    "PBF": ("sbuf", [128, 256], "float32"), "PBG": ("sbuf", [128, 128], "float32"),
+    "PB1": ("sbuf", [128, 128], "bfloat16"), "PBM": ("sbuf", [128, 128], "bfloat16"), "PB8": ("sbuf", [128, 128], "bfloat16"),
+    "PZ0": ("sbuf", [128, 128], "bfloat16"), "PZ1": ("sbuf", [128, 128], "bfloat16"),
     "PB2": ("sbuf", [128, 256], "bfloat16"), "PBN": ("sbuf", [128, 256], "bfloat16"),
-    "KC": ("sbuf", [128, C], "bfloat16"), "RB": ("sbuf", [128, 256], "float32"),
+    "KM": ("sbuf", [128, 768], "bfloat16"), "KB": ("sbuf", [128, 4 * C], "bfloat16"), "RB": ("sbuf", [128, 256], "float32"),
     "L": ("sbuf", [128, 256], "float32"), "XG": ("sbuf", [128, 256], "float32"),
-    "PI": ("sbuf", [128, 4], "int32"), "PF": ("sbuf", [128, 16], "float32"), "CB": ("sbuf", [128, 16], "bfloat16"),
-    "M16": ("sbuf", [128, 16], "float32"), "MS": ("sbuf", [128, 16], "bfloat16"),
-    "KD": ("sbuf", [128, C], "bfloat16"), "RL": ("sbuf", [128, C], "float32"), "E3": ("sbuf", [128, C], "float32"),
-    "JA": ("sbuf", [128, C], "float32"), "JB": ("sbuf", [128, C], "float32"),
-    "NI": ("sbuf", [128, C], "int32"), "DI": ("sbuf", [128, C], "int32"), "DJ": ("sbuf", [128, 2 * C], "int32"),
-    "DB": ("sbuf", [128, 2 * C], "bfloat16"), "PL": ("sbuf", [128, C], "int32"), "PLF": ("sbuf", [128, C], "float32"),
+    "PI": ("sbuf", [128, 4], "int32"), "PF": ("sbuf", [128, 16], "float32"), "CB": ("sbuf", [128, 8], "float32"),
+    "M16": ("sbuf", [128, 16], "float32"),
+    "NI": ("sbuf", [128, C], "int32"), "DI": ("sbuf", [128, C], "int32"), "PL": ("sbuf", [128, C], "int32"),
+    "DB": ("sbuf", [128, 2 * C], "bfloat16"),
     "FS": ("sbuf", [128, 4 * C], "float32"), "FL": ("sbuf", [128, 3 * C], "float32"), "EL": ("sbuf", [128, 3 * C], "float32"),
     "NU": ("sbuf", [128, 4 * C], "uint16"), "NS": ("sbuf", [128, C], "uint16"),
-    "OU": ("sbuf", [128, C], "uint16"), "DU": ("sbuf", [128, C], "uint16"),
+    "OU": ("sbuf", [128, C], "uint16"), "DU": ("sbuf", [128, C], "uint16"), "PU": ("sbuf", [128, C], "uint16"),
     "RU": ("sbuf", [128, C], "uint16"), "VU": ("sbuf", [128, C], "uint16"),
-    "NF": ("sbuf", [128, C], "float32"), "DM": ("sbuf", [128, C], "float32"), "LA": ("sbuf", [128, C], "float32"),
-    "WM": ("sbuf", [128, C], "float32"), "G1": ("sbuf", [128, C], "float32"), "G2": ("sbuf", [128, C], "float32"),
-    "SN": ("sbuf", [128, C], "float32"), "Y1": ("sbuf", [128, C], "float32"), "Y2": ("sbuf", [128, C], "float32"),
-    "BO": ("sbuf", [128, C], "bfloat16"), "NH": ("sbuf", [128, C], "bfloat16"),
+    "NF": ("sbuf", [128, C], "float32"), "YJ": ("sbuf", [128, 2 * C], "float32"),
+    "OF": ("sbuf", [128, C], "float32"), "TY": ("sbuf", [128, C], "float32"),
+    "RE": ("sbuf", [128, C], "float32"), "WM": ("sbuf", [128, C], "float32"), "TB": ("sbuf", [128, 384], "float32"),
+    "BT": ("sbuf", [128, C], "bfloat16"), "BL": ("sbuf", [128, C], "bfloat16"),
+    "NT": ("sbuf", [128, C], "bfloat16"), "NH": ("sbuf", [128, C], "bfloat16"), "ZZ": ("sbuf", [128, 2 * C], "bfloat16"),
 }
 for _b in range(8):
     SCRATCH["B%d" % _b] = ("psum", [128, 512], "float32")
 
-SEMAPHORES = (["qv", "qa", "qp", "qg"] + ["d%d" % i for i in range(40)] + ["l%d" % i for i in range(24)]
-              + ["rn%d" % t for t in range(1, 5)] + ["ra%d" % t for t in range(1, 5)] + ["rb%d" % t for t in range(1, 5)]
-              + ["rf%d" % t for t in range(1, 4)] + ["re%d" % t for t in range(1, 4)])
+SEMAPHORES = (["qv", "qa", "qp", "qg"] + ["d%d" % i for i in range(64)] + ["l%d" % i for i in range(36)]
+              + ["%s%d" % (n, t) for n in ("nx", "ny", "ra", "rb", "rc", "rd") for t in range(1, 5)]
+              + ["%s%d" % (n, t) for n in ("re", "rf", "rg") for t in range(1, 4)])
+
+
+def zs(t):
+    return (STEPS - t) * U
 
 
 def rank_program(g, core, T, topo):
@@ -56,26 +66,35 @@ def rank_program(g, core, T, topo):
         return [h for h in topo.cores_of(c) if h not in cores and topo.die(h) != topo.die(c)
                 and all(topo.may_write(h, d) for d in cores)][0]
 
+    def near(c):
+        return [h for h in topo.cores_of(c) if h not in cores and topo.die(h) == topo.die(c)
+                and all(topo.may_write(h, d) for d in cores)][0]
+
     def inner(c):
         far = set(e for d in cores if d != c for e in topo.engines(c, d))
         return [e for e in topo.engines(c, helper(c)) if e not in far]
 
+    def half(buf, h, n=128):
+        return buf[:, n * h:n * (h + 1)]
+
+    def rec(t, i, n=H):
+        return T.P[:, zs(t) + 128 + i * n:zs(t) + 128 + (i + 1) * n]
+
     if rank is None:
         for r, c in enumerate(cores):
-            if helper(c) == core:
-                jobs = []
-                for t in range(1, STEPS + 1):
-                    r0 = PRA if t <= 2 else PRB
-                    jobs.append(("ra%d" % t, (T.P0, T.P1)[(t - 1) % 2][:, r0:r0 + H], T.P0[:, (t - 1) * H:t * H], r + 1))
-                    if t > 1:
-                        e = T.EL[:, (t - 2) * C:(t - 1) * C]
-                        jobs.append(("re%d" % (t - 1), e, e, r - t + 1))
+            if core in (helper(c), near(c)):
+                if core == helper(c):
+                    jobs = [([("ra%d", "rd%d")[i] % t], rec(t, i, 1024), half(T.P, 2 * t - 2 + i, 1024), r + 1)
+                            for t in range(1, STEPS + 1) for i in range(2)]
+                else:
+                    jobs = [(["re%d" % t, "rg%d" % t], half(T.EL, t - 1, C), half(T.EL, t - 1, C), r - t) for t in range(1, STEPS)]
                 total = 0
-                for sem, out, in_, to in jobs:
+                for sems, out, in_, to in jobs:
                     dst = cores[to % n_ranks]
                     rid, pid, _ = topo.addr(dst)
-                    g.wait_ge(T.sem[sem], len(inner(c)))
-                    g.remote_dma(out, in_, T.sem[sem], T.sem.l0, pid, rid, topo.mask(core, dst))
+                    for sem in sems:
+                        g.wait_ge(T.sem[sem], len(inner(c)))
+                    g.remote_dma(out, in_, T.sem[sems[0]], T.sem.l0, pid, rid, topo.mask(core, dst))
                     total += len(topo.engines(core, dst))
                 g.wait_ge(T.sem.l0, total)
         return
@@ -93,7 +112,7 @@ def rank_program(g, core, T, topo):
             if tok is not None and not (q == "p" and tok[2] == "p"):
                 want[tok[0]] = max(want.get(tok[0], 0), tok[1])
         for k in reads:
-            add(wr.get(k))
+            add(wr[k])
         for k in writes:
             add(wr.get(k))
             for tok in rd.get(k, {}).values():
@@ -166,6 +185,21 @@ def rank_program(g, core, T, topo):
     def act(out, a, f, reads, writes, banks=(), **kw):
         op("a", lambda: g.scalar.activation(out, a, f, **kw), reads, writes, banks)
 
+    def scaled(q, out, a, col, reads, writes, banks=()):
+        if q == "v":
+            ts(out, a, col, None, OP.mult, None, reads, writes, banks)
+        else:
+            act(out, a, AF.Identity, reads, writes, banks, scale=col)
+
+    def fill(ap, v, key):
+        op("v", lambda: g.vector.memset(ap, v), [], [key])
+
+    def iota(out, pat, base, cm, key):
+        op("g", lambda: g.iota(out, pat, base, cm, allow_small_or_imprecise_dtypes=True), [], [key])
+
+    def spot(out, in_, pat, v, base, reads, key):
+        op("g", lambda: g.affine_select(out, in_, pat, OP.not_equal, v, base, 1), reads, [key])
+
     def mm(items, reads, writes, banks):
         def run():
             ins = None
@@ -174,399 +208,686 @@ def rank_program(g, core, T, topo):
             return ins
         op("p", run, reads, writes, banks)
 
-    def to_list(out, b, key, e, src, skeys, c0, c1, start, stop):
-        x = 144 * e + 15
-        mm([(out[:, c0:c1], T.EX[:, x - k:x - k + 128], src[:, 16 * c0 + k:16 * c1:16], start and k == 0, stop and k == 15)
-            for k in range(16)], skeys + ["EX%d" % e], [key], [b])
-    E_B, E_LA, E_SG, E_ID, E_FA, E_FB, E_OC, E_DN = range(8)
-
     B = [T["B%d" % b] for b in range(8)]
-    p_b, p_nm = B[0][:, 0:C], B[0][:, C:C + 128]
-    p_la, t2 = B[1][:, 0:C], B[1][:, C:2 * C]
-    p_sg, p_n = B[2][:, 0:C], B[2][:, C:2 * C]
-    p_co, p_own = B[3][:, 0:C], B[3][:, C:2 * C]
-    p_d, p_oc = B[4][:, 0:C], B[4][:, C:2 * C]
-    t0, t1 = B[5][:, 0:C], B[5][:, C:2 * C]
+    E_PT, E_DN, E_ID = range(3)
+
+    def to_list(out, b, key, e, cols, skeys, first=()):
+        x = 144 * e + 15
+        it = [(out, T.PB1[:], a, i == 0, False) for i, a in enumerate(first)]
+        it += [(out, T.EX[:, x - k:x - k + 128], cols(k), not first and k == 0, k == 15) for k in range(16)]
+        mm(it, skeys + ["EX%d" % e] + (["KB", "PB1"] if first else []), [key], [b])
+
+    def to_cells(b, q0, w, src, skeys, keys, stop=False):
+        n = w.shape[1] // 8
+        mm([(B[b][:, 128 * q0 + k:128 * (q0 + n):16], src[:, k:H:16], w, False, stop and k == 15) for k in range(16)], skeys, keys, [b])
+
+    def row(buf, r):
+        return buf[r:128:16, :]
 
     src_n = len(topo.engines(peer(-1), core))
+    lands("nx1", src_n, ["NU11", "NU10"])
+    lands("rb1", src_n, ["R11%d" % i for i in range(4)])
     for t in range(1, STEPS + 1):
-        lands("rn%d" % t, src_n, ["NU%d" % t])
-        lands("ra%d" % t, len(topo.engines(helper(peer(-1)), core)), ["R%dq0" % t, "R%dq1" % t])
-        lands("rb%d" % t, src_n, ["R1q2", "R1q3"] if t == 1 else ["SB%d" % t])
-    for t in range(1, STEPS):
-        lands("rf%d" % t, 2, ["F%d" % t])
-        lands("re%d" % t, len(topo.engines(helper(peer(t)), core)), ["EL%d" % t])
+        lands("ra%d" % t, len(topo.engines(helper(peer(-1)), core)), ["R%d00" % t])
+        lands("rd%d" % t, len(topo.engines(helper(peer(-1)), core)), ["R%d01" % t])
+        if t > 1:
+            lands("nx%d" % t, src_n, ["NU%d1" % t])
+            lands("ny%d" % t, src_n, ["NU%d0" % t])
+            lands("rb%d" % t, src_n, ["SB%d0" % t])
+            lands("rc%d" % t, src_n, ["SB%d1" % t])
+        if t < STEPS:
+            lands("rf%d" % t, 2, ["F%d" % t])
+            lands("re%d" % t, len(topo.engines(near(peer(t)), core)), ["EL%d" % t])
 
     dma("s", T.NI[:, 0:128], T.nm[:, 0:128], [], ["NIa"])
     dma("a", T.NI[16:128, 128:256], T.nm[0:112, 128:256], [], ["NIb"])
     dma("s", T.NI[0:16, 128:256], T.nm[112:128, 128:256], [], ["NIc"])
-    dma("a", T.RS[16:128, H:K], T.rc[0:112, H:K], [], ["RS2"])
-    dma("s", T.RS[0:16, H:K], T.rc[112:128, H:K], [], ["RS3"])
+    dma("a", T.DI[:], T.dn[:], [], ["DI"])
+    dma("s", T.RS[16:128, H:K], T.rc[0:112, H:K], [], ["RS2"])
+    dma("a", T.RS[0:16, H:K], T.rc[112:128, H:K], [], ["RS3"])
     dma("s", T.RS[:, 0:H], T.rc[:, 0:H], [], ["RS0", "RS1"])
-    dma("s", T.DI[:], T.dn[:], [], ["DI"])
-    dma("s", T.PL[0:8, :], T.pl[:], [], ["PL"])
-    dma("s", T.P0[:, PY:PY + K], T.wl[:], [], ["Y0"])
 
     op("g", lambda: g.iota(T.PI[:, 0:1], [[0, 1]], 0, 1), [], ["PI0"])
-    op("g", lambda: g.iota(T.L[:], [[1, 256]], 0, 0, allow_small_or_imprecise_dtypes=True), [], ["L"])
-    op("g", lambda: g.iota(T.XG[:], [[0, 2], [1, 8], [0, 16]], 0, 0, allow_small_or_imprecise_dtypes=True), [], ["XG"])
+    iota(T.L[:], [[1, 256]], 0, 0, "L")
+    iota(T.XG[:], [[0, 2], [1, 8], [0, 16]], 0, 0, "XG")
 
-    op("v", lambda: g.vector.memset(T.KC[:], 1024.0), [], ["KC"])
-    op("v", lambda: g.vector.memset(T.KD[:], 1.0 / 512), [], ["KD"])
-    for i, P in enumerate((T.P0, T.P1)):
-        op("v", lambda: g.vector.memset(P[:, PZ:PRA], 0.0), [], ["Za%d" % i])
-        op("v", lambda: g.vector.memset(P[:, PZ2:PRB], 0.0), [], ["Zb%d" % i])
-        op("v", lambda: g.vector.memset(P[:, PZ3:PEND], 0.0), [], ["Zc%d" % i])
+    idn = AF.Identity
+    fill(T.W[:], 0.0, "W")
+    cp("a", T.CY[:], T.W[:, 0:H], ["W"], ["CY"])
+    cp("a", T.WY[:], T.W[:], ["W"], ["WY"])
     ts(T.PI[:, 1:2], T.PI[:, 0:1], 15, None, OP.bitwise_and, None, ["PI0"], ["PI1"])
     ts(T.PI[:, 2:3], T.PI[:, 0:1], 4, None, OP.arith_shift_right, None, ["PI0"], ["PI2"])
     cp("v", T.PF[:, 0:3], T.PI[:, 0:3], ["PI0", "PI1", "PI2"], ["PF"])
+    cp("v", T.NS[:], T.NI[:], ["NIa", "NIb", "NIc"], ["NS0", "NS1"])
+    send(T.NU[:, 0:C], T.NS[:], peer(1), "nx1", ["NS0", "NS1"])
+    fill(T.KM[:, 0:512], 0.0, "KM")
+    z, zz = half(T.TY, 0), half(T.TY, 1)
+    ts(T.CB[:, 6:7], T.PF[:, 1:2], 128.0, None, OP.mult, None, ["PF"], ["CB6"])
     ts(T.M16[:], T.L[:, 0:16], T.PF[:, 1:2], None, OP.is_equal, None, ["L", "PF"], ["M16"])
+    ts(z, T.L[:, 0:128], T.CB[:, 6:7], 1.0 / 65536, OP.add, OP.mult, ["L", "CB6"], ["TYa"])
+    cp("v", T.DB[:, 0:C], T.DI[:], ["DI"], ["DBa"])
+    tt(zz, z, z, OP.mult, ["TYa"], ["TY"])
+    tt(T.DB[:, C:2 * C], T.DI[:], T.DB[:, 0:C], OP.subtract, ["DI", "DBa"], ["DBb"])
+    ts(zz, zz, 16.0 / 3, 4.0, OP.mult, OP.add, ["TY"], ["TY"])
     m = [T.M16[:, k:k + 1] for k in range(16)]
+    ts(T.CB[:, 5:6], m[R_ID], 16.0, m[R_FX], OP.mult, OP.add, ["M16"], ["CB5"])
+    tt(z, z, zz, OP.mult, ["TYa", "TY"], ["TYa"])
+    dma("s", row(T.CY, R_FY), z, ["TYa"], ["CY"])
+    need("s", [], ["W"])
+    dma("s", row(T.W, R_DN), T.DB[:, 0:C], ["DBa"], ["Wa"])
+    dma("s", row(T.W, R_DN + 1), T.DB[:, C:2 * C], ["DBb"], ["Wb"])
     for i in range(4):
-        ts(T.CB[:, i:i + 1], m[2], float(1 << i), None, OP.mult, None, ["M16"], ["CB%d" % i])
-    ts(T.PF[:, 3:4], m[2], 16.0, m[1], OP.mult, OP.add, ["M16"], ["PF3"])
-    ts(T.CS[:, 0:128], T.L[:, 0:128], m[3], m[0], OP.mult, OP.add, ["L", "M16"], ["CS"])
-    ts(T.CB[:, 4:5], T.PF[:, 3:4], m[0], None, OP.subtract, None, ["PF3", "M16"], ["CB4"])
-    ts(T.CB[:, 5:6], m[2], m[3], None, OP.add, None, ["M16"], ["CB5"])
-    ts(T.CB[:, 6:7], m[2], float(PY // 128), None, OP.mult, None, ["M16"], ["CB6"])
-    ts(T.CB[:, 7:8], m[2], float(PY // 128 + 16), None, OP.mult, None, ["M16"], ["CB7"])
-    ts(T.PF[:, 4:5], m[2], m[3], None, OP.add, None, ["M16"], ["PF4"])
-    ts(T.PF[:, 5:6], T.PF[:, 2:3], 16.0, 15.0, OP.mult, OP.add, ["PF"], ["PF5"])
-    ts(T.MS[:], T.M16[:], 8192.0, None, OP.mult, None, ["M16"], ["MS"])
-    cp("v", T.NS[:], T.NI[:], ["NIa", "NIb", "NIc"], ["NSa", "NSb"])
-    send(T.NU[:, 0:C], T.NS[:], peer(1), "rn1", ["NSa", "NSb"])
-    send(T.P0[:, PRA + H:PRA + K], T.RS[:, H:K], peer(1), "rb1", ["RS2", "RS3"])
-    send(T.P0[:, 0:H], T.RS[:, 0:H], aide, "ra1", ["RS0", "RS1"])
+        ts(T.CB[:, i:i + 1], m[R_ID], float(1 << i), None, OP.mult, None, ["M16"], ["CB%d" % i])
+    ts(T.CX[:, 0:128], T.L[:, 0:128], m[R_ID + 1], T.CB[:, 5:6], OP.mult, OP.add, ["L", "M16", "CB5"], ["CX"])
+    ts(T.GM[:, 0:16], T.XG[:, 0:256:16], T.PF[:, 2:3], None, OP.is_equal, None, ["XG", "PF"], ["GM"])
     for i in range(4):
         w = 128 << i
-        ts(T.CS[:, w:2 * w], T.CS[:, 0:w], T.CB[:, i:i + 1], None, OP.add, None, ["CS", "CB%d" % i], ["CS"])
-    ts(T.W0[:, 0:H], T.CS[:, 0:H], T.CB[:, 5:6], T.CB[:, 6:7], OP.mult, OP.add, ["CS", "CB5", "CB6"], ["W0"])
-    ts(T.W0[:, H:K], T.CS[:, 0:H], T.CB[:, 5:6], T.CB[:, 7:8], OP.mult, OP.add, ["CS", "CB5", "CB7"], ["W0h"])
-    ts(T.BM[:], T.L[:, 0:144], T.PF[:, 5:6], None, OP.is_equal, None, ["L", "PF5"], ["BM"])
-    ts(T.PBF[:, 0:128], T.L[:, 0:128], T.PF[:, 0:1], None, OP.is_equal, None, ["L", "PF"], ["PBFa"])
-    ts(T.PBF[:, 128:256], T.L[:, 0:128], T.PF[:, 0:1], None, OP.is_equal, None, ["L", "PF"], ["PBFb"])
-    op("g", lambda: g.iota(T.DN[:], [[0, K]], 0, 0, allow_small_or_imprecise_dtypes=True), [], ["DN"])
-    idn = AF.Identity
-    act(T.PF[:, 12:13], m[8], idn, ["M16"], ["W7c"], scale=128.0, bias=m[12])
-    act(T.PF[:, 6:7], m[15], idn, ["M16"], ["W0c"], scale=-1.0, bias=1.0)
-    act(T.PF[:, 7:8], m[15], idn, ["M16"], ["W1c"], scale=16.0)
-    act(T.PF[:, 8:9], m[15], idn, ["M16"], ["W2c"], scale=-32768.0)
-    act(T.PF[:, 9:10], m[2], idn, ["M16"], ["W3c"], scale=128.0, bias=m[3])
-    act(T.PF[:, 10:11], m[0], idn, ["M16"], ["W6c"], bias=m[1])
-    act(T.PF[:, 11:12], T.PF[:, 1:2], idn, ["PF"], ["PF11"], bias=float(PRA - PZ))
-    act(T.JA[:], T.L[:], idn, ["L", "PF11"], ["JA"], scale=16.0, bias=T.PF[:, 11:12])
-    act(T.JB[:], T.JA[:], idn, ["JA"], ["JB"], bias=float(PRB - PRA))
-    act(T.CS[:, H:K], T.CS[:, 0:H], idn, ["CS", "CB4"], ["CSb"], bias=T.CB[:, 4:5])
-    act(T.WT[:], T.CS[:], idn, ["CS", "CSb", "PF4", "CB6"], ["WT"], scale=T.PF[:, 4:5], bias=T.CB[:, 6:7])
-    cols = [T.PF[:, 6:7], T.PF[:, 7:8], T.PF[:, 8:9], T.PF[:, 9:10], m[0], m[1], T.PF[:, 10:11], T.PF[:, 12:13]]
-    for e in range(8):
-        act(T.EX[:, 144 * e:144 * e + 144], T.BM[:], idn, ["BM", "M16", "W%dc" % e], ["EX%d" % e], scale=cols[e])
-    act(T.PB1[:], T.PBF[:, 0:128], idn, ["PBFa"], ["PB1"])
-    act(T.PBM[:], T.PBF[:, 0:128], idn, ["PBFa"], ["PBM"], scale=-1.0)
-    act(T.PBN[:], T.PBF[:], idn, ["PBFa", "PBFb"], ["PBN"], scale=-2.0)
-    act(T.PB2[:], T.PBF[:], idn, ["PBFa", "PBFb"], ["PB2"], scale=2.0)
+        ts(T.CX[:, w:2 * w], T.CX[:, 0:w], T.CB[:, i:i + 1], None, OP.add, None, ["CX", "CB%d" % i], ["CX"])
+        if i == 0:
+            ts(T.GM[:, 16:32], T.XG[:, 0:256:16], T.PF[:, 2:3], -1.0, OP.is_equal, OP.mult, ["XG", "PF"], ["GMb"])
+    send(T.P[:, 0:1024], T.RS[:, 0:1024], aide, "ra1", ["RS0"])
+    send(T.P[:, 1024:H], T.RS[:, 1024:H], aide, "rd1", ["RS1"])
+    for name, v in (("PB1", 1.0), ("PBF", 1.0), ("PB2", 2.0), ("PBM", -1.0), ("PBG", -1.0), ("PB8", BIG),
+                    ("PZ1", 2 * LARGE), ("PZ0", -LARGE), ("PBN", -2.0)):
+        n = T[name].shape[1]
+        spot(T[name][:], T.KM[:, 0:n], [[0, n // 128], [-1, 128]], v, 0, ["KM"], name)
+    for q in "gs":
+        need(q, ["Wa", "Wb"], [])
+    send(rec(1, X_), T.RS[:, H:K], peer(1), "rb1", ["RS2", "RS3"])
+    need("s", ["CY"], [])
+    dma("s", T.P[:, Y0:Y0 + K], T.wl[:], [], ["Y0"])
+    for a, n, src, r, v in ((0, 8, 0, 15, 0.0), (8, 8, 0, 15, -16.0), (16, 16, 0, 15, -16.0), (32, 8, 16, 15, 0.0), (40, 16, 16, 15, 16.0),
+                            (56, 8, 16, 15, -4080.0), (64, 8, None, 15, -4096.0), (72, 8, None, R_DN, 1.0), (72, 8, -1, R_DN + 1, 1.0),
+                            (80, 16, None, R_FX, -BIG), (96, 16, None, R_FY, -2 * BIG), (112, 8, None, R_FX, 1.0), (112, 8, -1, R_FY, 4.0)):
+        in_ = T.KM[:, 0:n] if src is None else T.TW[:, a:a + n] if src < 0 else T.GM[:, src:src + n]
+        spot(T.TW[:, a:a + n], in_, [[0, n // 8], [-16, 8]], v, -r, ["KM", "GM", "GMb"] + (["TW%d" % a] if src == -1 else []), "TW%d" % a)
+    iota(T.KB[:, 0:4 * C], [[U, 4], [0, C]], U - 32768, 0, "KB")
+    dma("g", T.PL[0:8, :], T.pl[:], [], ["PL"])
+    tt(T.PF[:, 4:6], T.M16[:, R_PT:R_DN + 1:4], T.M16[:, R_PT + 1:R_DN + 2:4], OP.add, ["M16"], ["PF4"])
+    ts(T.PF[:, 7:8], T.PF[:, 1:2], R_FX + 0.5, None, OP.is_gt, None, ["PF"], ["MK"])
+    ts(T.PF[:, 6:7], m[R_ID], 128.0, m[R_ID + 1], OP.mult, OP.add, ["M16"], ["PF6"])
+    ts(T.PF[:, 3:4], T.PF[:, 2:3], 16.0, 15.0, OP.mult, OP.add, ["PF"], ["PF3"])
+    ts(T.PF[:, 6:7], m[R_FX], 32768.0, T.PF[:, 6:7], OP.mult, OP.add, ["M16", "PF6"], ["PF6"])
+    for i in range(8):
+        a = i * U if i < 4 else (i + 1) * U - 128
+        fill(T.P[:, a:a + 128], 0.0, "Z%d" % i)
+    for e in range(3):
+        ts(T.EX[:, 144 * e:144 * e + 144], T.L[:, 0:144], T.PF[:, 3:4], T.PF[:, 4 + e:5 + e], OP.is_equal, OP.mult, ["L", "PF3", "PF4", "PF6"], ["EX%d" % e])
+    ts(T.RB[0:8, :], T.XG[0:8, :], T.PF[0:8, 0:1], None, OP.is_equal, None, ["XG", "PF"], ["RB"])
+    ts(T.BD[:], T.XG[:, 0:128], T.PF[:, 2:3], None, OP.is_equal, None, ["XG", "PF"], ["BD"])
+    fill(T.KM[:, 512:768], -BIG, "KMb")
+    fill(T.TB[:], 0.0, "TBz")
+    act(T.PF[:, 9:10], T.PF[:, 1:2], idn, ["PF"], ["PF9"], bias=128.0)
+    act(T.PF[:, 11:12], T.PF[:, 1:2], idn, ["PF"], ["PF11"], scale=256.0)
+    act(half(T.YJ, 1), T.L[:, 0:128], idn, ["L", "PF9"], ["J0"], scale=16.0, bias=T.PF[:, 9:10])
+    act(half(T.YJ, 3), half(T.YJ, 1), idn, ["J0"], ["J1"], bias=float(H))
+    act(T.OF[:], T.L[:], idn, ["L", "PF11"], ["OF"], bias=T.PF[:, 11:12])
 
-    def setup_rest():
-        ts(T.DJ[:, 0:C], T.DI[:], 7, None, OP.arith_shift_right, None, ["DI"], ["DJa"])
-        ts(T.DJ[:, C:2 * C], T.DI[:], 127, None, OP.bitwise_and, None, ["DI"], ["DJb"])
-        ts(T.DB[:, 0:C], T.DJ[:, 0:C], float(YOFF // 128), None, OP.add, None, ["DJa"], ["DBa"])
-        cp("v", T.DB[:, C:2 * C], T.DJ[:, C:2 * C], ["DJb"], ["DBb"])
-        dma("s", T.DN[8:128:16, :], T.DB[:, 0:C], ["DBa", "DN"], ["DNa"])
-        dma("s", T.DN[12:128:16, :], T.DB[:, C:2 * C], ["DBb", "DN"], ["DNb"])
-        dma("s", T.WT[8:128:16, :], T.DB[:, 0:C], ["DBa", "WT"], ["WTa"])
-        dma("s", T.WT[12:128:16, :], T.DB[:, C:2 * C], ["DBb", "WT"], ["WTb"])
-        dma("s", T.W1[:], T.WT[:], ["WT", "WTa", "WTb"], ["W1"])
-        ts(T.BD[:], T.XG[:, 0:128], T.PF[:, 2:3], None, OP.is_equal, None, ["XG", "PF"], ["BD"])
-        ts(T.RB[0:8, :], T.XG[0:8, :], T.PF[0:8, 0:1], None, OP.is_equal, None, ["XG", "PF"], ["RB"])
-        ts(T.PLF[0:8, :], T.PL[0:8, :], -0.25, 0.0, OP.add, OP.max, ["PL"], ["PLF"])
-        for k in range(16):
-            ts(T.SEL[:, 128 * k:128 * k + 128], T.BD[:], T.MS[:, k:k + 1], None, OP.mult, None, ["BD", "MS"], ["SEL%d" % k])
+    def pulls():
+        ts(T.WM[0:8, :], T.PL[0:8, :], -0.25, 0.0, OP.add, OP.max, ["PL"], ["WM0", "WM1"])
 
-    def send_pulls():
-        for h in range(2):
+    def pulls_out():
+        for j in range(2):
             it = []
-            for j in range(2):
-                t = 2 * h + j + 1
-                it.append((B[6 + h][:, j * C:j * C + 128], T.RB[0:8, 128:256], T.PLF[0:8, 0:128], True, True))
-                it.append((B[6 + h][:, j * C + 128:(j + 1) * C], T.RB[0:8, 128 - 16 * t:256 - 16 * t], T.PLF[0:8, 128:256], True, True))
-            mm(it, ["RB", "PLF"], ["x%d" % h], [6 + h])
-            cp("a", T.FS[:, 512 * h:512 * h + 512], B[6 + h][:], ["x%d" % h], ["FS%d" % h] + (["F4"] if h else []), [6 + h])
+            for t in (2 * j + 1, 2 * j + 2):
+                a = (t - 1) % 2 * C
+                it.append((B[6 + j][:, a:a + 128], T.WM[0:8, 0:128], T.RB[0:8, 128:256], True, True))
+                it.append((B[6 + j][:, a + 128:a + C], T.WM[0:8, 128:256], T.RB[0:8, 128 - 16 * t:256 - 16 * t], True, True))
+            mm(it, ["RB", "WM0", "WM1"], ["x%d" % j], [6 + j])
+            cp("a", half(T.FS, j, 512), B[6 + j][:], ["x%d" % j], ["FS%d" % j] + (["F4"] if j else []), [6 + j])
         need("g", ["FS0", "FS1"], [])
         tr = []
         for t in range(1, STEPS):
             rid, pid, _ = topo.addr(peer(t))
             en = topo.engines(core, peer(t))
             tr.append(RemoteDMATransfer(dst_ids=[DstId(rid=rid, pnc=pid)], dma_engine_mask=(1 << en[2 * t]) | (1 << en[2 * t + 1]),
-                                        remote_sem=T.sem["rf%d" % t], src=T.FS[:, (t - 1) * C:t * C], dst=T.FL[:, (t - 1) * C:t * C]))
+                                        remote_sem=T.sem["rf%d" % t], src=half(T.FS, t - 1, C), dst=half(T.FL, t - 1, C)))
         s = lsem()
         g.remote_dma_fused(tr, local_sem=T.sem[s])
         done((s, 2 * (STEPS - 1), "r"), ["FS0", "FS1"], [])
 
-    def pool(t):
-        return (T.P0, T.P1)[(t - 1) % 2]
+    def setup_late():
+        iota(T.SEL[:], [[0, 2048]], int(BIG), 0, "SEL")
+        op("g", lambda: g.affine_select(T.SEL[:], T.SEL[:], [[-1, 16], [-16, 8], [0, 16]], OP.is_equal, 0.0, 0, 1), ["SEL"], ["SEL"])
 
-    def rkeys(t):
-        return ["R%dq%d" % (t, q) for q in range(4)]
+    def rkeys(t, h):
+        return ["R%d1%d" % (t, i) for i in range(4)] if h else ["R%d00" % t, "R%d01" % t]
+
+    def wall_keys(t):
+        return ["Y0"] + ["Z%d" % (4 + u) for u in range(min(t, STEPS))] + ["V%d%d" % (u, q) for u in range(1, t) for q in range(8)]
 
     def rec_window(t):
-        i = (t - 1) % 2
-        keys = ["Za%d" % i, "Zb%d" % i, "Y%d" % i, "Y%db" % i] + rkeys(t)
-        if t > 2:
-            return pool(t)[:, PZ:PEND], keys + ["Zc%d" % i] + rkeys(t - 2)
-        return pool(t)[:, PZ:PZ2 + 16], keys
+        keys = wall_keys(t) + [k for u in range(1, t + 1) for k in rkeys(u, 0) + rkeys(u, 1) + ["Z%d" % (STEPS - u)]]
+        return T.P[:, zs(t):Y0 + (t - 1) * U + K + 16], keys
 
-    def gather_r(q, t, c0, c1, keys):
+    def rsk(c0, c1):
+        return ["RQ%d" % c for c in range(c0 // 32, c1 // 32)]
+
+    def gather_r(q, t, c0, c1):
         win, wk = rec_window(t)
-        cp(q, T.RS[:, 16 * c0:16 * c1], win.indirect(T.RU[:, c0:c1]), wk + ["RU"], keys)
+        need(q, [], ["RS%d" % i for i in range(4)])
+        cp(q, T.RS[:, 16 * c0:16 * c1], win.indirect(T.RU[:, c0:c1]), wk + ["RU%d" % (c0 // 128)], rsk(c0, c1))
 
-    def gather_v(q, t, h):
+    def gather_v(q, t, c0, c1):
         win, wk = rec_window(t)
-        cp(q, pool(t)[:, PV + h * H:PV + h * H + H], win.indirect(T.VU[:, 128 * h:128 * h + 128]), wk + ["VU"],
-           ["V%d%d" % ((t - 1) % 2, h)])
+        a = Y0 + t * U
+        cp(q, T.P[:, a + 16 * c0:a + 16 * c1], win.indirect(T.VU[:, c0:c1]), wk + ["VU%d" % (c0 // 128)], ["V%d%d" % (t, c) for c in range(c0 // 32, c1 // 32)])
 
-    def gather_y(q, t, c0, c1, keys):
-        i = (t - 1) % 2
-        wk = ["V%d0" % i, "V%d1" % i, "Za%d" % i, "Y%d" % i, "Y%db" % i, "OU"] + rkeys(1 + i)
-        cp(q, pool(t + 1)[:, PY + 16 * c0:PY + 16 * c1], pool(t)[:, PV:PZ2].indirect(T.OU[:, c0:c1]), wk, keys)
+    def dk(h):
+        return ["D%d" % c for c in range(8 * h, 8 * h + 8)]
 
-    dk = ["D%d" % q for q in range(4)]
-    nk = ["N%d" % q for q in range(4)]
+    wk_ = ["W", "Wa", "Wb", "Wc"]
+    wr["Wc"] = None
 
-    def exp_mm(j):
-        b = 6 + j % 2
+    def exp_mm(h, j, b):
         it = []
-        for kk in range(2):
-            k = 2 * j + kk
-            o = B[b][:, kk * C:(kk + 1) * C]
-            it += [(o, T.PB1[:], T.D[:, k:K:16], True, False), (o, T.PBN[:, 0:128], T.NN[:, k:K:16], False, False),
-                   (o, T.SEL[:, 128 * k:128 * k + 128], T.NH[:], False, True)]
-        mm(it, dk + nk + ["NH", "PB1", "PBN", "SEL%d" % (2 * j), "SEL%d" % (2 * j + 1)], ["x%d" % (j % 2)], [b])
+        for kk in range(4):
+            k = 4 * j + kk
+            o = half(B[b], kk)
+            it += [(o, T.PB1[:], T.D[:, H * h + k:H * h + H:16], True, False), (o, T.PB2[:, 0:128], T.NN[:, H * h + k:H * h + H:16], False, False),
+                   (o, half(T.SEL, k), half(T.NH, h), False, True)]
+        mm(it, ["PB1", "PB2", "SEL"] + dk(h) + ["N%d" % h, "NH%d" % h], ["o%d" % b], [b])
 
-    def exp_act(j):
-        act(T.X[:, 512 * j:512 * j + 512], B[6 + j % 2][:], AF.Exp, ["x%d" % (j % 2)], ["X%d" % j], [6 + j % 2], scale=-1.0 / 64)
+    def exp_act(h, j, b):
+        act(half(T.X, 4 * h + j, 512), B[b][:], AF.Sigmoid, ["o%d" % b], ["X%d" % (4 * h + j)], [b], scale=-1.0 / 64, bias=-FAR)
 
-    def exp_both(j):
-        exp_mm(j)
-        exp_act(j)
+    def exp_half(h, j, b):
+        exp_mm(h, j, b)
+        exp_act(h, j, b)
 
-    def owners(t):
-        W = (T.W0, T.W1)[(t - 1) % 2]
-        to_list(p_own, 3, "own", E_ID, W, ["W%d" % ((t - 1) % 2)], 0, C, True, True)
-
-    def fold_home(t):
-        xk = ["X%d" % j for j in range(8)]
-        need("g", xk, [])
-        rid, pid, _ = topo.addr(aide)
+    def fold_home(t, h):
+        keys = ["X%d" % j for j in range(4 * h, 4 * h + 4)]
+        need("g", keys, [])
+        rid, pid, _ = topo.addr(near(core))
         s = lsem()
-        g.remote_dma_fused([RemoteDMATransfer(dst_ids=[DstId(rid=rid, pnc=pid)], dma_engine_mask=aide_mask,
-                                              remote_sem=T.sem["re%d" % t], srcs=[T.X[:, k * C:(k + 1) * C] for k in range(16)],
-                                              dsts=[T.EL[:, (t - 1) * C:t * C]], alu_op=1)], local_sem=T.sem[s])
-        done((s, len(inner(core)), "r"), xk, [])
+        g.remote_dma_fused([RemoteDMATransfer(dst_ids=[DstId(rid=rid, pnc=pid)], dma_engine_mask=aide_mask, remote_sem=T.sem[("re%d", "rg%d")[h] % t],
+                                              srcs=[half(T.X, 16 * h + k) for k in range(16)], dsts=[half(T.EL, 2 * t - 2 + h)], alu_op=1)], local_sem=T.sem[s])
+        done((s, len(inner(core)), "r"), keys, [])
+
+    def totals(h, j, stop=False):
+        mm([(B[3 + h][:, 0:128], T.PBF[:, 64 * h:64 * h + 128], half(T.X, 16 * h + 4 * j + kk), False, stop and kk == 3) for kk in range(4)],
+           ["PBF", "X%d" % (4 * h + j)], ["e%d" % h], [3 + h])
+
+    def earlier(h, us, start, stop):
+        mm([(B[3 + h][:, 0:128], T.PBF[:, 16 * u * h:16 * u * h + 128], half(T.EL, 2 * u - 2 + h), start and u == us[0], stop and u == us[-1]) for u in us],
+           ["PBF"] + ["EL%d" % u for u in us], ["e%d" % h], [3 + h])
+
+    def mix(b, parts, keys, start, stop):
+        mm([(B[b][:], w, src, start and i == 0, stop and i == len(parts) - 1) for i, (w, src) in enumerate(parts)],
+           keys + ["PB1", "PB2", "PBN"], ["o%d" % b], [b])
+
+    def mix_w(j):
+        mix(1 + 4 * j, [(T.PB1[:], half(T.OC, j, 512)), (T.PB2[:, 0:128], half(T.OC, 4 + j, 512))], ["y%d0" % j, "y%d1" % j], True, True)
+
+    def mix_x(j):
+        mix(2 * j, [(T.PB2[:, 64:192], half(T.RS, 4 + j, 512)), (T.PBN[:, 64:192], half(T.RS, 6 + j, 512))], rsk(128, 256), True, False)
+
+    def mix_y(j):
+        mix(2 * j, [(T.PB1[:], half(T.GL, j, 512))], ["r%d" % j], False, True)
+
+    def totals_out(q, h):
+        scaled(q, half(T.NF, h), B[3 + h][:, 0:128], math.exp(FAR), ["e%d" % h], ["NF%d" % h], [3 + h])
+
+    def last_pointers():
+        to_list(B[5][:, C:2 * C], 5, "own", E_PT, lambda k: T.W[:, k:K:16], wk_)
+
+    def last_offsets():
+        cp("v", T.OU[:], B[5][:, C:2 * C], ["own"], ["OU"], [5])
+
+    def store(q, b, out, okey, dst, j):
+        cp(q, half(out, j, 512), B[b][:], ["o%d" % b], [okey], [b])
+        dma("s", half(dst, j, 512), half(out, j, 512), [okey], [])
+
+    def pair(out, old, win, wk, off, ok, c0, key, first):
+        a, z_ = out[:, 16 * c0:16 * c0 + 512], out[:, 16 * c0 + 1024:16 * c0 + 1536]
+        if first:
+            cp(first, z_, win.indirect(off[:, c0 + 64:c0 + 96]), wk + [ok], [key + "z", old % (c0 // 32 + 2)])
+        else:
+            tt(a, win.indirect(off[:, c0:c0 + 32]), z_, OP.subtract, wk + [ok, key + "z"], [key, old % (c0 // 32)])
+
+    def pair_y(j, e, first=None):
+        pair(T.OC, "OC%d", T.P[:, Y0:PEND], wall_keys(STEPS + 1), T.OU, "OU", 128 * e + 32 * j, "y%d%d" % (j, e), first)
+
+    def pair_r(j, first=None):
+        win, wk = rec_window(STEPS)
+        pair(T.GL, "GL%d", win, wk, T.RU, "RU0", 32 * j, "r%d" % j, first)
 
     for t in range(1, STEPS + 1):
         last = t == STEPS
-        i = (t - 1) % 2
-        P, W, wk = pool(t), (T.W0, T.W1)[i], "W%d" % i
-        r0 = PRA if t <= 2 else PRB
-        nu, nuk = T.NU, "NU%d" % t
         n0 = (t - 1) * C
-        yk = ["Y%d" % i, "Y%db" % i]
-        if t > 1:
-            sb = T.SB[:, (t - 2) * H:(t - 1) * H]
-            dma("s", P[16:128, r0 + H:r0 + K], T.SB[0:112, (t - 2) * H:(t - 1) * H], ["SB%d" % t], ["R%dq2" % t])
-            dma("s", P[0:16, r0 + H:r0 + K], T.SB[112:128, (t - 2) * H:(t - 1) * H], ["SB%d" % t], ["R%dq3" % t])
-        dnk = [nuk, "DN", "DNa", "DNb"]
-        if t == 1 or last:
-            cp("v", W[:].indirect(nu[:, n0:n0 + 128]), T.CS[:, 0:H], [nuk, "CS"], [wk, "W0h"][:2 if t == 1 else 1])
-        else:
-            cp("v", T.GD[:, 0:1024], T.DN[:].indirect(nu[:, n0:n0 + 64]), dnk, ["GD0"])
-            cp("a", T.GD[:, 1024:H], T.DN[:].indirect(nu[:, n0 + 64:n0 + 128]), dnk, ["GD0b"])
-            tt(W[:].indirect(nu[:, n0:n0 + 128]), T.GD[:, 0:H], T.CS[:, 0:H], OP.add, [nuk, "CS", "GD0", "GD0b"], [wk])
-        if t > 1:
-            exp_both(4)
-            exp_both(5)
-            gather_v("a", t - 1, 1)
-            gather_v("a", t - 1, 0)
-        if t == 1:
-            setup_rest()
-            cp("a", T.GC[:, H:K], W[:].indirect(nu[:, n0 + 128:n0 + C]), [nuk, wk], ["GC2", "GC3"])
-        else:
-            cp("v", T.GC[:, H:H + 1024], W[:].indirect(nu[:, n0 + 128:n0 + 192]), [nuk, wk], ["GC2"])
-            cp("a", T.GC[:, H + 1024:K], W[:].indirect(nu[:, n0 + 192:n0 + C]), [nuk, wk], ["GC3"])
-        cp("v", W[:].indirect(nu[:, n0 + 128:n0 + C]), T.CS[:, H:K], [nuk, "CS", "CSb"], [wk])
-        if t > 1:
-            exp_both(6)
-            exp_both(7)
-            fold_home(t - 1)
-            gather_y("a", t - 1, 0, C, yk)
-        if t == 1:
-            send_pulls()
-            for h in range(2):
-                cp("a", T.GD[:, h * H:h * H + H], T.DN[:].indirect(nu[:, n0 + 128 * h:n0 + 128 * h + 128]), dnk, ["GD%d" % h])
-        if not last:
-            to_list(p_d, 4, "dA", E_DN, T.GD, ["GD0", "GD0b"], 0, 128, True, True)
-            if t == 1:
-                to_list(p_d, 4, "dB", E_DN, T.GD, ["GD1"], 128, C, True, True)
-            else:
-                to_list(p_d, 4, "dB", E_DN, T.GC, ["GC2", "GC3"], 128, C, True, True)
-        to_list(p_co, 3, "coB", E_FA, T.GC, ["GC2", "GC3"], 128, C, True, True)
-        R = P[:, r0:r0 + K]
-        to_list(p_b, 0, "b", E_B, R, rkeys(t), 0, C, True, False)
-        to_list(p_la, 1, "la", E_LA, R, rkeys(t), 0, C, True, False)
-        mm([(p_la, T.BD[:], T.KD[:], False, True)], ["BD", "KD"], ["la"], [1])
-        mm([(p_sg, T.BD[:], T.KC[:], True, False)], ["BD", "KC"], ["sg"], [2])
-        cp("a", T.GC[:, 0:H], W[:].indirect(nu[:, n0:n0 + 128]), [nuk, wk], ["GC0"])
-        if last:
-            it = []
-            for h in range(2):
-                for u in (1, 2):
-                    it.append((B[6][:, 128 * h:128 * h + 128], T.PBF[:, 16 * u * h:16 * u * h + 128],
-                               T.EL[:, (u - 1) * C + 128 * h:(u - 1) * C + 128 * h + 128], u == 1, u == 2))
-            mm(it, ["PBFa", "PBFb", "EL1", "EL2"], ["x0"], [6])
-            cp("a", T.E3[:], B[6][:, 0:C], ["x0"], ["E3"], [6])
 
-        def d_gather(q):
-            tt(T.D[:, 1024 * q:1024 * q + 1024], P[:, PY:PY + K].indirect(nu[:, n0 + 64 * q:n0 + 64 * q + 64]),
-               P[:, r0 + 1024 * q:r0 + 1024 * q + 1024], OP.subtract, yk + [nuk] + rkeys(t), ["D%d" % q])
-        d_gather(QO[0])
-        if not last:
-            ts(T.DU[:], p_d, float(-YOFF), None, OP.add, None, ["dA", "dB"], ["DU"], [4])
-            for h in range(2):
-                cp("a", T.GD[:, h * H:h * H + H], W[:].indirect(T.DU[:, 128 * h:128 * h + 128]), ["DU", wk], ["GD%d" % h, "GD0b"][:2 - h])
-        for a, q in enumerate(QO):
-            if a < 3:
-                d_gather(QO[a + 1])
-            ts(T.NN[:, 1024 * q:1024 * q + 1024], T.D[:, 1024 * q:1024 * q + 1024], 0.0, None, OP.min, None, ["D%d" % q], ["N%d" % q])
-            if a == 0:
-                to_list(p_sg, 2, "sg", E_SG, T.D, ["D%d" % q], 64 * q, 64 * q + 64, False, False)
-            if a < 3:
-                qn = QO[a + 1]
-                to_list(p_sg, 2, "sg", E_SG, T.D, ["D%d" % qn], 64 * qn, 64 * qn + 64, False, a == 2)
-            to_list(p_b, 0, "b", E_B, T.NN, ["N%d" % q], 64 * q, 64 * q + 64, False, a == 3)
-            if a == 0:
-                to_list(p_co, 3, "coA", E_FB, T.GC, ["GC0"], 0, 128, True, True)
-                ts(T.NF[:], nu[:, n0:n0 + C], float(YOFF), None, OP.add, None, [nuk], ["NF"])
-                if last:
-                    owners(t)
-                else:
-                    tt(T.DM[:], p_d, T.NF[:], OP.subtract, ["dA", "dB", "NF"], ["DM"], [4])
-            if a == 1 and not last:
-                to_list(p_oc, 4, "ocA", E_OC, T.GD, ["GD0"], 0, 128, True, True)
-        act(T.RL[:], p_sg, AF.Relu, ["sg"], ["RL"], [2], scale=1.0 / 2048, bias=-8.0)
-        act(T.BO[:], p_b, AF.Sign, ["b"], ["BO"], [0])
-        mm([(p_n, T.BD[:], T.BO[:], True, True)], ["BD", "BO"], ["n"], [2])
-        if last:
-            cp("v", T.OU[:], p_own, ["own"], ["OU"], [3])
+        def nu(c0, c1):
+            return T.NU[:, n0 + c0:n0 + c1]
+
+        def glk(c0, c1):
+            return ["GL%d" % c for c in range(c0 // 32, c1 // 32)]
+
+        def look(q, c0, c1):
+            scaled(q, T.GL[:, 16 * c0:16 * c1], T.W[:].indirect(nu(c0, c1)), T.PF[:, 7:8] if c0 >= 128 else 1.0,
+                   ["NU%d%d" % (t, c0 // 128), "MK"] + wk_, glk(c0, c1))
+
+        def scatter_x():
+            tt(T.W[:].indirect(nu(128, C)), half(T.GL, 1, H), T.CX[:], OP.add, ["NU%d1" % t, "CX"] + glk(128, C), wk_)
+
+        def scatter_y():
+            act(T.WY[:].indirect(nu(0, 128)), T.CY[:], AF.Sigmoid, ["NU%d0" % t, "CY"], ["WY"])
+
+        def flags_y():
+            if last:
+                need("g", ["TY"], [])
+            else:
+                dma("g", row(T.W, R_FY), row(T.WY, R_FY), ["WY"], wk_)
+
+        def cells_out(i, u=t):
+            if i < 2:
+                send(half(T.P, 2 * u - 2 + i, 1024), half(T.RS, i, 1024), aide, ("ra%d", "rd%d")[i] % u, rsk(64 * i, 64 * i + 64))
+            else:
+                send(half(T.SB, 2 * u - 6 + i, 1024), half(T.RS, i, 1024), peer(1), ("rb%d", "rc%d")[i - 2] % u, rsk(64 * i, 64 * i + 64))
+
+        def owners_x():
+            to_list(B[5][:, C:2 * C], 5, "own", E_ID, lambda k: half(T.W, k, C), wk_, (half(T.KB, t - 1, C),))
+
+        def owners_y():
+            dma("s", T.TY[:], row(T.WY, R_FY), ["WY"], ["TY", "TYa"])
+
+        def pointers():
+            x = B[5][:, C:2 * C]
+            return [lambda: tt(T.OF[:], x, T.OF[:], OP.max, ["own", "OF"], ["OF"], [5]),
+                    lambda: ts(T.DI[:], T.TY[:], 65536.0, t * U - 32768.0, OP.mult, OP.add, ["TY"], ["DI"]),
+                    lambda: tt(T.OF[:], T.DI[:], T.OF[:], OP.max, ["DI", "OF"], ["OF"]),
+                    lambda: cp("a", half(T.DB, 0, C), T.OF[:], ["OF"], ["DBa"]),
+                    lambda: mm([(x, T.PBF[:, 0:128], T.OF[:], True, False), (x, T.PBM[:], half(T.DB, 0, C), False, True)],
+                               ["OF", "DBa", "PBF", "PBM"], ["own"], [5]),
+                    lambda: cp("a", half(T.DB, 1, C), x, ["own"], ["DBb"], [5])]
+
+        def new_table():
+            need("s", [], wk_)
+            dma("s", row(T.W, R_PT), half(T.DB, 0, C), ["DBa"], ["Wa"])
+            dma("s", row(T.W, R_PT + 1), half(T.DB, 1, C), ["DBb"], ["Wb"])
+            if not last:
+                dma("s", row(T.W, R_FX), T.CX[5:128:8, :], ["CX"], ["Wc"])
+                dma("s", row(T.WY, R_FY), T.CY[1:128:8, :], ["CY"], ["WY"])
+
+        def lists(h):
+            cols, gk = lambda k: T.GL[:, H * h + k:H * h + H:16], glk(128 * h, 128 * h + 128)
+            if t > 1:
+                to_list(B[5 - h][:, 128:256], 5 - h, "p%d" % h, E_PT, cols, gk)
+            if not last:
+                to_list(B[5 - h][:, 0:128], 5 - h, "d%d" % h, E_DN, cols, gk)
+
+        def names_f(h):
+            if not last:
+                cp("v", half(T.NF, h), nu(128 * h, 128 * h + 128), ["NU%d%d" % (t, h)], ["NF%d" % h])
+
+        def pointer_f(h):
+            if t == 1:
+                act(half(T.YJ, 2 * h), half(T.NF, h), idn, ["NF%d" % h], ["YP%d" % h], bias=float(U))
+            elif h:
+                ts(half(T.YJ, 2 * h), B[5 - h][:, 128:256], float(t * U), None, OP.add, None, ["p%d" % h], ["YP%d" % h], [5 - h])
+            else:
+                act(half(T.YJ, 2 * h), B[5 - h][:, 128:256], idn, ["p%d" % h], ["YP%d" % h], [5 - h], bias=float(t * U))
+
+        def pointer_u(h):
+            if t > 1:
+                cp("v", half(T.PU, h), B[5 - h][:, 128:256], ["p%d" % h], ["PU%d" % h], [5 - h])
+            if not last:
+                cp("v", half(T.DU, h), B[5 - h][:, 0:128], ["d%d" % h], ["DU%d" % h], [5 - h])
+
+        def open_main(h):
+            mm([(B[1 - h][:, 0:384], T.PB1[:], T.KM[:, 0:384], True, False), (B[3 - h][:, 0:C], T.PB1[:], T.KM[:, 512:768], True, False)],
+               ["PB1", "KM", "KMb"], ["M%d" % h, "S%d" % h], [1 - h, 3 - h])
+            if not last:
+                to_cells(1 - h, 2, T.TW[:, 72:80], half(T.GL, h, H), glk(128 * h, 128 * h + 128) + ["TW72"], ["M%d" % h])
+                mm([(B[1 - h][:, 256:384], half(T.NF, h), T.PBG[:], False, False)], ["NF%d" % h, "PBG"], ["M%d" % h], [1 - h])
+
+        def own_share(h):
+            to_cells(1 - h, 0, T.TW[:, 0:16], rec(t, h), rkeys(t, h) + ["TW0", "TW8"], ["M%d" % h])
+            to_cells(3 - h, 0, T.TW[:, 16:32], rec(t, h), rkeys(t, h) + ["TW16"], ["S%d" % h])
+
+        def both(h):
+            src, sk = (T.GX[:], ["GX0", "GX1"]) if h else (half(T.GL, 0, H), glk(0, 128))
+            to_cells(3 - h, 0, T.TW[:, 80 + 16 * h:96 + 16 * h], src, sk + ["TW80", "TW96"], ["S%d" % h])
+
+        def look_x(q, i):
+            cp(q, half(T.GX, i, 1024), T.WY[:].indirect(nu(128 + 64 * i, 192 + 64 * i)), ["NU%d1" % t, "WY"], ["GX%d" % i])
+
+        def taken(c0, c1):
+            cp("a", T.OC[:, 16 * c0:16 * c1], T.W[:].indirect(T.DU[:, c0:c1]), ["DU%d" % (c0 // 128)] + wk_, ["OC%d" % c for c in range(c0 // 32, c1 // 32)])
+
+        def taken_mm(h):
+            mm([(B[6 + h][:, 256:384], T.PB1[:], T.KM[:, 0:128], True, False)], ["PB1", "KM"], ["oc%d" % h], [6 + h])
+            to_cells(6 + h, 2, T.TW[:, 112:120], half(T.OC, h, H), ["OC%d" % c for c in range(4 * h, 4 * h + 4)] + ["TW112"], ["oc%d" % h], True)
+
+        def d_gather(c0, c1):
+            h, a = c0 // 128, zs(t) + 128
+            off, ok = (nu(c0, c1), "NU1%d" % h) if t == 1 else (T.PU[:, c0:c1], "PU%d" % h)
+            n, q0, q1 = len(rkeys(t, h)) // 2, c0 // 64 % 2, (c1 - 1) // 64 % 2
+            tt(T.D[:, 16 * c0:16 * c1], T.P[:, Y0:Y0 + (t - 1) * U + K].indirect(off), T.P[:, a + 16 * c0:a + 16 * c1], OP.subtract,
+               wall_keys(t) + rkeys(t, h)[n * q0:n * q1 + n] + [ok], ["D%d" % c for c in range(c0 // 16, c1 // 16)])
+
+        def d_pass(h):
+            to_cells(3 - h, 1, T.TW[:, 64:72], half(T.D, h, H), dk(h) + ["TW64"], ["S%d" % h])
+
+        def n_pass(h):
+            ts(half(T.NN, h, H), half(T.D, h, H), -1.0, 0.0, OP.mult, OP.max, dk(h), ["N%d" % h])
+            to_cells(1 - h, 0, T.TW[:, 32:48], half(T.NN, h, H), ["N%d" % h, "TW32", "TW40"], ["M%d" % h], True)
+
+        def n_swap(h):
+            to_cells(3 - h, 0, T.TW[:, 48:64], half(T.NN, h, H), ["N%d" % h, "TW40", "TW56"], ["S%d" % h])
+
+        def bonds(h):
+            M, mk = B[1 - h], "M%d" % h
+
+            def bond():
+                ts(half(T.BT, h), M[:, 0:128], 0.0, None, OP.is_gt, None, [mk], ["BT%d" % h], [1 - h])
+                mm([(B[6 + h][:, 0:128], half(T.BT, h), T.PB1[:], True, True)], ["BT%d" % h, "PB1"], ["x%d" % h], [6 + h])
+            return [bond, lambda: ts(half(T.RE, h), M[:, 128:256], -1.0 / 32, 0.0, OP.add, OP.max, [mk], ["RE%d" % h], [1 - h]),
+                    lambda: cp("v", half(T.BL, h), B[6 + h][:, 0:128], ["x%d" % h], ["BL%d" % h], [6 + h])]
+
+        def holds(h):
+            F = half(T.FS, 6 + h) if last else half(T.FL, 2 * t - 2 + h)
+            n = B[1 - h][:, 128:256]
+
+            def weakest():
+                tt(half(T.WM, h), B[1 - h][:, 0:128], half(T.RE, h), OP.subtract, ["M%d" % h, "RE%d" % h], ["WM%d" % h], [1 - h])
+                mm([(n, half(T.BL, h), T.BD[:], True, True)], ["BL%d" % h, "BD"], ["n%d" % h], [1 - h])
+            return [weakest, lambda: tt(n, n, half(T.WM, h), OP.mult, ["n%d" % h, "WM%d" % h], ["n%d" % h], [1 - h]),
+                    lambda: tt(half(T.NT, h), n, F, OP.is_le, ["n%d" % h, "F%d" % t], ["NT%d" % h], [1 - h])]
+
+        def bases(h):
+            mm([(B[5 - h][:, 0:256], T.PBF[:, 0:128], half(T.YJ, h, 256), True, False)], ["PBF", "YP%d" % h, "J%d" % h],
+               ["pY%d" % h, "d%d" % h, "p%d" % h], [5 - h])
+            if not last:
+                x = 112 if h else 0
+                mm([(B[7 - h][:, 128:256], T.PBF[:, x:x + 128], half(T.NF, h), True, False)], ["PBF", "NF%d" % h], ["x%d" % (1 - h)], [7 - h])
+
+        def moves(h):
+            def step():
+                a = 144 if h else 0
+                tt(T.TB[:, a:a + 128], B[1 - h][:, 256:384], half(T.WM, h), OP.mult, ["M%d" % h, "WM%d" % h, "TBz"], ["TB%d" % h], [1 - h])
+                o = B[7 - h][:, 128:256]
+                it = [(o, T.TB[:, 128:256], T.PBF[:, 0:128], False, False), (o, T.TB[:, 256:384], T.PBF[:, 0:128], False, True)] if h else \
+                    [(o, T.TB[:, 0:128], T.PBF[:, 0:128], False, True)]
+                mm(it, ["TB%d" % h, "PBF"], ["x%d" % (1 - h)], [7 - h])
+            return [lambda: tt(half(T.WM, h), half(T.NT, h), B[6 + h][:, 256:384], OP.is_gt, ["NT%d" % h, "oc%d" % h], ["WM%d" % h], [6 + h]), step]
+
+        def names_out(h):
+            cp("v", half(T.NS, h), B[7 - h][:, 128:256], ["x%d" % (1 - h)], ["NS%d" % h], [7 - h])
+            send(half(T.NU, 2 * t + h), half(T.NS, h), peer(1), ("ny%d", "nx%d")[h] % (t + 1), ["NS%d" % h])
+
+        def swaps(h):
+            S, sk = B[3 - h], "S%d" % h
+            mm([(S[:, 0:128], T.PB8[:], half(T.NT, h), False, False), (S[:, 128:256], T.PB8[:], half(T.NT, h), False, True)],
+               ["PB8", "NT%d" % h], [sk], [3 - h])
+
+        def swaps_add(h):
+            ts(half(T.ZZ, h, 256), B[3 - h][:, 0:C], -0.5, 0.0, OP.add, OP.max, ["S%d" % h], ["ZZ%d" % h], [3 - h])
+            it = []
+            for a in (128, 0):
+                o = B[5 - h][:, a:a + 128]
+                it += [(o, half(T.ZZ, 2 * h + 1), T.PZ1[:], False, False), (o, half(T.ZZ, 2 * h), T.PZ0[:], False, a == 0)]
+            mm(it, ["ZZ%d" % h, "PZ0", "PZ1"], ["pY%d" % h], [5 - h])
+
+        def mask_list(h):
+            mm([(B[1 - h][:, 0:128], half(T.NT, h), T.PB1[:], True, True)], ["NT%d" % h, "PB1"], ["M%d" % h], [1 - h])
+
+        def mask_keep(h):
+            cp("a", half(T.NH, h), B[1 - h][:, 0:128], ["M%d" % h], ["NH%d" % h], [1 - h])
+
+        def rec_lists(h):
+            return [lambda: tt(half(T.WM, h), B[5 - h][:, 128:256], half(T.YJ, 2 * h), OP.min, ["pY%d" % h, "YP%d" % h], ["WM%d" % h], [5 - h]),
+                    lambda: tt(half(T.RE, h), B[5 - h][:, 0:128], half(T.YJ, 2 * h + 1), OP.max, ["pY%d" % h, "J%d" % h], ["RE%d" % h], [5 - h]),
+                    lambda: ts(half(T.RU, h), half(T.WM, h), 0.0, None, OP.max, None, ["WM%d" % h], ["RU%d" % h]),
+                    lambda: ts(half(T.VU, h), half(T.RE, h), float((2 * t - 1) * U + K), None, OP.min, None, ["RE%d" % h], ["VU%d" % h])]
+
+        if t == 1:
+            look("v", 128, 256)
+            scatter_y()
+            scatter_x()
+            look_x("a", 0)
+            lists(X_)
+            look_x("a", 1)
+            owners_x()
+            look("v", 0, 64)
+            look("a", 64, 128)
+            flags_y()
+            owners_y()
+            pulls()
+            pulls_out()
+            setup_late()
+            names_f(X_)
+            names_f(Y_)
+            pointer_u(X_)
+            pointer_f(X_)
+            open_main(X_)
+            lists(Y_)
         else:
-            to_list(p_oc, 4, "ocB", E_OC, T.GD, ["GD1"], 128, C, True, True)
-        tt(T.LA[:], p_la, T.RL[:], OP.subtract, ["la", "RL"], ["LA"], [1])
-        F = T.FS[:, 3 * C:4 * C] if last else T.FL[:, n0:n0 + C]
-        J, jk = (T.JA, "JA") if t <= 2 else (T.JB, "JB")
-        tt(T.WM[:], p_b, T.LA[:], OP.min, ["b", "LA"], ["WM"], [0])
-        tt(T.G1[:], p_b, T.LA[:], OP.is_gt, ["b", "LA"], ["G1"], [0])
-        tt(t0, p_n, T.WM[:], OP.mult, ["n", "WM"], ["t0"], [2, 5])
-        tt(T.G2[:], T.G1[:], p_co, OP.is_gt, ["G1", "coA", "coB"], ["G2"], [3])
-        tt(T.NH[:], t0, F, OP.is_le, ["t0", "F%d" % t], ["NH"], [5])
-        tt(t1, p_sg, T.G2[:], OP.mult, ["sg", "G2"], ["t1"], [2, 5])
-        exp_both(0)
-        exp_both(1)
-        up, lo, hi = (OP.add, OP.min, OP.max) if t <= 2 else (OP.subtract, OP.max, OP.min)
-        top = float((PZ2 if t <= 2 else PZ3) - PZ)
+            for i in range(2):
+                a, sb = zs(t) + 128 + H + 1024 * i, (t - 2) * H + 1024 * i
+                dma("s", T.P[16:128, a:a + 1024], T.SB[0:112, sb:sb + 1024], ["SB%d%d" % (t, i)], ["R%d1%d" % (t, 2 * i)])
+                dma("s", T.P[0:16, a:a + 1024], T.SB[112:128, sb:sb + 1024], ["SB%d%d" % (t, i)], ["R%d1%d" % (t, 2 * i + 1)])
+            look("a", 192, 256)
+            look("v", 128, 192)
+            exp_mm(Y_, 0, 6)
+            exp_mm(Y_, 1, 7)
+            exp_mm(Y_, 2, 0)
+            exp_mm(Y_, 3, 2)
+            lists(X_)
+            scatter_x()
+            gather_r("a", t - 1, 0, 64)
+            cells_out(0)
+            gather_r("a", t - 1, 64, 128)
+            cells_out(1)
+            exp_act(Y_, 0, 6)
+            exp_act(Y_, 3, 2)
+            scatter_y()
+            gather_v("a", t - 1, 0, 96)
+            owners_x()
+            pointer_u(X_)
+            exp_act(Y_, 1, 7)
+            names_f(X_)
+            names_f(Y_)
+            look("v", 0, 128)
+            exp_act(Y_, 2, 0)
+            owners_y()
+            flags_y()
+            fold_home(t - 1, Y_)
+            gather_v("v", t - 1, 128, 256)
+            gather_v("v", t - 1, 96, 128)
+            pointer_f(X_)
+            open_main(X_)
+            lists(Y_)
+            look_x("a", 0)
+            look_x("a", 1)
+        own_share(X_)
+        open_main(Y_)
+        both(Y_)
+        pt = pointers()
+        hx, hy = [bonds(h) + holds(h) + moves(h) for h in (X_, Y_)]
+        rx, ry = rec_lists(X_), rec_lists(Y_)
         if not last:
-            tt(t2, T.NH[:], p_oc, OP.is_gt, ["NH", "ocA", "ocB"], ["t2"], [4, 1])
-        tt(t0, t1, T.NH[:], OP.mult, ["t1", "NH"], ["t0"], [5])
-        if not last:
-            tt(t2, t2, T.DM[:], OP.mult, ["t2", "DM"], ["t2"], [1])
-            tt(t1, J[:], t0, up, [jk, "t0"], ["t1"], [5])
-            tt(T.SN[:], t2, T.NF[:], OP.add, ["t2", "NF"], ["SN"], [1])
-            mm([(p_nm, T.PBF[:, 112:240], T.SN[:, 128:C], True, True)], ["PBFa", "PBFb", "SN"], ["nm"], [0])
-            tt(T.Y1[:], t1, T.NF[:], lo, ["t1", "NF"], ["Y1"], [5])
-            ts(T.NS[:, 0:128], T.SN[:, 0:128], float(-YOFF), None, OP.add, None, ["SN"], ["NSa"])
-            ts(T.NS[:, 128:C], p_nm, float(-YOFF), None, OP.add, None, ["nm"], ["NSb"], [0])
-            send(T.NU[:, t * C:(t + 1) * C], T.NS[:], peer(1), "rn%d" % (t + 1), ["NSa", "NSb"])
-            ts(T.RU[:], T.Y1[:], 0.0, top, OP.max, OP.min, ["Y1"], ["RU"])
-            tt(t2, T.NF[:], t0, up, ["NF", "t0"], ["t2"], [5, 1])
-            exp_both(2)
-            exp_both(3)
-            owners(t)
-            gather_r("a", t, 0, 128, ["RS0", "RS1"])
-            tt(T.Y2[:], t2, J[:], hi, ["t2", jk], ["Y2"], [1])
-            gather_r("v", t, 128, C, ["RS2", "RS3"])
-            ts(T.VU[:], T.Y2[:], 0.0, top, OP.max, OP.min, ["Y2"], ["VU"])
-            cp("v", T.OU[:], p_own, ["own"], ["OU"], [3])
-            send(T.SB[:, (t - 1) * H:t * H], T.RS[:, H:K], peer(1), "rb%d" % (t + 1), ["RS2", "RS3"])
-            send(T.P0[:, t * H:(t + 1) * H], T.RS[:, 0:H], aide, "ra%d" % (t + 1), ["RS0", "RS1"])
-            if t <= 2:
-                dma("s", W[:], T.WT[:], ["WT", "WTa", "WTb"], [wk])
+            d_gather(128, 192)
+            d_gather(192, 256)
+            n_pass(X_)
+            d_pass(X_)
+            hx[0]()
+            both(X_)
+            pointer_f(Y_)
+            taken(128, 192)
+            bases(X_)
+            pt[1]()
+            taken(192, 256)
+            pointer_u(Y_)
+            hx[1]()
+            pt[0]()
+            n_swap(X_)
+            hx[2]()
+            hx[3]()
+            pt[2]()
+            hx[4]()
+            pt[3]()
+            d_gather(0, 32)
+            hx[5]()
+            taken_mm(X_)
+            pt[4]()
+            taken(0, 64)
+            swaps(X_)
+            pt[5]()
+            taken(64, 128)
+            new_table()
+            hx[6]()
+            hx[7]()
+            swaps_add(X_)
+            mask_list(X_)
+            d_gather(32, 64)
+            names_out(X_)
+            mask_keep(X_)
+            own_share(Y_)
+            rx[0]()
+            rx[1]()
+            rx[2]()
+            exp_mm(X_, 0, 0)
+            exp_mm(X_, 1, 2)
+            gather_r("a", t, 128, 192)
+            cells_out(2, t + 1)
+            d_gather(64, 128)
+            bases(Y_)
+            rx[3]()
+            d_pass(Y_)
+            n_pass(Y_)
+            exp_act(X_, 0, 0)
+            exp_act(X_, 1, 2)
+            taken_mm(Y_)
+            hy[0]()
+            n_swap(Y_)
+            hy[1]()
+            hy[2]()
+            hy[3]()
+            exp_mm(X_, 2, 0)
+            hy[4]()
+            exp_mm(X_, 3, 2)
+            hy[5]()
+            swaps(Y_)
+            gather_r("a", t, 192, 256)
+            hy[6]()
+            hy[7]()
+            swaps_add(Y_)
+            mask_list(Y_)
+            names_out(Y_)
+            exp_act(X_, 2, 0)
+            exp_act(X_, 3, 2)
+            fold_home(t, X_)
+            cells_out(3, t + 1)
+            ry[0]()
+            ry[1]()
+            ry[2]()
+            ry[3]()
+            mask_keep(Y_)
             continue
 
-        tt(t2, T.NF[:], t0, up, ["NF", "t0"], ["t2"], [5, 1])
-        tt(t1, J[:], t0, up, [jk, "t0"], ["t1"], [5])
-        tt(T.Y2[:], t2, J[:], hi, ["t2", jk], ["Y2"], [1])
-        tt(T.Y1[:], t1, T.NF[:], lo, ["t1", "NF"], ["Y1"], [5])
-        ts(T.VU[:], T.Y2[:], 0.0, top, OP.max, OP.min, ["Y2"], ["VU"])
-        ts(T.RU[:], T.Y1[:], 0.0, top, OP.max, OP.min, ["Y1"], ["RU"])
-        pb = ["PBFa", "PBFb"]
-        ea, eb = B[4][:, 0:128], B[1][:, 0:128]
-
-        def totals(j):
-            it = []
-            for k in (2 * j, 2 * j + 1):
-                it += [(ea, T.PBF[:, 0:128], T.X[:, k * C:k * C + 128], k == 0, False),
-                       (eb, T.PBF[:, 64:192], T.X[:, k * C + 128:(k + 1) * C], k == 0, False)]
-            mm(it, pb + ["X%d" % j], ["ea", "eb"], [4, 1])
-
-        def mix(src, keys, h, b, turn, out, okey, dst, q):
-            x = 64 if turn else 0
-            mats = (T.PB1[:], T.PBM[:], T.PB2[:, x:x + 128], T.PBN[:, x:x + 128])
-            mm([(B[b][:], mats[e], src[:, 1024 * e + 512 * h:1024 * e + 512 * h + 512], e == 0, e == 3) for e in range(4)],
-               keys + ["PB1", "PBM", "PB2", "PBN"], ["o%d" % b], [b])
-
-            def store():
-                cp(q, out[:, 512 * h:512 * h + 512], B[b][:], ["o%d" % b], [okey], [b])
-                dma("s", dst[:, 512 * h:512 * h + 512], out[:, 512 * h:512 * h + 512], [okey], [])
-            return store
-        Yn = pool(t + 1)[:, PY:PY + K]
-        exp_both(2)
-        gather_v("v", t, 1)
-        gather_v("a", t, 0)
-        exp_both(3)
-        totals(0)
-        exp_both(4)
-        totals(1)
-        totals(2)
-        for e in range(4):
-            gather_r("v", t, 64 * e, 64 * e + 32, ["RS%d" % e])
-        for e in range(4):
-            gather_y("a", t, 64 * e, 64 * e + 32, ["Yf0%d" % e, "Y0", "Y0b"][:3 if e == 0 else 1])
-        for e in range(4):
-            gather_y("v", t, 64 * e + 32, 64 * e + 64, ["Yf1%d" % e])
-        exp_mm(5)
-        exp_mm(6)
-        st_r0 = mix(T.RS, ["RS%d" % e for e in range(4)], 0, 0, True, T.YR, "YR0", T.yr, "a")
-        totals(3)
-        exp_act(5)
-        exp_act(6)
-        st_r0()
-        st_w0 = mix(Yn, ["Yf0%d" % e for e in range(4)], 0, 2, False, T.YW, "YW0", T.yw, "a")
-        exp_both(7)
-        st_w0()
-        totals(4)
-        st_w1 = mix(Yn, ["Yf1%d" % e for e in range(4)], 1, 3, False, T.YW, "YW1", T.yw, "v")
-        for e in range(3):
-            gather_r("v", t, 64 * e + 32, 64 * e + 64, ["RT%d" % e])
-        gather_r("a", t, 64 * 3 + 32, 64 * 3 + 64, ["RT3"])
-        st_w1()
-        totals(5)
-        totals(6)
-        st_r1 = mix(T.RS, ["RT%d" % e for e in range(4)], 1, 5, True, T.YR, "YR1", T.yr, "a")
-        totals(7)
-        mm([(ea, T.PBF[:, 0:128], T.EL[:, 2 * C:2 * C + 128], False, True),
-            (eb, T.PBF[:, 48:176], T.EL[:, 2 * C + 128:3 * C], False, True)], pb + ["EL3"], ["ea", "eb"], [4, 1])
-        st_r1()
-        tt(T.YE[:, 0:128], ea, T.E3[:, 0:128], OP.add, ["ea", "E3"], ["YEa"], [4])
-        tt(T.YE[:, 128:C], eb, T.E3[:, 128:C], OP.add, ["eb", "E3"], ["YEb"], [1])
-        dma("a", T.ye[:], T.YE[:], ["YEa", "YEb"], [])
+        d_gather(128, 192)
+        d_gather(192, 256)
+        d_pass(X_)
+        bases(X_)
+        n_pass(X_)
+        both(X_)
+        pointer_u(Y_)
+        pt[0]()
+        hx[0]()
+        pointer_f(Y_)
+        n_swap(X_)
+        hx[1]()
+        pt[1]()
+        hx[2]()
+        hx[3]()
+        pt[2]()
+        hx[4]()
+        pt[3]()
+        hx[5]()
+        swaps(X_)
+        mask_list(X_)
+        mask_keep(X_)
+        pt[4]()
+        pt[5]()
+        new_table()
+        swaps_add(X_)
+        exp_half(X_, 0, 0)
+        rx[1]()
+        rx[0]()
+        rx[3]()
+        rx[2]()
+        exp_half(X_, 1, 2)
+        own_share(Y_)
+        d_gather(0, 64)
+        gather_v("a", t, 128, 192)
+        exp_half(X_, 2, 0)
+        exp_half(X_, 3, 2)
+        d_gather(64, 128)
+        d_pass(Y_)
+        bases(Y_)
+        n_pass(Y_)
+        gather_v("a", t, 192, 256)
+        earlier(X_, (1, 2), True, False)
+        n_swap(Y_)
+        hy[1]()
+        hy[0]()
+        totals(X_, 0)
+        hy[2]()
+        hy[3]()
+        gather_r("a", t, 128, 192)
+        totals(X_, 1)
+        hy[4]()
+        hy[5]()
+        swaps(Y_)
+        mask_list(Y_)
+        swaps_add(Y_)
+        mask_keep(Y_)
+        exp_half(Y_, 0, 6)
+        ry[1]()
+        ry[0]()
+        ry[3]()
+        ry[2]()
+        exp_half(Y_, 1, 7)
+        last_pointers()
+        gather_v("v", t, 0, 64)
+        gather_v("a", t, 64, 128)
+        last_offsets()
+        exp_half(Y_, 2, 6)
+        exp_half(Y_, 3, 7)
+        gather_r("v", t, 192, 256)
+        totals(X_, 2)
+        totals(X_, 3)
+        earlier(X_, (3,), False, True)
+        earlier(Y_, (1, 2, 3), True, False)
+        pair_y(0, 0, "v")
+        pair_y(0, 1, "a")
+        pair_y(0, 0)
+        pair_y(1, 0, "a")
+        pair_y(0, 1)
+        pair_y(1, 1, "a")
+        totals(Y_, 0)
+        totals(Y_, 1)
+        mix_w(0)
+        mix_x(0)
+        mix_x(1)
+        totals(Y_, 2)
+        totals(Y_, 3, True)
+        pair_r(0, "a")
+        pair_y(1, 0)
+        pair_y(1, 1)
+        pair_r(1, "a")
+        pair_r(0)
+        pair_r(1)
+        mix_y(0)
+        store("a", 1, T.YW, "YW0", T.yw, 0)
+        mix_w(1)
+        mix_y(1)
+        totals_out("v", X_)
+        totals_out("v", Y_)
+        store("a", 0, T.YR, "YR0", T.yr, 0)
+        store("v", 2, T.YR, "YR1", T.yr, 1)
+        dma("a", T.ye[:], T.NF[:], ["NF0", "NF1"], [])
+        store("a", 5, T.YW, "YW1", T.yw, 1)
 
     for s, v in final.items():
         if all(seen[q].get(s, 0) < v for q in Q):

@@ -6,55 +6,67 @@ K = 4096
 H = 2048
 C = 256
 STEPS = 4
-U = K + 128
-Y0, PEND = 4 * U, 9 * U - 128
-X_, Y_ = 1, 0
+Y0 = 256
+PEND = Y0 + 9 * K
+Y_, X_ = 0, 1
 BIG = 8192.0
-LARGE = 131072.0
+LARGE = 65536.0
+CODE = 81920.0
 FAR = 20.0
-R_ID, R_FX, R_PT, R_DN, R_FY = 0, 2, 4, 8, 12
+ROUND = 1.5 * 2.0 ** 31
+R_PT, R_DN, R_FLAG = 0, 1, (8, 12)
+R_V, R_A = 2, 6
 
 SCRATCH = {
-    "P": ("sbuf", [128, PEND], "bfloat16"),
-    "SB": ("sbuf", [128, 3 * H], "bfloat16"), "RS": ("sbuf", [128, K], "bfloat16"),
-    "W": ("sbuf", [128, K], "bfloat16"), "CX": ("sbuf", [128, H], "bfloat16"),
-    "WY": ("sbuf", [128, K], "float32"), "CY": ("sbuf", [128, H], "float32"),
-    "D": ("sbuf", [128, K], "bfloat16"), "NN": ("sbuf", [128, K], "bfloat16"),
-    "GL": ("sbuf", [128, K], "bfloat16"), "GX": ("sbuf", [128, H], "bfloat16"), "OC": ("sbuf", [128, K], "bfloat16"),
-    "X": ("sbuf", [128, K], "float32"),
-    "YW": ("sbuf", [128, 1024], "float32"), "YR": ("sbuf", [128, 1024], "float32"),
-    "SEL": ("sbuf", [128, 16 * 128], "bfloat16"), "EX": ("sbuf", [128, 3 * 144], "bfloat16"),
-    "TW": ("sbuf", [128, 120], "bfloat16"), "GM": ("sbuf", [128, 32], "bfloat16"), "BD": ("sbuf", [128, 128], "bfloat16"),
-    "PBF": ("sbuf", [128, 256], "float32"), "PBG": ("sbuf", [128, 128], "float32"),
-    "PB1": ("sbuf", [128, 128], "bfloat16"), "PBM": ("sbuf", [128, 128], "bfloat16"), "PB8": ("sbuf", [128, 128], "bfloat16"),
+    "P": ("sbuf", [128, PEND], "bfloat16"), "RS": ("sbuf", [128, K], "bfloat16"),
+    "W": ("sbuf", [128, K], "float32"), "WV": ("sbuf", [128, K], "float32"), "WA": ("sbuf", [128, K], "float32"),
+    "CS": ("sbuf", [128, H], "float32"),
+    "D": ("sbuf", [128, 2 * K], "bfloat16"), "NN": ("sbuf", [128, 2 * K], "bfloat16"),
+    "GL": ("sbuf", [128, K], "bfloat16"), "X": ("sbuf", [128, K], "float32"),
+    "SEL": ("sbuf", [128, 16 * 128], "bfloat16"), "EX": ("sbuf", [128, 2 * 144], "bfloat16"),
+    "TW": ("sbuf", [128, 96], "bfloat16"), "GM": ("sbuf", [128, 32], "bfloat16"), "BD": ("sbuf", [128, 128], "bfloat16"),
+    "PBF": ("sbuf", [128, 256], "float32"), "PB1": ("sbuf", [128, 128], "bfloat16"), "PBM": ("sbuf", [128, 128], "bfloat16"),
     "PZ0": ("sbuf", [128, 128], "bfloat16"), "PZ1": ("sbuf", [128, 128], "bfloat16"),
     "PB2": ("sbuf", [128, 256], "bfloat16"), "PBN": ("sbuf", [128, 256], "bfloat16"),
-    "KM": ("sbuf", [128, 768], "bfloat16"), "KB": ("sbuf", [128, 4 * C], "bfloat16"), "RB": ("sbuf", [128, 256], "float32"),
-    "L": ("sbuf", [128, 256], "float32"), "XG": ("sbuf", [128, 256], "float32"),
-    "PI": ("sbuf", [128, 4], "int32"), "PF": ("sbuf", [128, 16], "float32"), "CB": ("sbuf", [128, 8], "float32"),
-    "M16": ("sbuf", [128, 16], "float32"),
-    "NI": ("sbuf", [128, C], "int32"), "DI": ("sbuf", [128, C], "int32"), "PL": ("sbuf", [128, C], "int32"),
-    "DB": ("sbuf", [128, 2 * C], "bfloat16"),
-    "FS": ("sbuf", [128, 4 * C], "float32"), "FL": ("sbuf", [128, 3 * C], "float32"), "EL": ("sbuf", [128, 3 * C], "float32"),
+    "KM": ("sbuf", [128, 256], "bfloat16"), "LK": ("sbuf", [128, 512], "bfloat16"), "RK": ("sbuf", [128, 768], "bfloat16"),
+    "L": ("sbuf", [128, 256], "float32"), "XG": ("sbuf", [128, 256], "float32"), "ZF": ("sbuf", [128, 256], "float32"),
+    "PI": ("sbuf", [128, 4], "int32"), "PF": ("sbuf", [128, 16], "float32"), "M16": ("sbuf", [128, 16], "float32"),
+    "DI": ("sbuf", [128, 2 * C], "int32"), "TT": ("sbuf", [128, 2 * C], "float32"), "HL": ("sbuf", [128, 2 * C], "float32"),
+    "PL": ("sbuf", [128, C], "int32"), "FL": ("sbuf", [128, 4 * C], "float32"), "EL": ("sbuf", [128, 4 * C], "float32"),
     "NU": ("sbuf", [128, 4 * C], "uint16"), "NS": ("sbuf", [128, C], "uint16"),
-    "OU": ("sbuf", [128, C], "uint16"), "DU": ("sbuf", [128, C], "uint16"), "PU": ("sbuf", [128, C], "uint16"),
-    "RU": ("sbuf", [128, C], "uint16"), "VU": ("sbuf", [128, C], "uint16"),
-    "NF": ("sbuf", [128, C], "float32"), "YJ": ("sbuf", [128, 2 * C], "float32"),
-    "OF": ("sbuf", [128, C], "float32"), "TY": ("sbuf", [128, C], "float32"),
-    "RE": ("sbuf", [128, C], "float32"), "WM": ("sbuf", [128, C], "float32"), "TB": ("sbuf", [128, 384], "float32"),
+    "PD": ("sbuf", [128, 2 * C], "uint16"), "RV": ("sbuf", [128, 2 * C], "uint16"),
+    "NF": ("sbuf", [128, C], "float32"), "RE": ("sbuf", [128, C], "float32"), "WM": ("sbuf", [128, C], "float32"),
+    "DS": ("sbuf", [128, C], "float32"), "ST": ("sbuf", [128, C], "float32"), "PQ": ("sbuf", [128, 2 * C], "float32"),
     "BT": ("sbuf", [128, C], "bfloat16"), "BL": ("sbuf", [128, C], "bfloat16"),
-    "NT": ("sbuf", [128, C], "bfloat16"), "NH": ("sbuf", [128, C], "bfloat16"), "ZZ": ("sbuf", [128, 2 * C], "bfloat16"),
+    "HD": ("sbuf", [128, C], "bfloat16"), "NH": ("sbuf", [128, C], "bfloat16"), "ZZ": ("sbuf", [128, 2 * C], "bfloat16"),
 }
-for _b in range(8):
-    SCRATCH["B%d" % _b] = ("psum", [128, 512], "float32")
+for _b in range(4):
+    SCRATCH["B%d" % _b] = ("psum", [128, 1024], "float32")
 
-SEMAPHORES = (["qv", "qa", "qp", "qg"] + ["d%d" % i for i in range(64)] + ["l%d" % i for i in range(36)]
-              + ["%s%d" % (n, t) for n in ("nx", "ny", "ra", "rb", "rc", "rd") for t in range(1, 5)]
-              + ["%s%d" % (n, t) for n in ("re", "rf", "rg") for t in range(1, 4)])
+SEMAPHORES = (["qv", "qa", "qp", "qg"] + ["d%d" % i for i in range(70)] + ["l%d" % i for i in range(38)]
+              + ["%s%d" % (n, t) for n in ("nx", "ny", "ra", "rb", "rc", "rd", "re") for t in range(1, 5)]
+              + ["rf%d" % t for t in range(1, 4)])
 
 
-def zs(t):
-    return (STEPS - t) * U
+def rs(t):
+    return Y0 + (2 * t - 1) * K
+
+
+def vs(t):
+    return Y0 + 2 * t * K
+
+
+def lead(t):
+    return t % 2
+
+
+def straight(u, i):
+    return i % 2 == (u > 1)
+
+
+def quarter(u, i):
+    a = rs(u) + 1024 * i if i < 2 or u == 1 else vs(u) + 1024 * (i - 2)
+    return a, ("ra%d", "rd%d", "rb%d", "rc%d")[i] % u
 
 
 def rank_program(g, core, T, topo):
@@ -78,23 +90,27 @@ def rank_program(g, core, T, topo):
         return buf[:, n * h:n * (h + 1)]
 
     def rec(t, i, n=H):
-        return T.P[:, zs(t) + 128 + i * n:zs(t) + 128 + (i + 1) * n]
+        return T.P[:, rs(t) + i * n:rs(t) + (i + 1) * n]
 
     if rank is None:
         for r, c in enumerate(cores):
             if core in (helper(c), near(c)):
-                if core == helper(c):
-                    jobs = [([("ra%d", "rd%d")[i] % t], rec(t, i, 1024), half(T.P, 2 * t - 2 + i, 1024), r + 1)
-                            for t in range(1, STEPS + 1) for i in range(2)]
-                else:
-                    jobs = [(["re%d" % t, "rg%d" % t], half(T.EL, t - 1, C), half(T.EL, t - 1, C), r - t) for t in range(1, STEPS)]
+                jobs = []
+                for t in range(1, STEPS + 1):
+                    if core == helper(c):
+                        for i in (3, 1) if t == 1 else (2 - 2 * lead(t), 2 * lead(t)):
+                            a, sem = quarter(t, i)
+                            jobs.append(([sem], T.P[:, a:a + 1024], r + 1, inner(c)))
+                    else:
+                        buf = half(T.EL, t - 1, C) if t < STEPS else half(T.EL, 2 * t - 2 + lead(t))
+                        jobs.append((["re%d" % t], buf, r - t, topo.engines(c, core)))
                 total = 0
-                for sems, out, in_, to in jobs:
+                for sems, buf, to, en in jobs:
                     dst = cores[to % n_ranks]
                     rid, pid, _ = topo.addr(dst)
                     for sem in sems:
-                        g.wait_ge(T.sem[sem], len(inner(c)))
-                    g.remote_dma(out, in_, T.sem[sems[0]], T.sem.l0, pid, rid, topo.mask(core, dst))
+                        g.wait_ge(T.sem[sem], len(en))
+                    g.remote_dma(buf, buf, T.sem[sems[0]], T.sem.l0, pid, rid, topo.mask(core, dst))
                     total += len(topo.engines(core, dst))
                 g.wait_ge(T.sem.l0, total)
         return
@@ -185,12 +201,6 @@ def rank_program(g, core, T, topo):
     def act(out, a, f, reads, writes, banks=(), **kw):
         op("a", lambda: g.scalar.activation(out, a, f, **kw), reads, writes, banks)
 
-    def scaled(q, out, a, col, reads, writes, banks=()):
-        if q == "v":
-            ts(out, a, col, None, OP.mult, None, reads, writes, banks)
-        else:
-            act(out, a, AF.Identity, reads, writes, banks, scale=col)
-
     def fill(ap, v, key):
         op("v", lambda: g.vector.memset(ap, v), [], [key])
 
@@ -200,6 +210,12 @@ def rank_program(g, core, T, topo):
     def spot(out, in_, pat, v, base, reads, key):
         op("g", lambda: g.affine_select(out, in_, pat, OP.not_equal, v, base, 1), reads, [key])
 
+    def only(ap, r, v, key):
+        op("g", lambda: g.affine_select(ap, ap, [[0, ap.shape[1]]], OP.is_equal, v, -r, 1), [key], [key])
+
+    def put(ap, r, v, key):
+        spot(ap, ap, [[0, ap.shape[1]]], v, -r, [key], key)
+
     def mm(items, reads, writes, banks):
         def run():
             ins = None
@@ -208,41 +224,64 @@ def rank_program(g, core, T, topo):
             return ins
         op("p", run, reads, writes, banks)
 
-    B = [T["B%d" % b] for b in range(8)]
-    E_PT, E_DN, E_ID = range(3)
+    B = [half(T["B%d" % (b // 2)], b % 2, 512) for b in range(8)]
 
-    def to_list(out, b, key, e, cols, skeys, first=()):
-        x = 144 * e + 15
-        it = [(out, T.PB1[:], a, i == 0, False) for i, a in enumerate(first)]
-        it += [(out, T.EX[:, x - k:x - k + 128], cols(k), not first and k == 0, k == 15) for k in range(16)]
-        mm(it, skeys + ["EX%d" % e] + (["KB", "PB1"] if first else []), [key], [b])
-
-    def to_cells(b, q0, w, src, skeys, keys, stop=False):
+    def to_cells(b, q0, w, src, skeys, keys, alone=False, stop=False):
         n = w.shape[1] // 8
-        mm([(B[b][:, 128 * q0 + k:128 * (q0 + n):16], src[:, k:H:16], w, False, stop and k == 15) for k in range(16)], skeys, keys, [b])
+        mm([(B[b][:, 128 * q0 + k:128 * (q0 + n):16], src[:, k:H:16], w, alone, alone or (stop and k == 15)) for k in range(16)], skeys, keys, [b])
 
     def row(buf, r):
         return buf[r:128:16, :]
 
-    src_n = len(topo.engines(peer(-1), core))
-    lands("nx1", src_n, ["NU11", "NU10"])
-    lands("rb1", src_n, ["R11%d" % i for i in range(4)])
-    for t in range(1, STEPS + 1):
-        lands("ra%d" % t, len(topo.engines(helper(peer(-1)), core)), ["R%d00" % t])
-        lands("rd%d" % t, len(topo.engines(helper(peer(-1)), core)), ["R%d01" % t])
-        if t > 1:
-            lands("nx%d" % t, src_n, ["NU%d1" % t])
-            lands("ny%d" % t, src_n, ["NU%d0" % t])
-            lands("rb%d" % t, src_n, ["SB%d0" % t])
-            lands("rc%d" % t, src_n, ["SB%d1" % t])
-        if t < STEPS:
-            lands("rf%d" % t, 2, ["F%d" % t])
-            lands("re%d" % t, len(topo.engines(near(peer(t)), core)), ["EL%d" % t])
+    def pieces(name, c0, c1, n=32):
+        return ["%s%d" % (name, c) for c in range(c0 // n, (c1 + n - 1) // n)]
 
-    dma("s", T.NI[:, 0:128], T.nm[:, 0:128], [], ["NIa"])
-    dma("a", T.NI[16:128, 128:256], T.nm[0:112, 128:256], [], ["NIb"])
-    dma("s", T.NI[0:16, 128:256], T.nm[112:128, 128:256], [], ["NIc"])
-    dma("a", T.DI[:], T.dn[:], [], ["DI"])
+    def of(name, h):
+        return pieces(name, 128 * h, 128 * h + 128)
+
+    src_n = len(topo.engines(peer(-1), core))
+    lands("nx1", src_n, ["NU10", "NU11"])
+    for t in range(1, STEPS + 1):
+        lands("re%d" % t, len(topo.engines(near(peer(t)), core)), ["EL%d" % t])
+        for i in range(4):
+            n = src_n if straight(t, i) else len(topo.engines(helper(peer(-1)), core))
+            lands(quarter(t, i)[1], n, ["R%d0%d" % (t, i)] if i < 2 else ["SB%d%d" % (t, i - 2)] if t > 1 else ["R11%d" % (2 * i - 4), "R11%d" % (2 * i - 3)])
+        if t > 1:
+            lands("ny%d" % t, src_n, ["NU%d0" % t])
+            lands("nx%d" % t, src_n, ["NU%d1" % t])
+        if t < STEPS:
+            lands("rf%d" % t, len(topo.engines(peer(-t), core)), ["F%d" % t])
+
+    xp = B[4][:, C:2 * C]
+    wk_ = ["W", "W2", "Wp", "Wq", "Wd", "We", "Wf0", "Wf1"]
+
+    def parts(src, reads, r, keys, banks=(), buf=T.HL, name="HL"):
+        hi, lo = half(buf, 0, C), half(buf, 1, C)
+        return [lambda: ts(hi, src, ROUND, -ROUND, OP.add, OP.add, reads, [name + "0"], banks),
+                lambda: tt(lo, src, hi, OP.subtract, reads + [name + "0"], [name + "1"], banks),
+                lambda: (need("s", [], keys), dma("s", row(T.W, r), hi, [name + "0"], keys[:1]),
+                         dma("s", row(T.W, r + 4), lo, [name + "1"], keys[1:]))]
+
+    tab = {"v": (T.WV, R_V, "WV", 0), "a": (T.WA, R_A, "WA", 1)}
+
+    def clear(q, first=False):
+        buf, r, key, _ = tab[q]
+        if first:
+            for i in range(2):
+                dma("s", half(row(buf, r), i, H), row(T.CS, r + 9), ["CS"], [key + str(i)])
+        else:
+            dma("s", row(buf, r), row(T.W, r + 9), ["W", "W2"], [key])
+
+    def cells_out(i, u, keys=None):
+        a, sem = quarter(u, i)
+        send(T.P[:, a:a + 1024], half(T.RS, i, 1024), peer(1) if straight(u, i) else aide, sem, keys or pieces("RQ", 64 * i, 64 * i + 64))
+
+    NI = half(T.DI, 1, C)
+    dma("s", NI[:, 0:128], T.nm[:, 0:128], [], ["NIa"])
+    dma("a", NI[16:128, 128:256], T.nm[0:112, 128:256], [], ["NIb"])
+    dma("s", NI[0:16, 128:256], T.nm[112:128, 128:256], [], ["NIc"])
+    dma("a", half(T.DI, 0, C), T.dn[:], [], ["DN"])
+    dma("a", T.PL[0:8, :], T.pl[:], [], ["PL"])
     dma("s", T.RS[16:128, H:K], T.rc[0:112, H:K], [], ["RS2"])
     dma("a", T.RS[0:16, H:K], T.rc[112:128, H:K], [], ["RS3"])
     dma("s", T.RS[:, 0:H], T.rc[:, 0:H], [], ["RS0", "RS1"])
@@ -251,643 +290,574 @@ def rank_program(g, core, T, topo):
     iota(T.L[:], [[1, 256]], 0, 0, "L")
     iota(T.XG[:], [[0, 2], [1, 8], [0, 16]], 0, 0, "XG")
 
-    idn = AF.Identity
-    fill(T.W[:], 0.0, "W")
-    cp("a", T.CY[:], T.W[:, 0:H], ["W"], ["CY"])
-    cp("a", T.WY[:], T.W[:], ["W"], ["WY"])
+    fill(T.GL[:, 0:H], 0.0, "GL0")
+    fill(T.ZF[:], 0.0, "ZF")
+    cp("a", T.CS[:], T.GL[:, 0:H], ["GL0"], ["CS"])
+    act(half(T.W, 0, H), T.GL[:, 0:H], AF.Sigmoid, ["GL0"], ["W"], bias=-200.0)
     ts(T.PI[:, 1:2], T.PI[:, 0:1], 15, None, OP.bitwise_and, None, ["PI0"], ["PI1"])
     ts(T.PI[:, 2:3], T.PI[:, 0:1], 4, None, OP.arith_shift_right, None, ["PI0"], ["PI2"])
+    fill(T.KM[:], 0.0, "KM")
     cp("v", T.PF[:, 0:3], T.PI[:, 0:3], ["PI0", "PI1", "PI2"], ["PF"])
-    cp("v", T.NS[:], T.NI[:], ["NIa", "NIb", "NIc"], ["NS0", "NS1"])
-    send(T.NU[:, 0:C], T.NS[:], peer(1), "nx1", ["NS0", "NS1"])
-    fill(T.KM[:, 0:512], 0.0, "KM")
-    z, zz = half(T.TY, 0), half(T.TY, 1)
-    ts(T.CB[:, 6:7], T.PF[:, 1:2], 128.0, None, OP.mult, None, ["PF"], ["CB6"])
+    z, zz, zx = half(T.TT, 0), half(T.TT, 1), half(T.TT, 2)
+    ts(T.PF[:, 6:7], T.PF[:, 1:2], 128.0, None, OP.mult, None, ["PF"], ["PF6"])
     ts(T.M16[:], T.L[:, 0:16], T.PF[:, 1:2], None, OP.is_equal, None, ["L", "PF"], ["M16"])
-    ts(z, T.L[:, 0:128], T.CB[:, 6:7], 1.0 / 65536, OP.add, OP.mult, ["L", "CB6"], ["TYa"])
-    cp("v", T.DB[:, 0:C], T.DI[:], ["DI"], ["DBa"])
-    tt(zz, z, z, OP.mult, ["TYa"], ["TY"])
-    tt(T.DB[:, C:2 * C], T.DI[:], T.DB[:, 0:C], OP.subtract, ["DI", "DBa"], ["DBb"])
-    ts(zz, zz, 16.0 / 3, 4.0, OP.mult, OP.add, ["TY"], ["TY"])
-    m = [T.M16[:, k:k + 1] for k in range(16)]
-    ts(T.CB[:, 5:6], m[R_ID], 16.0, m[R_FX], OP.mult, OP.add, ["M16"], ["CB5"])
-    tt(z, z, zz, OP.mult, ["TYa", "TY"], ["TYa"])
-    dma("s", row(T.CY, R_FY), z, ["TYa"], ["CY"])
-    need("s", [], ["W"])
-    dma("s", row(T.W, R_DN), T.DB[:, 0:C], ["DBa"], ["Wa"])
-    dma("s", row(T.W, R_DN + 1), T.DB[:, C:2 * C], ["DBb"], ["Wb"])
-    for i in range(4):
-        ts(T.CB[:, i:i + 1], m[R_ID], float(1 << i), None, OP.mult, None, ["M16"], ["CB%d" % i])
-    ts(T.CX[:, 0:128], T.L[:, 0:128], m[R_ID + 1], T.CB[:, 5:6], OP.mult, OP.add, ["L", "M16", "CB5"], ["CX"])
-    ts(T.GM[:, 0:16], T.XG[:, 0:256:16], T.PF[:, 2:3], None, OP.is_equal, None, ["XG", "PF"], ["GM"])
-    for i in range(4):
-        w = 128 << i
-        ts(T.CX[:, w:2 * w], T.CX[:, 0:w], T.CB[:, i:i + 1], None, OP.add, None, ["CX", "CB%d" % i], ["CX"])
-        if i == 0:
-            ts(T.GM[:, 16:32], T.XG[:, 0:256:16], T.PF[:, 2:3], -1.0, OP.is_equal, OP.mult, ["XG", "PF"], ["GMb"])
-    send(T.P[:, 0:1024], T.RS[:, 0:1024], aide, "ra1", ["RS0"])
-    send(T.P[:, 1024:H], T.RS[:, 1024:H], aide, "rd1", ["RS1"])
-    for name, v in (("PB1", 1.0), ("PBF", 1.0), ("PB2", 2.0), ("PBM", -1.0), ("PBG", -1.0), ("PB8", BIG),
-                    ("PZ1", 2 * LARGE), ("PZ0", -LARGE), ("PBN", -2.0)):
-        n = T[name].shape[1]
-        spot(T[name][:], T.KM[:, 0:n], [[0, n // 128], [-1, 128]], v, 0, ["KM"], name)
-    for q in "gs":
-        need(q, ["Wa", "Wb"], [])
-    send(rec(1, X_), T.RS[:, H:K], peer(1), "rb1", ["RS2", "RS3"])
-    need("s", ["CY"], [])
+    ts(z, T.L[:, 0:128], T.PF[:, 6:7], 1.0 / CODE, OP.add, OP.mult, ["L", "PF6"], ["Z0"])
+    ts(T.PF[:, 7:8], T.PF[:, 1:2], 256.0, float(Y0), OP.mult, OP.add, ["PF"], ["PF7"])
+    tt(zz, z, z, OP.mult, ["Z0"], ["Z1"])
+    ts(zx, z, 0.5, None, OP.add, None, ["Z0"], ["Z2"])
+    ts(zz, zz, 16.0 / 3, 4.0, OP.mult, OP.add, ["Z1"], ["Z1"])
+    cp("v", T.NS[:], NI, ["NIa", "NIb", "NIc"], ["NS0", "NS1"])
+    send(T.NU[:, 0:C], T.NS[:], peer(1), "nx1", ["NS0", "NS1"])
+    tt(zz, z, zz, OP.mult, ["Z0", "Z1"], ["Z1"])
+    need("s", [], ["CS"])
+    dma("s", row(T.CS, R_V), zx, ["Z2"], ["CSv"])
+    dma("s", row(T.CS, R_A), zz, ["Z1"], ["CSa"])
+    clear("v", True)
+    clear("a", True)
+    need("s", ["CSv", "CSa"], [])
     dma("s", T.P[:, Y0:Y0 + K], T.wl[:], [], ["Y0"])
-    for a, n, src, r, v in ((0, 8, 0, 15, 0.0), (8, 8, 0, 15, -16.0), (16, 16, 0, 15, -16.0), (32, 8, 16, 15, 0.0), (40, 16, 16, 15, 16.0),
-                            (56, 8, 16, 15, -4080.0), (64, 8, None, 15, -4096.0), (72, 8, None, R_DN, 1.0), (72, 8, -1, R_DN + 1, 1.0),
-                            (80, 16, None, R_FX, -BIG), (96, 16, None, R_FY, -2 * BIG), (112, 8, None, R_FX, 1.0), (112, 8, -1, R_FY, 4.0)):
-        in_ = T.KM[:, 0:n] if src is None else T.TW[:, a:a + n] if src < 0 else T.GM[:, src:src + n]
-        spot(T.TW[:, a:a + n], in_, [[0, n // 8], [-16, 8]], v, -r, ["KM", "GM", "GMb"] + (["TW%d" % a] if src == -1 else []), "TW%d" % a)
-    iota(T.KB[:, 0:4 * C], [[U, 4], [0, C]], U - 32768, 0, "KB")
-    dma("g", T.PL[0:8, :], T.pl[:], [], ["PL"])
-    tt(T.PF[:, 4:6], T.M16[:, R_PT:R_DN + 1:4], T.M16[:, R_PT + 1:R_DN + 2:4], OP.add, ["M16"], ["PF4"])
-    ts(T.PF[:, 7:8], T.PF[:, 1:2], R_FX + 0.5, None, OP.is_gt, None, ["PF"], ["MK"])
-    ts(T.PF[:, 6:7], m[R_ID], 128.0, m[R_ID + 1], OP.mult, OP.add, ["M16"], ["PF6"])
-    ts(T.PF[:, 3:4], T.PF[:, 2:3], 16.0, 15.0, OP.mult, OP.add, ["PF"], ["PF3"])
-    ts(T.PF[:, 6:7], m[R_FX], 32768.0, T.PF[:, 6:7], OP.mult, OP.add, ["M16", "PF6"], ["PF6"])
-    for i in range(8):
-        a = i * U if i < 4 else (i + 1) * U - 128
-        fill(T.P[:, a:a + 128], 0.0, "Z%d" % i)
-    for e in range(3):
-        ts(T.EX[:, 144 * e:144 * e + 144], T.L[:, 0:144], T.PF[:, 3:4], T.PF[:, 4 + e:5 + e], OP.is_equal, OP.mult, ["L", "PF3", "PF4", "PF6"], ["EX%d" % e])
-    ts(T.RB[0:8, :], T.XG[0:8, :], T.PF[0:8, 0:1], None, OP.is_equal, None, ["XG", "PF"], ["RB"])
-    ts(T.BD[:], T.XG[:, 0:128], T.PF[:, 2:3], None, OP.is_equal, None, ["XG", "PF"], ["BD"])
-    fill(T.KM[:, 512:768], -BIG, "KMb")
-    fill(T.TB[:], 0.0, "TBz")
-    act(T.PF[:, 9:10], T.PF[:, 1:2], idn, ["PF"], ["PF9"], bias=128.0)
-    act(T.PF[:, 11:12], T.PF[:, 1:2], idn, ["PF"], ["PF11"], scale=256.0)
-    act(half(T.YJ, 1), T.L[:, 0:128], idn, ["L", "PF9"], ["J0"], scale=16.0, bias=T.PF[:, 9:10])
-    act(half(T.YJ, 3), half(T.YJ, 1), idn, ["J0"], ["J1"], bias=float(H))
-    act(T.OF[:], T.L[:], idn, ["L", "PF11"], ["OF"], bias=T.PF[:, 11:12])
+    RB = T.RE[0:8, :]
+    ts(RB, T.XG[0:8, :], T.PF[0:8, 0:1], None, OP.is_equal, None, ["XG", "PF"], ["RE0", "RE1"])
+    for i, v in enumerate((1.0, -1.0, 1.0 / K, -1.0 / K)):
+        ts(half(T.GM, i, 8), T.XG[:, 0:128:16], T.PF[:, 2:3], v, OP.is_equal, OP.mult, ["XG", "PF"], ["GM%d" % i])
+    ts(T.WM[0:8, :], T.PL[0:8, :], -0.25, 0.0, OP.add, OP.max, ["PL"], ["WM0", "WM1"])
+    fill(half(T.W, 1, H), 0.0, "W2")
+    first = [parts(half(T.DI, 0, C), ["DN"], R_DN, ["Wd", "We"], (), T.PQ, "PQ"), parts(xp, ["xp"], R_PT, ["Wp", "Wq"], [4])]
+    ts(xp, T.L[:], T.PF[:, 7:8], None, OP.add, None, ["L", "PF7"], ["xp"], [4])
+    for i in range(3):
+        if i == 2:
+            need("s", [], ["W", "W2"])
+        for f in first:
+            f[i]()
 
     def pulls():
-        ts(T.WM[0:8, :], T.PL[0:8, :], -0.25, 0.0, OP.add, OP.max, ["PL"], ["WM0", "WM1"])
-
-    def pulls_out():
+        FS = T.X[:, 0:4 * C]
         for j in range(2):
             it = []
             for t in (2 * j + 1, 2 * j + 2):
                 a = (t - 1) % 2 * C
-                it.append((B[6 + j][:, a:a + 128], T.WM[0:8, 0:128], T.RB[0:8, 128:256], True, True))
-                it.append((B[6 + j][:, a + 128:a + C], T.WM[0:8, 128:256], T.RB[0:8, 128 - 16 * t:256 - 16 * t], True, True))
-            mm(it, ["RB", "WM0", "WM1"], ["x%d" % j], [6 + j])
-            cp("a", half(T.FS, j, 512), B[6 + j][:], ["x%d" % j], ["FS%d" % j] + (["F4"] if j else []), [6 + j])
-        need("g", ["FS0", "FS1"], [])
-        tr = []
-        for t in range(1, STEPS):
-            rid, pid, _ = topo.addr(peer(t))
-            en = topo.engines(core, peer(t))
-            tr.append(RemoteDMATransfer(dst_ids=[DstId(rid=rid, pnc=pid)], dma_engine_mask=(1 << en[2 * t]) | (1 << en[2 * t + 1]),
-                                        remote_sem=T.sem["rf%d" % t], src=half(T.FS, t - 1, C), dst=half(T.FL, t - 1, C)))
-        s = lsem()
-        g.remote_dma_fused(tr, local_sem=T.sem[s])
-        done((s, 2 * (STEPS - 1), "r"), ["FS0", "FS1"], [])
+                it.append((B[6 + j][:, a:a + 128], T.WM[0:8, 0:128], RB[:, 128:256], True, True))
+                it.append((B[6 + j][:, a + 128:a + C], T.WM[0:8, 128:256], RB[:, 128 - 16 * t:256 - 16 * t], True, True))
+            mm(it, ["RE0", "RE1", "WM0", "WM1"], ["o%d" % (6 + j)], [6 + j])
+        cp("a", FS[:, 0:512], B[6][:], ["o6"], ["X0"], [6])
+        cp("a", FS[:, 512:768], B[7][:, 0:C], ["o7"], ["X1"], [7])
+        cp("a", half(T.FL, 3, C), B[7][:, C:2 * C], ["o7"], ["F4"], [7])
 
-    def setup_late():
-        iota(T.SEL[:], [[0, 2048]], int(BIG), 0, "SEL")
-        op("g", lambda: g.affine_select(T.SEL[:], T.SEL[:], [[-1, 16], [-16, 8], [0, 16]], OP.is_equal, 0.0, 0, 1), ["SEL"], ["SEL"])
+    def pull_out(t):
+        send(half(T.FL, t - 1, C), half(T.X, t - 1, C), peer(t), "rf%d" % t, ["X%d" % (t // 3)])
+
+    def identities(names):
+        for name, v in names:
+            n = T[name].shape[1]
+            spot(T[name][:], (T.ZF if name == "PBF" else T.KM)[:, 0:n], [[0, n // 128], [-1, 128]], v, 0, ["KM", "ZF"], name)
+
+    for i in (3, 2, 1):
+        cells_out(i, 1, (["RS%d" % i] if i < 2 else ["RS2", "RS3"]) + (["CSv", "CSa"] if straight(1, i) else []))
+    for a, src, r, v in ((0, 0, 15, 0.0), (1, 0, 15, -16.0), (2, 2, 15, -16.0 / K), (3, 1, 15, 0.0), (4, 1, 15, 16.0), (5, 3, 15, 16.0 / K),
+                         (6, None, R_FLAG[X_], -4.0), (7, None, R_PT, 1.0), (7, -1, R_PT + 4, 1.0), (8, None, R_FLAG[Y_], -4.0),
+                         (9, None, R_PT, 1.0), (9, -1, R_PT + 4, 1.0), (10, None, 15, -1.0 / 512), (11, None, R_FLAG[0], -4.0), (11, -1, R_FLAG[1], -4.0)):
+        in_, key = (T.KM[:, 0:8], "KM") if src is None else (half(T.TW, a, 8), "TW%d" % a) if src < 0 else (half(T.GM, src, 8), "GM%d" % src)
+        spot(half(T.TW, a, 8), in_, [[-16, 8]], v, -r, [key], "TW%d" % a)
+    pulls()
+    iota(T.LK[0:7, 0:C], [[0, 2], [16, 128]], 0, 0, "LK")
+    iota(T.LK[0:7, C:2 * C], [[0, 16], [1, 16]], 0, 0, "LK")
+    only(T.LK[0:7, :], 2, 1.0, "LK")
+    put(T.LK[0:7, 0:128], 3, 0.0, "LK")
+    put(T.LK[0:7, C:C + 128], 3, 0.0, "LK")
+    own = T.RK[0:7, 384:512]
+    iota(own, [[0, 8], [-1, 16]], 0, 0, "RKa")
+    only(own, 1, -2.0 * K, "RKa")
+    for r, v in ((0, -rs(1)), (2, -1), (3, -H)):
+        put(own, r, float(v), "RKa")
+    identities((("PB1", 1.0), ("PBF", 1.0)))
+
+    def last_tables():
+        iota(T.RK[0:4, 512:768], [[0, 2], [16, 128]], 0, 0, "RKb")
+        only(T.RK[0:4, 512:768], 1, 1.0, "RKb")
+        put(T.RK[0:4, 512:768], 3, float(H), "RKb")
+        put(T.RK[0:4, 512:640], 0, rs(1) - LARGE, "RKb")
+        put(T.RK[0:4, 640:768], 0, float(rs(1)), "RKb")
+        identities((("PZ1", LARGE), ("PZ0", -LARGE), ("PB2", 2.0)))
+
+    wr["Wf0"] = wr["Wf1"] = None
+    ts(T.PF[:, 3:4], T.PF[:, 2:3], 16.0, 15.0, OP.mult, OP.add, ["PF"], ["PF3"])
+    tt(T.PF[:, 4:6], T.M16[:, 0:2], T.M16[:, 4:6], OP.add, ["M16"], ["PF4"])
+    fill(T.RK[0:7, 0:384], 0.0, "RKc")
+    fill(T.P[:, 0:Y0], 0.0, "Z")
+    for e in range(2):
+        ts(T.EX[:, 144 * e:144 * e + 144], T.L[:, 0:144], T.PF[:, 3:4], T.PF[:, 4 + e:5 + e], OP.is_equal, OP.mult, ["L", "PF3", "PF4"], ["EX%d" % e])
+    ts(T.BD[:], T.XG[:, 0:128], T.PF[:, 2:3], None, OP.is_equal, None, ["XG", "PF"], ["BD"])
+    ts(T.M16[:], T.M16[:], -BIG, None, OP.mult, None, ["M16"], ["M16"])
+
+    def spread(ks):
+        for k in ks:
+            act(half(T.SEL, k), T.BD[:], AF.Identity, ["BD", "M16"], ["SEL%d" % k], scale=T.M16[:, k:k + 1])
+
+    spread(range(5))
 
     def rkeys(t, h):
         return ["R%d1%d" % (t, i) for i in range(4)] if h else ["R%d00" % t, "R%d01" % t]
 
-    def wall_keys(t):
-        return ["Y0"] + ["Z%d" % (4 + u) for u in range(min(t, STEPS))] + ["V%d%d" % (u, q) for u in range(1, t) for q in range(8)]
+    def pool(t, r):
+        keys = ["Z", "Y0"] + [k for u in range(1, t + r) for k in rkeys(u, 0) + rkeys(u, 1)]
+        keys += [k for u in range(1, t) for k in pieces("V%d_" % u, 0, C)]
+        return T.P[:, 0:(vs(t) if r else rs(t))], keys
 
-    def rec_window(t):
-        keys = wall_keys(t) + [k for u in range(1, t + 1) for k in rkeys(u, 0) + rkeys(u, 1) + ["Z%d" % (STEPS - u)]]
-        return T.P[:, zs(t):Y0 + (t - 1) * U + K + 16], keys
+    def span(h, part):
+        return 128 * h + 32 * part[0], 128 * h + 32 * part[1]
 
-    def rsk(c0, c1):
-        return ["RQ%d" % c for c in range(c0 // 32, c1 // 32)]
+    def gather_r(q, t, h, part=(0, 4)):
+        c0, c1 = span(h, part)
+        win, wk = pool(t, 1)
+        need(q, [], ["RS%d" % (2 * h), "RS%d" % (2 * h + 1)])
+        cp(q, T.RS[:, 16 * c0:16 * c1], win.indirect(T.RV[:, 128 * h + c0:128 * h + c1]), wk + ["RU%d" % h], pieces("RQ", c0, c1))
 
-    def gather_r(q, t, c0, c1):
-        win, wk = rec_window(t)
-        need(q, [], ["RS%d" % i for i in range(4)])
-        cp(q, T.RS[:, 16 * c0:16 * c1], win.indirect(T.RU[:, c0:c1]), wk + ["RU%d" % (c0 // 128)], rsk(c0, c1))
+    def gather_v(q, t, h, part=(0, 4)):
+        c0, c1 = span(h, part)
+        win, wk = pool(t, 1)
+        sb = ["SB%d%d" % (t, i) for i in range(2)] if t > 1 and h == 0 else []
+        cp(q, T.P[:, vs(t) + 16 * c0:vs(t) + 16 * c1], win.indirect(T.RV[:, 128 * h + 128 + c0:128 * h + 128 + c1]), wk + ["VU%d" % h],
+           pieces("V%d_" % t, c0, c1) + sb)
 
-    def gather_v(q, t, c0, c1):
-        win, wk = rec_window(t)
-        a = Y0 + t * U
-        cp(q, T.P[:, a + 16 * c0:a + 16 * c1], win.indirect(T.VU[:, c0:c1]), wk + ["VU%d" % (c0 // 128)], ["V%d%d" % (t, c) for c in range(c0 // 32, c1 // 32)])
+    def dn_of(buf, t, h):
+        return half(buf, 2 * (t % 2) + h, H)
 
-    def dk(h):
-        return ["D%d" % c for c in range(8 * h, 8 * h + 8)]
+    def nu(t, c0, c1):
+        return T.NU[:, (t - 1) * C + c0:(t - 1) * C + c1]
 
-    wk_ = ["W", "Wa", "Wb", "Wc"]
-    wr["Wc"] = None
+    def scatter(q, t):
+        h = lead(t) if q == "v" else 1 - lead(t)
+        buf, r, key, _ = tab[q]
+        out, keys = buf[:].indirect(nu(t, 128 * h, 128 * h + 128)), ["NU%d%d" % (t, h), "CS", "CSv", "CSa", key + "0", key + "1"]
+        if q == "v":
+            cp("v", out, T.CS[:], keys, [key])
+        else:
+            act(out, T.CS[:], AF.Sigmoid, keys, [key])
 
-    def exp_mm(h, j, b):
-        it = []
-        for kk in range(4):
-            k = 4 * j + kk
-            o = half(B[b], kk)
-            it += [(o, T.PB1[:], T.D[:, H * h + k:H * h + H:16], True, False), (o, T.PB2[:, 0:128], T.NN[:, H * h + k:H * h + H:16], False, False),
-                   (o, half(T.SEL, k), half(T.NH, h), False, True)]
-        mm(it, ["PB1", "PB2", "SEL"] + dk(h) + ["N%d" % h, "NH%d" % h], ["o%d" % b], [b])
+    def flags(q, t, by="s"):
+        h = lead(t) if q == "v" else 1 - lead(t)
+        buf, r, key, i = tab[q]
+        dma(by, row(T.W, R_FLAG[h]), row(buf, r), [key, "W", "W2"], ["Wf%d" % h])
 
-    def exp_act(h, j, b):
-        act(half(T.X, 4 * h + j, 512), B[b][:], AF.Sigmoid, ["o%d" % b], ["X%d" % (4 * h + j)], [b], scale=-1.0 / 64, bias=-FAR)
+    def owners(q, t):
+        buf, r, key, i = tab[q]
+        dma("s", half(T.TT, i, C), row(buf, r), [key], ["TT%d" % i] + (["Z2"] if i else ["Z0", "Z1"]))
+        if t < STEPS:
+            clear(q)
 
-    def exp_half(h, j, b):
-        exp_mm(h, j, b)
-        exp_act(h, j, b)
+    terms, made = [], [0, 0]
 
-    def fold_home(t, h):
-        keys = ["X%d" % j for j in range(4 * h, 4 * h + 4)]
+    def term_bank(i):
+        return (6, 7, 0, 2)[i % 4] if i >= 8 * (STEPS - 1) else (6, 7, 0, 1, 2, 3, 6, 7)[i % 8]
+
+    def term_mm(n=1):
+        for _ in range(n):
+            t, h, j = terms[made[0]]
+            b = term_bank(made[0])
+            made[0] += 1
+            it, hs = [], (0, 1) if h is None else (h,)
+            for kk in range(4):
+                k, o = (2 * j + kk // 2 if len(hs) == 2 else 4 * j + kk), half(B[b], kk)
+                h = hs[kk % len(hs)]
+                it += [(o, T.PB1[:], dn_of(T.D, t, h)[:, k:H:16], True, False), (o, T.PB2[:, 0:128], dn_of(T.NN, t, h)[:, k:H:16], False, False),
+                       (o, half(T.SEL, k), half(T.NH, h), False, True)]
+            mm(it, ["PB1", "PB2"] + ["SEL%d" % k for k in range(16)]
+               + [k for h in hs for k in ["NH%d" % h] + of("D%d_" % (t % 2), h) + of("N%d_" % (t % 2), h)], ["o%d" % b], [b])
+
+    def term_buf(t):
+        return (T.W, "XL%d") if t == STEPS else (T.X, "X%d")
+
+    def term_act(n=2):
+        t, h, j = terms[made[1]]
+        b = term_bank(made[1])
+        made[1] += n
+        x = j if h is None else 4 * (h != lead(t)) + j
+        buf, key = term_buf(t)
+        act(buf[:, 512 * x:512 * (x + n)], T["B%d" % (b // 2)][:, 512 * (b % 2):512 * (b % 2 + n)], AF.Sigmoid, ["o%d" % (b + i) for i in range(n)],
+            [key % (x + i) for i in range(n)], [b + i for i in range(n)], scale=-1.0 / 64, bias=-FAR - BIG / 64)
+
+    def fold_home(t):
+        buf, key = term_buf(t)
+        n, dst = (C, half(T.EL, t - 1, C)) if t < STEPS else (128, half(T.EL, 2 * t - 2 + lead(t)))
+        keys = [key % j for j in range(n // 32)]
         need("g", keys, [])
         rid, pid, _ = topo.addr(near(core))
         s = lsem()
-        g.remote_dma_fused([RemoteDMATransfer(dst_ids=[DstId(rid=rid, pnc=pid)], dma_engine_mask=aide_mask, remote_sem=T.sem[("re%d", "rg%d")[h] % t],
-                                              srcs=[half(T.X, 16 * h + k) for k in range(16)], dsts=[half(T.EL, 2 * t - 2 + h)], alu_op=1)], local_sem=T.sem[s])
-        done((s, len(inner(core)), "r"), keys, [])
+        g.remote_dma_fused([RemoteDMATransfer(dst_ids=[DstId(rid=rid, pnc=pid)], dma_engine_mask=topo.mask(core, near(core)), remote_sem=T.sem["re%d" % t],
+                                              srcs=[half(buf, k, n) for k in range(16)], dsts=[dst], alu_op=1)], local_sem=T.sem[s])
+        done((s, len(topo.engines(core, near(core))), "r"), keys, [])
 
-    def totals(h, j, stop=False):
-        mm([(B[3 + h][:, 0:128], T.PBF[:, 64 * h:64 * h + 128], half(T.X, 16 * h + 4 * j + kk), False, stop and kk == 3) for kk in range(4)],
-           ["PBF", "X%d" % (4 * h + j)], ["e%d" % h], [3 + h])
+    def totals(us):
+        mm([(half(B[4], h), T.PBF[:, 16 * u * h:16 * u * h + 128], half(T.EL, 2 * u - 2 + h), False, u == STEPS)
+            for u in us for h in ((0, 1) if u < STEPS else (lead(u),))], ["PBF"] + ["EL%d" % u for u in us], ["e"], [4])
 
-    def earlier(h, us, start, stop):
-        mm([(B[3 + h][:, 0:128], T.PBF[:, 16 * u * h:16 * u * h + 128], half(T.EL, 2 * u - 2 + h), start and u == us[0], stop and u == us[-1]) for u in us],
-           ["PBF"] + ["EL%d" % u for u in us], ["e%d" % h], [3 + h])
+    def summed(h, j):
+        mm([(half(B[4], h), T.PBF[:, 64 * h:64 * h + 128], half(T.W, 16 + 4 * j + kk), False, False) for kk in range(4)], ["PBF", "XL%d" % (4 + j)], ["e"], [4])
 
-    def mix(b, parts, keys, start, stop):
-        mm([(B[b][:], w, src, start and i == 0, stop and i == len(parts) - 1) for i, (w, src) in enumerate(parts)],
-           keys + ["PB1", "PB2", "PBN"], ["o%d" % b], [b])
-
-    def mix_w(j):
-        mix(1 + 4 * j, [(T.PB1[:], half(T.OC, j, 512)), (T.PB2[:, 0:128], half(T.OC, 4 + j, 512))], ["y%d0" % j, "y%d1" % j], True, True)
-
-    def mix_x(j):
-        mix(2 * j, [(T.PB2[:, 64:192], half(T.RS, 4 + j, 512)), (T.PBN[:, 64:192], half(T.RS, 6 + j, 512))], rsk(128, 256), True, False)
-
-    def mix_y(j):
-        mix(2 * j, [(T.PB1[:], half(T.GL, j, 512))], ["r%d" % j], False, True)
-
-    def totals_out(q, h):
-        scaled(q, half(T.NF, h), B[3 + h][:, 0:128], math.exp(FAR), ["e%d" % h], ["NF%d" % h], [3 + h])
-
-    def last_pointers():
-        to_list(B[5][:, C:2 * C], 5, "own", E_PT, lambda k: T.W[:, k:K:16], wk_)
-
-    def last_offsets():
-        cp("v", T.OU[:], B[5][:, C:2 * C], ["own"], ["OU"], [5])
-
-    def store(q, b, out, okey, dst, j):
-        cp(q, half(out, j, 512), B[b][:], ["o%d" % b], [okey], [b])
-        dma("s", half(dst, j, 512), half(out, j, 512), [okey], [])
-
-    def pair(out, old, win, wk, off, ok, c0, key, first):
-        a, z_ = out[:, 16 * c0:16 * c0 + 512], out[:, 16 * c0 + 1024:16 * c0 + 1536]
-        if first:
-            cp(first, z_, win.indirect(off[:, c0 + 64:c0 + 96]), wk + [ok], [key + "z", old % (c0 // 32 + 2)])
-        else:
-            tt(a, win.indirect(off[:, c0:c0 + 32]), z_, OP.subtract, wk + [ok, key + "z"], [key, old % (c0 // 32)])
-
-    def pair_y(j, e, first=None):
-        pair(T.OC, "OC%d", T.P[:, Y0:PEND], wall_keys(STEPS + 1), T.OU, "OU", 128 * e + 32 * j, "y%d%d" % (j, e), first)
-
-    def pair_r(j, first=None):
-        win, wk = rec_window(STEPS)
-        pair(T.GL, "GL%d", win, wk, T.RU, "RU0", 32 * j, "r%d" % j, first)
+    def turn(t, *quarters):
+        for i in quarters:
+            a, sb = rs(t) + H + 1024 * i, vs(t) + 1024 * i
+            dma("s", T.P[16:128, a:a + 1024], T.P[0:112, sb:sb + 1024], ["SB%d%d" % (t, i)], ["R%d1%d" % (t, 2 * i)])
+            dma("s", T.P[0:16, a:a + 1024], T.P[112:128, sb:sb + 1024], ["SB%d%d" % (t, i)], ["R%d1%d" % (t, 2 * i + 1)])
 
     for t in range(1, STEPS + 1):
         last = t == STEPS
-        n0 = (t - 1) * C
 
-        def nu(c0, c1):
-            return T.NU[:, n0 + c0:n0 + c1]
-
-        def glk(c0, c1):
-            return ["GL%d" % c for c in range(c0 // 32, c1 // 32)]
-
-        def look(q, c0, c1):
-            scaled(q, T.GL[:, 16 * c0:16 * c1], T.W[:].indirect(nu(c0, c1)), T.PF[:, 7:8] if c0 >= 128 else 1.0,
-                   ["NU%d%d" % (t, c0 // 128), "MK"] + wk_, glk(c0, c1))
-
-        def scatter_x():
-            tt(T.W[:].indirect(nu(128, C)), half(T.GL, 1, H), T.CX[:], OP.add, ["NU%d1" % t, "CX"] + glk(128, C), wk_)
-
-        def scatter_y():
-            act(T.WY[:].indirect(nu(0, 128)), T.CY[:], AF.Sigmoid, ["NU%d0" % t, "CY"], ["WY"])
-
-        def flags_y():
-            if last:
-                need("g", ["TY"], [])
-            else:
-                dma("g", row(T.W, R_FY), row(T.WY, R_FY), ["WY"], wk_)
-
-        def cells_out(i, u=t):
-            if i < 2:
-                send(half(T.P, 2 * u - 2 + i, 1024), half(T.RS, i, 1024), aide, ("ra%d", "rd%d")[i] % u, rsk(64 * i, 64 * i + 64))
-            else:
-                send(half(T.SB, 2 * u - 6 + i, 1024), half(T.RS, i, 1024), peer(1), ("rb%d", "rc%d")[i - 2] % u, rsk(64 * i, 64 * i + 64))
-
-        def owners_x():
-            to_list(B[5][:, C:2 * C], 5, "own", E_ID, lambda k: half(T.W, k, C), wk_, (half(T.KB, t - 1, C),))
-
-        def owners_y():
-            dma("s", T.TY[:], row(T.WY, R_FY), ["WY"], ["TY", "TYa"])
+        def look(q, h, part=(0, 4)):
+            c0, c1 = span(h, part)
+            cp(q, T.GL[:, 16 * c0:16 * c1], T.W[:].indirect(nu(t, c0, c1)), ["NU%d%d" % (t, h)] + wk_, pieces("GL", c0, c1))
 
         def pointers():
-            x = B[5][:, C:2 * C]
-            return [lambda: tt(T.OF[:], x, T.OF[:], OP.max, ["own", "OF"], ["OF"], [5]),
-                    lambda: ts(T.DI[:], T.TY[:], 65536.0, t * U - 32768.0, OP.mult, OP.add, ["TY"], ["DI"]),
-                    lambda: tt(T.OF[:], T.DI[:], T.OF[:], OP.max, ["DI", "OF"], ["OF"]),
-                    lambda: cp("a", half(T.DB, 0, C), T.OF[:], ["OF"], ["DBa"]),
-                    lambda: mm([(x, T.PBF[:, 0:128], T.OF[:], True, False), (x, T.PBM[:], half(T.DB, 0, C), False, True)],
-                               ["OF", "DBa", "PBF", "PBM"], ["own"], [5]),
-                    lambda: cp("a", half(T.DB, 1, C), x, ["own"], ["DBb"], [5])]
+            di = [half(T.DI, i, C) for i in range(2)]
+            at = [vs(t) + H * (lead(t) if i == 0 else 1 - lead(t)) - CODE / 2 for i in range(2)]
+            return [lambda: ts(di[1], half(T.TT, 1, C), CODE, at[1], OP.mult, OP.add, ["TT1"], ["DI1", "NIa", "NIb", "NIc"]),
+                    lambda: tt(xp, xp, di[1], OP.max, ["xp", "DI1"], ["xp"], [4]),
+                    lambda: ts(di[0], half(T.TT, 0, C), CODE, at[0], OP.mult, OP.add, ["TT0"], ["DI0", "DN"]),
+                    lambda: tt(xp, xp, di[0], OP.max, ["xp", "DI0"], ["xp"], [4])] + parts(xp, ["xp"], R_PT, ["Wp", "Wq"], [4])
 
-        def new_table():
-            need("s", [], wk_)
-            dma("s", row(T.W, R_PT), half(T.DB, 0, C), ["DBa"], ["Wa"])
-            dma("s", row(T.W, R_PT + 1), half(T.DB, 1, C), ["DBb"], ["Wb"])
-            if not last:
-                dma("s", row(T.W, R_FX), T.CX[5:128:8, :], ["CX"], ["Wc"])
-                dma("s", row(T.WY, R_FY), T.CY[1:128:8, :], ["CY"], ["WY"])
+        def lb_(h):
+            return 5 if h == lead(t) else 2 + h
 
         def lists(h):
-            cols, gk = lambda k: T.GL[:, H * h + k:H * h + H:16], glk(128 * h, 128 * h + 128)
-            if t > 1:
-                to_list(B[5 - h][:, 128:256], 5 - h, "p%d" % h, E_PT, cols, gk)
-            if not last:
-                to_list(B[5 - h][:, 0:128], 5 - h, "d%d" % h, E_DN, cols, gk)
+            for e in range(2):
+                if (t > 1, not last)[e]:
+                    x = 144 * e + 15
+                    mm([(half(B[lb_(h)], e), T.EX[:, x - k:x - k + 128], T.GL[:, H * h + k:H * h + H:16], k == 0, k == 15) for k in range(16)],
+                       of("GL", h) + ["EX%d" % e], ["pd"[e] + str(h)], [lb_(h)])
+
+        def offsets(h):
+            a, z_ = 128 if t == 1 else 0, 128 if last else C
+            cp("v", T.PD[:, C * h + a:C * h + z_], B[lb_(h)][:, a:z_], (["p%d" % h] if t > 1 else []) + ([] if last else ["d%d" % h]), ["PD%d" % h], [lb_(h)])
 
         def names_f(h):
-            if not last:
-                cp("v", half(T.NF, h), nu(128 * h, 128 * h + 128), ["NU%d%d" % (t, h)], ["NF%d" % h])
+            cp("v", half(T.NF, h), nu(t, 128 * h, 128 * h + 128), ["NU%d%d" % (t, h)], ["NF%d" % h])
 
-        def pointer_f(h):
-            if t == 1:
-                act(half(T.YJ, 2 * h), half(T.NF, h), idn, ["NF%d" % h], ["YP%d" % h], bias=float(U))
-            elif h:
-                ts(half(T.YJ, 2 * h), B[5 - h][:, 128:256], float(t * U), None, OP.add, None, ["p%d" % h], ["YP%d" % h], [5 - h])
-            else:
-                act(half(T.YJ, 2 * h), B[5 - h][:, 128:256], idn, ["p%d" % h], ["YP%d" % h], [5 - h], bias=float(t * U))
+        def stride(h):
+            tt(half(T.DS, h), half(B[lb_(h)], 1), half(T.NF, h), OP.subtract, ["d%d" % h, "NF%d" % h], ["DS%d" % h], [lb_(h)])
 
-        def pointer_u(h):
-            if t > 1:
-                cp("v", half(T.PU, h), B[5 - h][:, 128:256], ["p%d" % h], ["PU%d" % h], [5 - h])
-            if not last:
-                cp("v", half(T.DU, h), B[5 - h][:, 0:128], ["d%d" % h], ["DU%d" % h], [5 - h])
-
-        def open_main(h):
-            mm([(B[1 - h][:, 0:384], T.PB1[:], T.KM[:, 0:384], True, False), (B[3 - h][:, 0:C], T.PB1[:], T.KM[:, 512:768], True, False)],
-               ["PB1", "KM", "KMb"], ["M%d" % h, "S%d" % h], [1 - h, 3 - h])
-            if not last:
-                to_cells(1 - h, 2, T.TW[:, 72:80], half(T.GL, h, H), glk(128 * h, 128 * h + 128) + ["TW72"], ["M%d" % h])
-                mm([(B[1 - h][:, 256:384], half(T.NF, h), T.PBG[:], False, False)], ["NF%d" % h, "PBG"], ["M%d" % h], [1 - h])
+        def opened(h):
+            mm([(B[h][:], half(T.LK, h)[0:3 + t, :], T.RK[0:3 + t, 0:512], True, False)], ["LK", "RKa", "RKc"], ["M%d" % h], [h])
 
         def own_share(h):
-            to_cells(1 - h, 0, T.TW[:, 0:16], rec(t, h), rkeys(t, h) + ["TW0", "TW8"], ["M%d" % h])
-            to_cells(3 - h, 0, T.TW[:, 16:32], rec(t, h), rkeys(t, h) + ["TW16"], ["S%d" % h])
+            to_cells(h, 0, T.TW[:, 0:24], rec(t, h), rkeys(t, h) + ["TW0", "TW1", "TW2"], ["M%d" % h])
 
-        def both(h):
-            src, sk = (T.GX[:], ["GX0", "GX1"]) if h else (half(T.GL, 0, H), glk(0, 128))
-            to_cells(3 - h, 0, T.TW[:, 80 + 16 * h:96 + 16 * h], src, sk + ["TW80", "TW96"], ["S%d" % h])
+        def site_share(h, stop=False):
+            to_cells(h, 2, T.TW[:, 48 + 16 * h:64 + 16 * h], half(T.GL, h, H), of("GL", h) + ["TW%d" % (6 + 2 * h), "TW%d" % (7 + 2 * h)], ["M%d" % h], False, stop)
 
-        def look_x(q, i):
-            cp(q, half(T.GX, i, 1024), T.WY[:].indirect(nu(128 + 64 * i, 192 + 64 * i)), ["NU%d1" % t, "WY"], ["GX%d" % i])
+        def turned(h, src, key, start):
+            mm([(half(B[4], h), T.PBF[:, 112 * h:112 * h + 128], half(src, h), start, not start)], ["PBF", key + str(h)], ["nm%d" % h], [4])
 
-        def taken(c0, c1):
-            cp("a", T.OC[:, 16 * c0:16 * c1], T.W[:].indirect(T.DU[:, c0:c1]), ["DU%d" % (c0 // 128)] + wk_, ["OC%d" % c for c in range(c0 // 32, c1 // 32)])
+        def taken(q, h, part=(0, 4)):
+            c0, c1 = span(h, part)
+            need(q, [], ["RS%d" % (2 * h), "RS%d" % (2 * h + 1)])
+            cp(q, T.RS[:, 16 * c0:16 * c1], T.W[:].indirect(T.PD[:, 128 * (h + 1) + c0:128 * (h + 1) + c1]), ["PD%d" % h] + wk_, pieces("RQ", c0, c1))
 
         def taken_mm(h):
-            mm([(B[6 + h][:, 256:384], T.PB1[:], T.KM[:, 0:128], True, False)], ["PB1", "KM"], ["oc%d" % h], [6 + h])
-            to_cells(6 + h, 2, T.TW[:, 112:120], half(T.OC, h, H), ["OC%d" % c for c in range(4 * h, 4 * h + 4)] + ["TW112"], ["oc%d" % h], True)
+            to_cells(2 + h, 2, T.TW[:, 88:96], half(T.RS, h, H), of("RQ", h) + ["TW11"], ["oc%d" % h], True)
 
-        def d_gather(c0, c1):
-            h, a = c0 // 128, zs(t) + 128
-            off, ok = (nu(c0, c1), "NU1%d" % h) if t == 1 else (T.PU[:, c0:c1], "PU%d" % h)
-            n, q0, q1 = len(rkeys(t, h)) // 2, c0 // 64 % 2, (c1 - 1) // 64 % 2
-            tt(T.D[:, 16 * c0:16 * c1], T.P[:, Y0:Y0 + (t - 1) * U + K].indirect(off), T.P[:, a + 16 * c0:a + 16 * c1], OP.subtract,
-               wall_keys(t) + rkeys(t, h)[n * q0:n * q1 + n] + [ok], ["D%d" % c for c in range(c0 // 16, c1 // 16)])
+        def d_gather(h, part=(0, 4)):
+            c0, c1 = span(h, part)
+            if t == 1:
+                win, keys = T.P[:, Y0:Y0 + K].indirect(nu(t, c0, c1)), ["Y0", "NU1%d" % h]
+            else:
+                win, keys = pool(t, 0)
+                win, keys = win.indirect(T.PD[:, 128 * h + c0:128 * h + c1]), keys + ["PD%d" % h]
+            n, q0, q1 = len(rkeys(t, h)) // 2, part[0] // 2, (part[1] - 1) // 2
+            a = K * (t % 2)
+            tt(T.D[:, a + 16 * c0:a + 16 * c1], win, T.P[:, rs(t) + 16 * c0:rs(t) + 16 * c1], OP.subtract,
+               keys + rkeys(t, h)[n * q0:n * q1 + n], pieces("D%d_" % (t % 2), c0, c1))
 
         def d_pass(h):
-            to_cells(3 - h, 1, T.TW[:, 64:72], half(T.D, h, H), dk(h) + ["TW64"], ["S%d" % h])
+            to_cells(2 + h, 3, T.TW[:, 80:88], dn_of(T.D, t, h), of("D%d_" % (t % 2), h) + ["TW10"], ["dd%d" % h], True)
 
-        def n_pass(h):
-            ts(half(T.NN, h, H), half(T.D, h, H), -1.0, 0.0, OP.mult, OP.max, dk(h), ["N%d" % h])
-            to_cells(1 - h, 0, T.TW[:, 32:48], half(T.NN, h, H), ["N%d" % h, "TW32", "TW40"], ["M%d" % h], True)
+        def n_make(q, h):
+            o, i, r, w = dn_of(T.NN, t, h), dn_of(T.D, t, h), of("D%d_" % (t % 2), h), of("N%d_" % (t % 2), h)
+            if q == "v":
+                ts(o, i, -1.0, 0.0, OP.mult, OP.max, r, w)
+            else:
+                act(o, i, AF.Relu, r, w, scale=-1.0)
 
-        def n_swap(h):
-            to_cells(3 - h, 0, T.TW[:, 48:64], half(T.NN, h, H), ["N%d" % h, "TW40", "TW56"], ["S%d" % h])
+        def n_pass(h, stop=True):
+            to_cells(h, 0, T.TW[:, 24:48], dn_of(T.NN, t, h), of("N%d_" % (t % 2), h) + ["TW3", "TW4", "TW5"], ["M%d" % h], False, stop)
 
-        def bonds(h):
-            M, mk = B[1 - h], "M%d" % h
+        def flip(h, e, src, key):
+            mm([(half(B[2 + h], e), half(src, h), T.PB1[:], True, True)], [key + str(h), "PB1"], ["lm"[e] + str(h)], [2 + h])
+
+        def choices(h):
+            M, S, mk, n = B[h], B[2 + h], "M%d" % h, half(B[2 + h], 1)
+            k = lambda name: name + str(h)
+            ob = 6 if h == lead(t) else 5
+            O, ok = B[ob], "o%d" % ob
+            z1, z2, p1, q2 = half(T.ZZ, 2 * h), half(T.ZZ, 2 * h + 1), half(T.PQ, 2 * h), half(T.PQ, 2 * h + 1)
 
             def bond():
-                ts(half(T.BT, h), M[:, 0:128], 0.0, None, OP.is_gt, None, [mk], ["BT%d" % h], [1 - h])
-                mm([(B[6 + h][:, 0:128], half(T.BT, h), T.PB1[:], True, True)], ["BT%d" % h, "PB1"], ["x%d" % h], [6 + h])
-            return [bond, lambda: ts(half(T.RE, h), M[:, 128:256], -1.0 / 32, 0.0, OP.add, OP.max, [mk], ["RE%d" % h], [1 - h]),
-                    lambda: cp("v", half(T.BL, h), B[6 + h][:, 0:128], ["x%d" % h], ["BL%d" % h], [6 + h])]
+                ts(half(T.BT, h), half(M, 0), 0.0, None, OP.is_gt, None, [mk], [k("BT")], [h])
+                flip(h, 0, T.BT, "BT")
 
-        def holds(h):
-            F = half(T.FS, 6 + h) if last else half(T.FL, 2 * t - 2 + h)
-            n = B[1 - h][:, 128:256]
+            def excess():
+                ts(half(T.RE, h), half(M, 1), -1.0 / 32, 0.0, OP.add, OP.max, [mk], [k("RE")], [h])
+
+            def count():
+                cp("v", half(T.BL, h), half(S, 0), [k("l")], [k("BL")], [2 + h])
+                mm([(n, half(T.BL, h), T.BD[:], True, True)], [k("BL"), "BD"], [k("m")], [2 + h])
 
             def weakest():
-                tt(half(T.WM, h), B[1 - h][:, 0:128], half(T.RE, h), OP.subtract, ["M%d" % h, "RE%d" % h], ["WM%d" % h], [1 - h])
-                mm([(n, half(T.BL, h), T.BD[:], True, True)], ["BL%d" % h, "BD"], ["n%d" % h], [1 - h])
-            return [weakest, lambda: tt(n, n, half(T.WM, h), OP.mult, ["n%d" % h, "WM%d" % h], ["n%d" % h], [1 - h]),
-                    lambda: tt(half(T.NT, h), n, F, OP.is_le, ["n%d" % h, "F%d" % t], ["NT%d" % h], [1 - h])]
+                tt(half(T.WM, h), half(M, 0), half(T.RE, h), OP.subtract, [mk, k("RE")], [k("WM")], [h])
 
-        def bases(h):
-            mm([(B[5 - h][:, 0:256], T.PBF[:, 0:128], half(T.YJ, h, 256), True, False)], ["PBF", "YP%d" % h, "J%d" % h],
-               ["pY%d" % h, "d%d" % h, "p%d" % h], [5 - h])
-            if not last:
-                x = 112 if h else 0
-                mm([(B[7 - h][:, 128:256], T.PBF[:, x:x + 128], half(T.NF, h), True, False)], ["PBF", "NF%d" % h], ["x%d" % (1 - h)], [7 - h])
+            def strength():
+                tt(n, n, half(T.WM, h), OP.mult, [k("m"), k("WM")], [k("m")], [2 + h])
 
-        def moves(h):
-            def step():
-                a = 144 if h else 0
-                tt(T.TB[:, a:a + 128], B[1 - h][:, 256:384], half(T.WM, h), OP.mult, ["M%d" % h, "WM%d" % h, "TBz"], ["TB%d" % h], [1 - h])
-                o = B[7 - h][:, 128:256]
-                it = [(o, T.TB[:, 128:256], T.PBF[:, 0:128], False, False), (o, T.TB[:, 256:384], T.PBF[:, 0:128], False, True)] if h else \
-                    [(o, T.TB[:, 0:128], T.PBF[:, 0:128], False, True)]
-                mm(it, ["TB%d" % h, "PBF"], ["x%d" % (1 - h)], [7 - h])
-            return [lambda: tt(half(T.WM, h), half(T.NT, h), B[6 + h][:, 256:384], OP.is_gt, ["NT%d" % h, "oc%d" % h], ["WM%d" % h], [6 + h]), step]
+            def holds():
+                tt(half(T.HD, h), n, half(T.FL, 2 * t - 2 + h), OP.is_gt, [k("m"), "F%d" % t], [k("HD")], [2 + h])
+                mm([(half(O, 0), half(T.LK, 2 + h)[0:4, :], T.RK[0:4, 512:640], True, False)], ["LK", "RKb"], [ok], [ob])
 
-        def names_out(h):
-            cp("v", half(T.NS, h), B[7 - h][:, 128:256], ["x%d" % (1 - h)], ["NS%d" % h], [7 - h])
-            send(half(T.NU, 2 * t + h), half(T.NS, h), peer(1), ("ny%d", "nx%d")[h] % (t + 1), ["NS%d" % h])
+            def free():
+                tt(half(T.BT, h), half(T.HD, h), half(S, 2), OP.is_le, [k("HD"), k("oc")], [k("BT")], [2 + h])
+                flip(h, 0, T.BT, "BT")
 
-        def swaps(h):
-            S, sk = B[3 - h], "S%d" % h
-            mm([(S[:, 0:128], T.PB8[:], half(T.NT, h), False, False), (S[:, 128:256], T.PB8[:], half(T.NT, h), False, True)],
-               ["PB8", "NT%d" % h], [sk], [3 - h])
+            def moves():
+                tt(half(T.ST, h), half(S, 0), half(T.DS, h), OP.mult, [k("l"), k("DS")], [k("ST")], [2 + h])
+                turned(h, T.ST, "ST", False)
 
-        def swaps_add(h):
-            ts(half(T.ZZ, h, 256), B[3 - h][:, 0:C], -0.5, 0.0, OP.add, OP.max, ["S%d" % h], ["ZZ%d" % h], [3 - h])
-            it = []
-            for a in (128, 0):
-                o = B[5 - h][:, a:a + 128]
-                it += [(o, half(T.ZZ, 2 * h + 1), T.PZ1[:], False, False), (o, half(T.ZZ, 2 * h), T.PZ0[:], False, a == 0)]
-            mm(it, ["ZZ%d" % h, "PZ0", "PZ1"], ["pY%d" % h], [5 - h])
+            def names_out():
+                cp("v", half(T.NS, h), half(B[4], h), [k("nm")], [k("NS")], [4])
+                send(half(T.NU, 2 * t + h), half(T.NS, h), peer(1), ("ny%d", "nx%d")[h] % (t + 1), [k("NS")])
 
-        def mask_list(h):
-            mm([(B[1 - h][:, 0:128], half(T.NT, h), T.PB1[:], True, True)], ["NT%d" % h, "PB1"], ["M%d" % h], [1 - h])
+            def stays():
+                tt(z1, half(T.HD, h), half(M, 2), OP.is_ge, [k("HD"), mk], [k("Za")], [h])
 
-        def mask_keep(h):
-            cp("a", half(T.NH, h), B[1 - h][:, 0:128], ["M%d" % h], ["NH%d" % h], [1 - h])
+            def takes():
+                tt(z2, z1, half(S, 3), OP.is_le, [k("Za"), k("dd")], [k("Zb")], [2 + h])
+                mm([(half(O, 0), z1, T.PZ1[:], False, False), (half(O, 0), z2, T.PZ1[:], False, False)], [k("Za"), k("Zb"), "PZ1"], [ok], [ob])
 
-        def rec_lists(h):
-            return [lambda: tt(half(T.WM, h), B[5 - h][:, 128:256], half(T.YJ, 2 * h), OP.min, ["pY%d" % h, "YP%d" % h], ["WM%d" % h], [5 - h]),
-                    lambda: tt(half(T.RE, h), B[5 - h][:, 0:128], half(T.YJ, 2 * h + 1), OP.max, ["pY%d" % h, "J%d" % h], ["RE%d" % h], [5 - h]),
-                    lambda: ts(half(T.RU, h), half(T.WM, h), 0.0, None, OP.max, None, ["WM%d" % h], ["RU%d" % h]),
-                    lambda: ts(half(T.VU, h), half(T.RE, h), float((2 * t - 1) * U + K), None, OP.min, None, ["RE%d" % h], ["VU%d" % h])]
+            def keeps():
+                tt(q2, half(M, 3), z1, OP.mult, [mk, k("Za")], [k("PQb"), "PQ0", "PQ1"], [h])
+                mm([(half(O, 1), half(T.LK, 2 + h)[0:4, :], T.RK[0:4, 640:768], True, False), (half(O, 1), z2, T.PZ0[:], False, False),
+                    (half(O, 1), q2, T.PBF[:, 0:128], False, True)], [k("PQb"), k("Zb"), "PZ0", "PBF"], [ok], [ob])
 
-        if t == 1:
-            look("v", 128, 256)
-            scatter_y()
-            scatter_x()
-            look_x("a", 0)
-            lists(X_)
-            look_x("a", 1)
-            owners_x()
-            look("v", 0, 64)
-            look("a", 64, 128)
-            flags_y()
-            owners_y()
-            pulls()
-            pulls_out()
-            setup_late()
-            names_f(X_)
-            names_f(Y_)
-            pointer_u(X_)
-            pointer_f(X_)
-            open_main(X_)
-            lists(Y_)
-        else:
-            for i in range(2):
-                a, sb = zs(t) + 128 + H + 1024 * i, (t - 2) * H + 1024 * i
-                dma("s", T.P[16:128, a:a + 1024], T.SB[0:112, sb:sb + 1024], ["SB%d%d" % (t, i)], ["R%d1%d" % (t, 2 * i)])
-                dma("s", T.P[0:16, a:a + 1024], T.SB[112:128, sb:sb + 1024], ["SB%d%d" % (t, i)], ["R%d1%d" % (t, 2 * i + 1)])
-            look("a", 192, 256)
-            look("v", 128, 192)
-            exp_mm(Y_, 0, 6)
-            exp_mm(Y_, 1, 7)
-            exp_mm(Y_, 2, 0)
-            exp_mm(Y_, 3, 2)
-            lists(X_)
-            scatter_x()
-            gather_r("a", t - 1, 0, 64)
-            cells_out(0)
-            gather_r("a", t - 1, 64, 128)
-            cells_out(1)
-            exp_act(Y_, 0, 6)
-            exp_act(Y_, 3, 2)
-            scatter_y()
-            gather_v("a", t - 1, 0, 96)
-            owners_x()
-            pointer_u(X_)
-            exp_act(Y_, 1, 7)
-            names_f(X_)
-            names_f(Y_)
-            look("v", 0, 128)
-            exp_act(Y_, 2, 0)
-            owners_y()
-            flags_y()
-            fold_home(t - 1, Y_)
-            gather_v("v", t - 1, 128, 256)
-            gather_v("v", t - 1, 96, 128)
-            pointer_f(X_)
-            open_main(X_)
-            lists(Y_)
-            look_x("a", 0)
-            look_x("a", 1)
-        own_share(X_)
-        open_main(Y_)
-        both(Y_)
+            def reach():
+                tt(p1, half(M, 3), z2, OP.mult, [mk, k("Zb")], [k("PQa")], [h])
+                mm([(half(O, 0), p1, T.PBF[:, 0:128], False, True)], [k("PQa"), "PBF"], [ok], [ob])
+
+            def rec_lists(a=0, z_=2):
+                ts(T.RV[:, C * h + 128 * a:C * h + 128 * z_], O[:, 128 * a:128 * z_], float(2 * K * (t - 1)), None, OP.add, None, [ok],
+                   [k("RU"), k("VU")][a:z_], [ob])
+
+            def mask(q):
+                flip(h, 1, T.HD, "HD")
+                cp(q, half(T.NH, h), n, [k("m")], [k("NH")], [2 + h])
+                if last:
+                    terms.extend((t, h, j) for j in range(4))
+                elif h != lead(t):
+                    terms.extend((t, None, j) for j in range(8))
+            return [bond, excess, count, weakest, strength, holds], [free, moves, names_out], [stays, takes, reach, keeps, rec_lists], mask
+
+        L_, E_ = lead(t), 1 - lead(t)
         pt = pointers()
-        hx, hy = [bonds(h) + holds(h) + moves(h) for h in (X_, Y_)]
-        rx, ry = rec_lists(X_), rec_lists(Y_)
-        if not last:
-            d_gather(128, 192)
-            d_gather(192, 256)
-            n_pass(X_)
-            d_pass(X_)
-            hx[0]()
-            both(X_)
-            pointer_f(Y_)
-            taken(128, 192)
-            bases(X_)
-            pt[1]()
-            taken(192, 256)
-            pointer_u(Y_)
-            hx[1]()
+        (la, lb, lc, lmask), (ea, eb, ec, emask) = choices(L_), choices(E_)
+        if t == 1:
+            scatter("v", t)
+            scatter("a", t)
+            flags("a", t, "a")
+            flags("v", t)
+            need("g", ["WV", "WA"], [])
+            pull_out(1)
+            cells_out(0, 1, ["RS0"])
+            last_tables()
+            owners("a", t)
+            owners("v", t)
+            opened(L_)
+            opened(E_)
+            spread(range(5, 16))
+            names_f(L_)
+            names_f(E_)
+            d_gather(L_, (0, 2))
+            d_gather(L_, (2, 4))
+            own_share(L_)
+            d_pass(L_)
+            n_make("v", L_)
+            n_pass(L_, False)
+            look("v", L_, (0, 2))
+            look("a", L_, (2, 4))
+            lists(L_)
+            site_share(L_, True)
+            look("v", E_, (0, 2))
+            look("a", E_, (2, 4))
+            offsets(L_)
+            need("g", ["Wf0", "Wf1"], [])
+            pull_out(2)
+            pull_out(3)
+        else:
+            turn(t, *((1, 0) if L_ == X_ else (0,)))
+            look("a", L_)
+            scatter("v", t)
+            term_mm(2)
+            lists(L_)
+            term_act()
+            flags("v", t, "a")
+            opened(L_)
+            opened(E_)
+            term_act()
+            owners("a", t)
+            owners("v", t)
+            if E_ == X_:
+                turn(t, 1)
+            gather_v("v", t - 1, E_, (0, 3))
+            offsets(L_)
+            term_act()
+            need("g", rkeys(t, X_) + ["Wf%d" % L_], [])
+            fold_home(t - 1)
+            d_gather(L_, (2, 4))
+            site_share(L_)
+            own_share(L_)
+            d_gather(L_, (0, 2))
+            d_pass(L_)
+            n_make("v", L_)
+            n_pass(L_)
+            if not last:
+                names_f(L_)
+                names_f(E_)
+            look("a", E_)
+        if last:
             pt[0]()
-            n_swap(X_)
-            hx[2]()
-            hx[3]()
+            pt[1]()
+        else:
+            stride(L_)
+            turned(L_, T.NF, "NF", True)
+            taken("a", L_)
+        for f in la:
+            f()
+        lists(E_)
+        for f in lc[:4] + ([] if last else pt[:2]):
+            f()
+        offsets(E_)
+        if not last:
+            taken_mm(L_)
+            taken("a", E_)
+        lc[4]()
+        if last:
+            gather_v("a", t, L_)
+            mm([(B[4][:, 0:C], T.PB1[:], T.KM[:], True, False)], ["PB1", "KM"], ["e"], [4])
+            totals((1, 2))
+        d_gather(E_, (0, 1))
+        if not last:
+            lb[0]()
+            stride(E_)
+            lb[1]()
+        lmask("v")
+        if not last:
+            lb[2]()
+        own_share(E_)
+        site_share(E_)
+        d_gather(E_, (1, 4))
+        if last:
+            term_mm(4)
+        d_pass(E_)
+        n_make("v", E_)
+        n_pass(E_)
+        if not last:
             pt[2]()
-            hx[4]()
             pt[3]()
-            d_gather(0, 32)
-            hx[5]()
-            taken_mm(X_)
+            gather_r("a", t, L_)
+            cells_out(2 * L_, t + 1)
+            scatter("a", t + 1)
+            flags("a", t + 1, "a")
+            ea[0]()
+            ea[1]()
+            taken_mm(E_)
             pt[4]()
-            taken(0, 64)
-            swaps(X_)
-            pt[5]()
-            taken(64, 128)
-            new_table()
-            hx[6]()
-            hx[7]()
-            swaps_add(X_)
-            mask_list(X_)
-            d_gather(32, 64)
-            names_out(X_)
-            mask_keep(X_)
-            own_share(Y_)
-            rx[0]()
-            rx[1]()
-            rx[2]()
-            exp_mm(X_, 0, 0)
-            exp_mm(X_, 1, 2)
-            gather_r("a", t, 128, 192)
-            cells_out(2, t + 1)
-            d_gather(64, 128)
-            bases(Y_)
-            rx[3]()
-            d_pass(Y_)
-            n_pass(Y_)
-            exp_act(X_, 0, 0)
-            exp_act(X_, 1, 2)
-            taken_mm(Y_)
-            hy[0]()
-            n_swap(Y_)
-            hy[1]()
-            hy[2]()
-            hy[3]()
-            exp_mm(X_, 2, 0)
-            hy[4]()
-            exp_mm(X_, 3, 2)
-            hy[5]()
-            swaps(Y_)
-            gather_r("a", t, 192, 256)
-            hy[6]()
-            hy[7]()
-            swaps_add(Y_)
-            mask_list(Y_)
-            names_out(Y_)
-            exp_act(X_, 2, 0)
-            exp_act(X_, 3, 2)
-            fold_home(t, X_)
-            cells_out(3, t + 1)
-            ry[0]()
-            ry[1]()
-            ry[2]()
-            ry[3]()
-            mask_keep(Y_)
+            ea[2]()
+            ea[3]()
+            turned(E_, T.NF, "NF", True)
+            for f in (ea[4], ea[5], eb[0], ec[0], eb[1], ec[1], ec[2], pt[5], pt[6], eb[2]):
+                f()
+            ec[4](0, 1)
+            ec[3]()
+            gather_r("v", t, E_, (0, 2))
+            cells_out(2 * E_, t + 1)
+            emask("v")
+            ec[4](1, 2)
+            term_mm(6)
+            gather_v("a", t, L_, (3, 4))
+            gather_v("a", t, E_)
+            term_act()
+            gather_r("v", t, E_, (2, 4))
+            need("g", ["WA"], [])
+            cells_out(2 * E_ + 1, t + 1)
+            cells_out(2 * L_ + 1, t + 1)
             continue
 
-        d_gather(128, 192)
-        d_gather(192, 256)
-        d_pass(X_)
-        bases(X_)
-        n_pass(X_)
-        both(X_)
-        pointer_u(Y_)
-        pt[0]()
-        hx[0]()
-        pointer_f(Y_)
-        n_swap(X_)
-        hx[1]()
-        pt[1]()
-        hx[2]()
-        hx[3]()
-        pt[2]()
-        hx[4]()
-        pt[3]()
-        hx[5]()
-        swaps(X_)
-        mask_list(X_)
-        mask_keep(X_)
-        pt[4]()
-        pt[5]()
-        new_table()
-        swaps_add(X_)
-        exp_half(X_, 0, 0)
-        rx[1]()
-        rx[0]()
-        rx[3]()
-        rx[2]()
-        exp_half(X_, 1, 2)
-        own_share(Y_)
-        d_gather(0, 64)
-        gather_v("a", t, 128, 192)
-        exp_half(X_, 2, 0)
-        exp_half(X_, 3, 2)
-        d_gather(64, 128)
-        d_pass(Y_)
-        bases(Y_)
-        n_pass(Y_)
-        gather_v("a", t, 192, 256)
-        earlier(X_, (1, 2), True, False)
-        n_swap(Y_)
-        hy[1]()
-        hy[0]()
-        totals(X_, 0)
-        hy[2]()
-        hy[3]()
-        gather_r("a", t, 128, 192)
-        totals(X_, 1)
-        hy[4]()
-        hy[5]()
-        swaps(Y_)
-        mask_list(Y_)
-        swaps_add(Y_)
-        mask_keep(Y_)
-        exp_half(Y_, 0, 6)
-        ry[1]()
-        ry[0]()
-        ry[3]()
-        ry[2]()
-        exp_half(Y_, 1, 7)
-        last_pointers()
-        gather_v("v", t, 0, 64)
-        gather_v("a", t, 64, 128)
-        last_offsets()
-        exp_half(Y_, 2, 6)
-        exp_half(Y_, 3, 7)
-        gather_r("v", t, 192, 256)
-        totals(X_, 2)
-        totals(X_, 3)
-        earlier(X_, (3,), False, True)
-        earlier(Y_, (1, 2, 3), True, False)
-        pair_y(0, 0, "v")
-        pair_y(0, 1, "a")
-        pair_y(0, 0)
-        pair_y(1, 0, "a")
-        pair_y(0, 1)
-        pair_y(1, 1, "a")
-        totals(Y_, 0)
-        totals(Y_, 1)
-        mix_w(0)
-        mix_x(0)
-        mix_x(1)
-        totals(Y_, 2)
-        totals(Y_, 3, True)
-        pair_r(0, "a")
-        pair_y(1, 0)
-        pair_y(1, 1)
-        pair_r(1, "a")
-        pair_r(0)
-        pair_r(1)
-        mix_y(0)
-        store("a", 1, T.YW, "YW0", T.yw, 0)
-        mix_w(1)
-        mix_y(1)
-        totals_out("v", X_)
-        totals_out("v", Y_)
-        store("a", 0, T.YR, "YR0", T.yr, 0)
-        store("v", 2, T.YR, "YR1", T.yr, 1)
-        dma("a", T.ye[:], T.NF[:], ["NF0", "NF1"], [])
-        store("a", 5, T.YW, "YW1", T.yw, 1)
+        YW, YR = T.WV[:, 0:1024], T.WA[:, 0:1024]
+        weights = [(T.PB1, "PB1"), (T.PBM, "PBM"), (T.PB2, "PB2"), (T.PBN, "PBN")]
+
+        def wall(q, c0, c1):
+            win, wk = pool(STEPS + 1, 0)
+            cp(q, T.GL[:, 16 * c0:16 * c1], win.indirect(T.PD[:, c0:c1]), wk + ["PD0"], pieces("GL", c0, c1))
+
+        def wall_mm(c0, c1):
+            for j in range(2):
+                b = 1 + 2 * j
+                mm([(B[b][:, C * a + c0:C * a + c1], weights[i][0][:, 0:128], T.GL[:, 16 * c0 + 2 * j + a + 4 * i:16 * c1:16], i == 0, i == 3)
+                    for a in range(2) for i in range(4)], pieces("GL", c0, c1) + [w[1] for w in weights], ["o%d" % b], [b])
+
+        def cells(h, j):
+            mm([(B[2 * j][:], weights[i][0][:, 64 * h:64 * h + 128], half(T.RS, 2 * i + j, 512), i == 0, i == 3) for i in (2 * h, 2 * h + 1)],
+               ["RQ%d" % (2 * i + j) for i in (2 * h, 2 * h + 1)] + [w[1] for w in weights], ["o%d" % (2 * j)], [2 * j])
+
+        def store(q, b, out, okey, dst, j):
+            cp(q, half(out, j, 512), B[b][:], ["o%d" % b], [okey + str(j)], [b])
+            dma("s", half(dst, j, 512), half(out, j, 512), [okey + str(j)], [])
+
+        identities((("PBM", -1.0), ("PBN", -2.0)))
+        need("a", [], wk_)
+        term_act()
+        term_act(1)
+        term_act(1)
+        fold_home(t)
+        gather_r("a", t, L_)
+        for f in pt[2:4] + ea:
+            f()
+        emask("v")
+        ec[0]()
+        term_mm(1)
+        ec[1]()
+        ec[2]()
+        ec[3]()
+        term_mm(3)
+        cp("v", T.PD[:, 0:C], xp, ["xp"], ["PD0"], [4])
+        ec[4]()
+        term_act()
+        summed(E_, 0)
+        gather_v("v", t, E_, (0, 3))
+        gather_v("a", t, E_, (3, 4))
+        need("v", [], ["WV", "WA"])
+        need("a", [], ["WV", "WA"])
+        summed(E_, 1)
+        term_act(1)
+        term_act(1)
+        wall("v", 0, 64)
+        cells(L_, 0)
+        summed(E_, 2)
+        gather_r("a", t, E_)
+        wall("v", 64, 128)
+        cells(L_, 1)
+        wall_mm(0, 64)
+        summed(E_, 3)
+        wall("v", 128, 192)
+        wall_mm(64, 128)
+        totals((3,))
+        wall("v", 192, 256)
+        cells(E_, 0)
+        cells(E_, 1)
+        wall_mm(128, 192)
+        store("a", 0, YR, "YR", T.yr, 0)
+        store("a", 2, YR, "YR", T.yr, 1)
+        wall_mm(192, 256)
+        totals((4,))
+        store("v", 1, YW, "YW", T.yw, 0)
+        store("a", 3, YW, "YW", T.yw, 1)
+        ts(T.NF[:], B[4][:, 0:C], math.exp(FAR), None, OP.mult, None, ["e"], ["NF0", "NF1"], [4])
+        dma("s", T.ye[:], T.NF[:], ["NF0", "NF1"], [])
 
     for s, v in final.items():
         if all(seen[q].get(s, 0) < v for q in Q):

import math
from concourse.bass import DstId, RemoteDMATransfer
from concourse.mybir import AluOpType as OP, ActivationFunctionType as AF

K = 4096
H = 2048
C = 256
STEPS = 4
Y0 = 256
PEND = Y0 + 9 * K
Y_, X_ = 0, 1
BIG = 8192.0
LARGE = 65536.0
CODE = 81920.0
FAR = 20.0
ROUND = 1.5 * 2.0 ** 31
R_PT, R_DN, R_FLAG = 0, 1, (8, 12)
R_V, R_A = 2, 6

SCRATCH = {
    "P": ("sbuf", [128, PEND], "bfloat16"), "RS": ("sbuf", [128, K], "bfloat16"),
    "W": ("sbuf", [128, K], "float32"), "WV": ("sbuf", [128, K], "float32"), "WA": ("sbuf", [128, K], "float32"),
    "CS": ("sbuf", [128, H], "float32"),
    "D": ("sbuf", [128, 2 * K], "bfloat16"), "NN": ("sbuf", [128, 2 * K], "bfloat16"),
    "GL": ("sbuf", [128, K], "bfloat16"), "X": ("sbuf", [128, K], "float32"),
    "SEL": ("sbuf", [128, 16 * 128], "bfloat16"), "EX": ("sbuf", [128, 2 * 144], "bfloat16"),
    "TW": ("sbuf", [128, 96], "bfloat16"), "GM": ("sbuf", [128, 32], "bfloat16"), "BD": ("sbuf", [128, 128], "bfloat16"),
    "PBF": ("sbuf", [128, 256], "float32"), "PB1": ("sbuf", [128, 128], "bfloat16"), "PBM": ("sbuf", [128, 128], "bfloat16"),
    "PZ0": ("sbuf", [128, 128], "bfloat16"), "PZ1": ("sbuf", [128, 128], "bfloat16"),
    "PB2": ("sbuf", [128, 256], "bfloat16"), "PBN": ("sbuf", [128, 256], "bfloat16"),
    "KM": ("sbuf", [128, 256], "bfloat16"), "LK": ("sbuf", [128, 512], "bfloat16"), "RK": ("sbuf", [128, 768], "bfloat16"),
    "L": ("sbuf", [128, 256], "float32"), "XG": ("sbuf", [128, 256], "float32"), "ZF": ("sbuf", [128, 256], "float32"),
    "PI": ("sbuf", [128, 4], "int32"), "PF": ("sbuf", [128, 16], "float32"), "M16": ("sbuf", [128, 16], "float32"),
    "DI": ("sbuf", [128, 2 * C], "int32"), "TT": ("sbuf", [128, 2 * C], "float32"), "HL": ("sbuf", [128, 2 * C], "float32"),
    "PL": ("sbuf", [128, C], "int32"), "FL": ("sbuf", [128, 4 * C], "float32"), "EL": ("sbuf", [128, 4 * C], "float32"),
    "NU": ("sbuf", [128, 4 * C], "uint16"), "NS": ("sbuf", [128, C], "uint16"),
    "PD": ("sbuf", [128, 2 * C], "uint16"), "RV": ("sbuf", [128, 2 * C], "uint16"),
    "NF": ("sbuf", [128, C], "float32"), "RE": ("sbuf", [128, C], "float32"), "WM": ("sbuf", [128, C], "float32"),
    "DS": ("sbuf", [128, C], "float32"), "ST": ("sbuf", [128, C], "float32"), "PQ": ("sbuf", [128, 2 * C], "float32"),
    "BT": ("sbuf", [128, C], "bfloat16"), "BL": ("sbuf", [128, C], "bfloat16"),
    "HD": ("sbuf", [128, C], "bfloat16"), "NH": ("sbuf", [128, C], "bfloat16"), "ZZ": ("sbuf", [128, 2 * C], "bfloat16"),
}
for _b in range(4):
    SCRATCH["B%d" % _b] = ("psum", [128, 1024], "float32")

SEMAPHORES = (["qv", "qa", "qp", "qg"] + ["d%d" % i for i in range(70)] + ["l%d" % i for i in range(38)]
              + ["%s%d" % (n, t) for n in ("nx", "ny", "ra", "rb", "rc", "rd", "re") for t in range(1, 5)]
              + ["rf%d" % t for t in range(1, 4)])


def rs(t):
    return Y0 + (2 * t - 1) * K


def vs(t):
    return Y0 + 2 * t * K


def lead(t):
    return t % 2


def straight(u, i):
    return i % 2 == (u > 1)


def quarter(u, i):
    a = rs(u) + 1024 * i if i < 2 or u == 1 else vs(u) + 1024 * (i - 2)
    return a, ("ra%d", "rd%d", "rb%d", "rc%d")[i] % u


def rank_program(g, core, T, topo):
    rank = T.rank_of(core)
    cores = list(T.cores)
    n_ranks = len(cores)

    def helper(c):
        return [h for h in topo.cores_of(c) if h not in cores and topo.die(h) != topo.die(c)
                and all(topo.may_write(h, d) for d in cores)][0]

    def near(c):
        return [h for h in topo.cores_of(c) if h not in cores and topo.die(h) == topo.die(c)
                and all(topo.may_write(h, d) for d in cores)][0]

    def inner(c):
        far = set(e for d in cores if d != c for e in topo.engines(c, d))
        return [e for e in topo.engines(c, helper(c)) if e not in far]

    def half(buf, h, n=128):
        return buf[:, n * h:n * (h + 1)]

    def rec(t, i, n=H):
        return T.P[:, rs(t) + i * n:rs(t) + (i + 1) * n]

    if rank is None:
        for r, c in enumerate(cores):
            if core in (helper(c), near(c)):
                jobs = []
                for t in range(1, STEPS + 1):
                    if core == helper(c):
                        for i in (3, 1) if t == 1 else (2 - 2 * lead(t), 2 * lead(t)):
                            a, sem = quarter(t, i)
                            jobs.append(([sem], T.P[:, a:a + 1024], r + 1, inner(c)))
                    else:
                        buf = half(T.EL, t - 1, C) if t < STEPS else half(T.EL, 2 * t - 2 + lead(t))
                        jobs.append((["re%d" % t], buf, r - t, topo.engines(c, core)))
                total = 0
                for sems, buf, to, en in jobs:
                    dst = cores[to % n_ranks]
                    rid, pid, _ = topo.addr(dst)
                    for sem in sems:
                        g.wait_ge(T.sem[sem], len(en))
                    g.remote_dma(buf, buf, T.sem[sems[0]], T.sem.l0, pid, rid, topo.mask(core, dst))
                    total += len(topo.engines(core, dst))
                g.wait_ge(T.sem.l0, total)
        return
    aide = helper(core)
    aide_mask = sum(1 << e for e in inner(core))
    Q = {"v": g.vector, "a": g.scalar, "p": g.tensor, "g": g, "s": g.sync}
    cnt = {"v": 0, "a": 0, "p": 0, "g": 0, "d": 0, "l": 0}
    seen = {q: {} for q in Q}
    wr, rd, bank, final = {}, {}, {}, {}

    def need(q, reads, writes, banks=()):
        want = {}

        def add(tok):
            if tok is not None and not (q == "p" and tok[2] == "p"):
                want[tok[0]] = max(want.get(tok[0], 0), tok[1])
        for k in reads:
            add(wr[k])
        for k in writes:
            add(wr.get(k))
            for tok in rd.get(k, {}).values():
                add(tok)
        for b in banks:
            for e, tok in bank.get(b, {}).items():
                if e != q:
                    add(tok)
        for s, v in want.items():
            if seen[q].get(s, 0) < v:
                Q[q].wait_ge(T.sem[s], v)
                seen[q][s] = v

    def done(tok, reads, writes, banks=()):
        for k in reads:
            rd.setdefault(k, {})[tok[0]] = tok
        for k in writes:
            wr[k] = tok
            rd[k] = {}
        for b in banks:
            bank.setdefault(b, {})[tok[2]] = tok
        final[tok[0]] = tok[1]

    def op(q, fn, reads, writes, banks=()):
        need(q, reads, writes, banks)
        ins = fn()
        cnt[q] += 1
        ins.then_inc(T.sem["q" + q], 1)
        done(("q" + q, cnt[q], q), reads, writes, banks)

    def dma(q, out, in_, reads, writes):
        need(q, reads, writes)
        s = "d%d" % cnt["d"]
        cnt["d"] += 1
        Q[q].dma_start(out, in_).then_inc(T.sem[s], 16)
        done((s, 16, "d"), reads, writes)

    def peer(t):
        return cores[(rank + t) % n_ranks]

    def lsem():
        cnt["l"] += 1
        return "l%d" % (cnt["l"] - 1)

    def send(out, in_, dst, sem, reads):
        need("g", reads, [])
        s = lsem()
        rid, pid, _ = topo.addr(dst)
        g.remote_dma(out, in_, T.sem[sem], T.sem[s], pid, rid, aide_mask if dst == aide else topo.mask(core, dst))
        done((s, len(inner(core) if dst == aide else topo.engines(core, dst)), "r"), reads, [])

    def lands(sem, n, keys):
        done((sem, n, "r"), [], keys)

    def tt(out, a, b, o, reads, writes, banks=()):
        op("v", lambda: g.vector.tensor_tensor(out, a, b, o), reads, writes, banks)

    def ts(out, a, s1, s2, o0, o1, reads, writes, banks=()):
        if o1 is None:
            op("v", lambda: g.vector.tensor_scalar(out, a, s1, None, o0), reads, writes, banks)
        else:
            op("v", lambda: g.vector.tensor_scalar(out, a, s1, s2, o0, o1), reads, writes, banks)

    def cp(q, out, a, reads, writes, banks=()):
        if q == "v":
            op("v", lambda: g.vector.tensor_copy(out, a), reads, writes, banks)
        else:
            op("a", lambda: g.scalar.activation(out, a, AF.Copy), reads, writes, banks)

    def act(out, a, f, reads, writes, banks=(), **kw):
        op("a", lambda: g.scalar.activation(out, a, f, **kw), reads, writes, banks)

    def fill(ap, v, key):
        op("v", lambda: g.vector.memset(ap, v), [], [key])

    def iota(out, pat, base, cm, key):
        op("g", lambda: g.iota(out, pat, base, cm, allow_small_or_imprecise_dtypes=True), [], [key])

    def spot(out, in_, pat, v, base, reads, key):
        op("g", lambda: g.affine_select(out, in_, pat, OP.not_equal, v, base, 1), reads, [key])

    def only(ap, r, v, key):
        op("g", lambda: g.affine_select(ap, ap, [[0, ap.shape[1]]], OP.is_equal, v, -r, 1), [key], [key])

    def put(ap, r, v, key):
        spot(ap, ap, [[0, ap.shape[1]]], v, -r, [key], key)

    def mm(items, reads, writes, banks):
        def run():
            ins = None
            for it in items:
                ins = g.tensor.matmul(*it)
            return ins
        op("p", run, reads, writes, banks)

    B = [half(T["B%d" % (b // 2)], b % 2, 512) for b in range(8)]

    def to_cells(b, q0, w, src, skeys, keys, alone=False, stop=False):
        n = w.shape[1] // 8
        mm([(B[b][:, 128 * q0 + k:128 * (q0 + n):16], src[:, k:H:16], w, alone, alone or (stop and k == 15)) for k in range(16)], skeys, keys, [b])

    def row(buf, r):
        return buf[r:128:16, :]

    def pieces(name, c0, c1, n=32):
        return ["%s%d" % (name, c) for c in range(c0 // n, (c1 + n - 1) // n)]

    def of(name, h):
        return pieces(name, 128 * h, 128 * h + 128)

    src_n = len(topo.engines(peer(-1), core))
    lands("nx1", src_n, ["NU10", "NU11"])
    for t in range(1, STEPS + 1):
        lands("re%d" % t, len(topo.engines(near(peer(t)), core)), ["EL%d" % t])
        for i in range(4):
            n = src_n if straight(t, i) else len(topo.engines(helper(peer(-1)), core))
            lands(quarter(t, i)[1], n, ["R%d0%d" % (t, i)] if i < 2 else ["SB%d%d" % (t, i - 2)] if t > 1 else ["R11%d" % (2 * i - 4), "R11%d" % (2 * i - 3)])
        if t > 1:
            lands("ny%d" % t, src_n, ["NU%d0" % t])
            lands("nx%d" % t, src_n, ["NU%d1" % t])
        if t < STEPS:
            lands("rf%d" % t, len(topo.engines(peer(-t), core)), ["F%d" % t])

    xp = B[4][:, C:2 * C]
    wk_ = ["W", "W2", "Wp", "Wq", "Wd", "We", "Wf0", "Wf1"]

    def parts(src, reads, r, keys, banks=(), buf=T.HL, name="HL"):
        hi, lo = half(buf, 0, C), half(buf, 1, C)
        return [lambda: ts(hi, src, ROUND, -ROUND, OP.add, OP.add, reads, [name + "0"], banks),
                lambda: tt(lo, src, hi, OP.subtract, reads + [name + "0"], [name + "1"], banks),
                lambda: (need("s", [], keys), dma("s", row(T.W, r), hi, [name + "0"], keys[:1]),
                         dma("s", row(T.W, r + 4), lo, [name + "1"], keys[1:]))]

    tab = {"v": (T.WV, R_V, "WV", 0), "a": (T.WA, R_A, "WA", 1)}

    def clear(q, first=False):
        buf, r, key, _ = tab[q]
        if first:
            for i in range(2):
                dma("s", half(row(buf, r), i, H), row(T.CS, r + 9), ["CS"], [key + str(i)])
        else:
            dma("s", row(buf, r), row(T.W, r + 9), ["W", "W2"], [key])

    def cells_out(i, u, keys=None):
        a, sem = quarter(u, i)
        send(T.P[:, a:a + 1024], half(T.RS, i, 1024), peer(1) if straight(u, i) else aide, sem, keys or pieces("RQ", 64 * i, 64 * i + 64))

    NI = half(T.DI, 1, C)
    dma("s", NI[:, 0:128], T.nm[:, 0:128], [], ["NIa"])
    dma("a", NI[16:128, 128:256], T.nm[0:112, 128:256], [], ["NIb"])
    dma("s", NI[0:16, 128:256], T.nm[112:128, 128:256], [], ["NIc"])
    dma("a", half(T.DI, 0, C), T.dn[:], [], ["DN"])
    dma("a", T.PL[0:8, :], T.pl[:], [], ["PL"])
    dma("s", T.RS[16:128, H:K], T.rc[0:112, H:K], [], ["RS2"])
    dma("a", T.RS[0:16, H:K], T.rc[112:128, H:K], [], ["RS3"])
    dma("s", T.RS[:, 0:H], T.rc[:, 0:H], [], ["RS0", "RS1"])

    op("g", lambda: g.iota(T.PI[:, 0:1], [[0, 1]], 0, 1), [], ["PI0"])
    iota(T.L[:], [[1, 256]], 0, 0, "L")
    iota(T.XG[:], [[0, 2], [1, 8], [0, 16]], 0, 0, "XG")

    fill(T.GL[:, 0:H], 0.0, "GL0")
    fill(T.ZF[:], 0.0, "ZF")
    cp("a", T.CS[:], T.GL[:, 0:H], ["GL0"], ["CS"])
    act(half(T.W, 0, H), T.GL[:, 0:H], AF.Sigmoid, ["GL0"], ["W"], bias=-200.0)
    ts(T.PI[:, 1:2], T.PI[:, 0:1], 15, None, OP.bitwise_and, None, ["PI0"], ["PI1"])
    ts(T.PI[:, 2:3], T.PI[:, 0:1], 4, None, OP.arith_shift_right, None, ["PI0"], ["PI2"])
    fill(T.KM[:], 0.0, "KM")
    cp("v", T.PF[:, 0:3], T.PI[:, 0:3], ["PI0", "PI1", "PI2"], ["PF"])
    z, zz, zx = half(T.TT, 0), half(T.TT, 1), half(T.TT, 2)
    ts(T.PF[:, 6:7], T.PF[:, 1:2], 128.0, None, OP.mult, None, ["PF"], ["PF6"])
    ts(T.M16[:], T.L[:, 0:16], T.PF[:, 1:2], None, OP.is_equal, None, ["L", "PF"], ["M16"])
    ts(z, T.L[:, 0:128], T.PF[:, 6:7], 1.0 / CODE, OP.add, OP.mult, ["L", "PF6"], ["Z0"])
    ts(T.PF[:, 7:8], T.PF[:, 1:2], 256.0, float(Y0), OP.mult, OP.add, ["PF"], ["PF7"])
    tt(zz, z, z, OP.mult, ["Z0"], ["Z1"])
    ts(zx, z, 0.5, None, OP.add, None, ["Z0"], ["Z2"])
    ts(zz, zz, 16.0 / 3, 4.0, OP.mult, OP.add, ["Z1"], ["Z1"])
    cp("v", T.NS[:], NI, ["NIa", "NIb", "NIc"], ["NS0", "NS1"])
    send(T.NU[:, 0:C], T.NS[:], peer(1), "nx1", ["NS0", "NS1"])
    tt(zz, z, zz, OP.mult, ["Z0", "Z1"], ["Z1"])
    need("s", [], ["CS"])
    dma("s", row(T.CS, R_V), zx, ["Z2"], ["CSv"])
    dma("s", row(T.CS, R_A), zz, ["Z1"], ["CSa"])
    clear("v", True)
    clear("a", True)
    need("s", ["CSv", "CSa"], [])
    dma("s", T.P[:, Y0:Y0 + K], T.wl[:], [], ["Y0"])
    RB = T.RE[0:8, :]
    ts(RB, T.XG[0:8, :], T.PF[0:8, 0:1], None, OP.is_equal, None, ["XG", "PF"], ["RE0", "RE1"])
    for i, v in enumerate((1.0, -1.0, 1.0 / K, -1.0 / K)):
        ts(half(T.GM, i, 8), T.XG[:, 0:128:16], T.PF[:, 2:3], v, OP.is_equal, OP.mult, ["XG", "PF"], ["GM%d" % i])
    ts(T.WM[0:8, :], T.PL[0:8, :], -0.25, 0.0, OP.add, OP.max, ["PL"], ["WM0", "WM1"])
    fill(half(T.W, 1, H), 0.0, "W2")
    first = [parts(half(T.DI, 0, C), ["DN"], R_DN, ["Wd", "We"], (), T.PQ, "PQ"), parts(xp, ["xp"], R_PT, ["Wp", "Wq"], [4])]
    ts(xp, T.L[:], T.PF[:, 7:8], None, OP.add, None, ["L", "PF7"], ["xp"], [4])
    for i in range(3):
        if i == 2:
            need("s", [], ["W", "W2"])
        for f in first:
            f[i]()

    def pulls():
        FS = T.X[:, 0:4 * C]
        for j in range(2):
            it = []
            for t in (2 * j + 1, 2 * j + 2):
                a = (t - 1) % 2 * C
                it.append((B[6 + j][:, a:a + 128], T.WM[0:8, 0:128], RB[:, 128:256], True, True))
                it.append((B[6 + j][:, a + 128:a + C], T.WM[0:8, 128:256], RB[:, 128 - 16 * t:256 - 16 * t], True, True))
            mm(it, ["RE0", "RE1", "WM0", "WM1"], ["o%d" % (6 + j)], [6 + j])
        cp("a", FS[:, 0:512], B[6][:], ["o6"], ["X0"], [6])
        cp("a", FS[:, 512:768], B[7][:, 0:C], ["o7"], ["X1"], [7])
        cp("a", half(T.FL, 3, C), B[7][:, C:2 * C], ["o7"], ["F4"], [7])

    def pull_out(t):
        send(half(T.FL, t - 1, C), half(T.X, t - 1, C), peer(t), "rf%d" % t, ["X%d" % (t // 3)])

    def identities(names):
        for name, v in names:
            n = T[name].shape[1]
            spot(T[name][:], (T.ZF if name == "PBF" else T.KM)[:, 0:n], [[0, n // 128], [-1, 128]], v, 0, ["KM", "ZF"], name)

    for i in (3, 2, 1):
        cells_out(i, 1, (["RS%d" % i] if i < 2 else ["RS2", "RS3"]) + (["CSv", "CSa"] if straight(1, i) else []))
    for a, src, r, v in ((0, 0, 15, 0.0), (1, 0, 15, -16.0), (2, 2, 15, -16.0 / K), (3, 1, 15, 0.0), (4, 1, 15, 16.0), (5, 3, 15, 16.0 / K),
                         (6, None, R_FLAG[X_], -4.0), (7, None, R_PT, 1.0), (7, -1, R_PT + 4, 1.0), (8, None, R_FLAG[Y_], -4.0),
                         (9, None, R_PT, 1.0), (9, -1, R_PT + 4, 1.0), (10, None, 15, -1.0 / 512), (11, None, R_FLAG[0], -4.0), (11, -1, R_FLAG[1], -4.0)):
        in_, key = (T.KM[:, 0:8], "KM") if src is None else (half(T.TW, a, 8), "TW%d" % a) if src < 0 else (half(T.GM, src, 8), "GM%d" % src)
        spot(half(T.TW, a, 8), in_, [[-16, 8]], v, -r, [key], "TW%d" % a)
    pulls()
    iota(T.LK[0:7, 0:C], [[0, 2], [16, 128]], 0, 0, "LK")
    iota(T.LK[0:7, C:2 * C], [[0, 16], [1, 16]], 0, 0, "LK")
    only(T.LK[0:7, :], 2, 1.0, "LK")
    put(T.LK[0:7, 0:128], 3, 0.0, "LK")
    put(T.LK[0:7, C:C + 128], 3, 0.0, "LK")
    own = T.RK[0:7, 384:512]
    iota(own, [[0, 8], [-1, 16]], 0, 0, "RKa")
    only(own, 1, -2.0 * K, "RKa")
    for r, v in ((0, -rs(1)), (2, -1), (3, -H)):
        put(own, r, float(v), "RKa")
    identities((("PB1", 1.0), ("PBF", 1.0)))

    def last_tables():
        iota(T.RK[0:4, 512:768], [[0, 2], [16, 128]], 0, 0, "RKb")
        only(T.RK[0:4, 512:768], 1, 1.0, "RKb")
        put(T.RK[0:4, 512:768], 3, float(H), "RKb")
        put(T.RK[0:4, 512:640], 0, rs(1) - LARGE, "RKb")
        put(T.RK[0:4, 640:768], 0, float(rs(1)), "RKb")
        identities((("PZ1", LARGE), ("PZ0", -LARGE), ("PB2", 2.0)))

    wr["Wf0"] = wr["Wf1"] = None
    ts(T.PF[:, 3:4], T.PF[:, 2:3], 16.0, 15.0, OP.mult, OP.add, ["PF"], ["PF3"])
    tt(T.PF[:, 4:6], T.M16[:, 0:2], T.M16[:, 4:6], OP.add, ["M16"], ["PF4"])
    fill(T.RK[0:7, 0:384], 0.0, "RKc")
    fill(T.P[:, 0:Y0], 0.0, "Z")
    for e in range(2):
        ts(T.EX[:, 144 * e:144 * e + 144], T.L[:, 0:144], T.PF[:, 3:4], T.PF[:, 4 + e:5 + e], OP.is_equal, OP.mult, ["L", "PF3", "PF4"], ["EX%d" % e])
    ts(T.BD[:], T.XG[:, 0:128], T.PF[:, 2:3], None, OP.is_equal, None, ["XG", "PF"], ["BD"])
    ts(T.M16[:], T.M16[:], -BIG, None, OP.mult, None, ["M16"], ["M16"])

    def spread(ks):
        for k in ks:
            act(half(T.SEL, k), T.BD[:], AF.Identity, ["BD", "M16"], ["SEL%d" % k], scale=T.M16[:, k:k + 1])

    spread(range(5))

    def rkeys(t, h):
        return ["R%d1%d" % (t, i) for i in range(4)] if h else ["R%d00" % t, "R%d01" % t]

    def pool(t, r):
        keys = ["Z", "Y0"] + [k for u in range(1, t + r) for k in rkeys(u, 0) + rkeys(u, 1)]
        keys += [k for u in range(1, t) for k in pieces("V%d_" % u, 0, C)]
        return T.P[:, 0:(vs(t) if r else rs(t))], keys

    def span(h, part):
        return 128 * h + 32 * part[0], 128 * h + 32 * part[1]

    def gather_r(q, t, h, part=(0, 4)):
        c0, c1 = span(h, part)
        win, wk = pool(t, 1)
        need(q, [], ["RS%d" % (2 * h), "RS%d" % (2 * h + 1)])
        cp(q, T.RS[:, 16 * c0:16 * c1], win.indirect(T.RV[:, 128 * h + c0:128 * h + c1]), wk + ["RU%d" % h], pieces("RQ", c0, c1))

    def gather_v(q, t, h, part=(0, 4)):
        c0, c1 = span(h, part)
        win, wk = pool(t, 1)
        sb = ["SB%d%d" % (t, i) for i in range(2)] if t > 1 and h == 0 else []
        cp(q, T.P[:, vs(t) + 16 * c0:vs(t) + 16 * c1], win.indirect(T.RV[:, 128 * h + 128 + c0:128 * h + 128 + c1]), wk + ["VU%d" % h],
           pieces("V%d_" % t, c0, c1) + sb)

    def dn_of(buf, t, h):
        return half(buf, 2 * (t % 2) + h, H)

    def nu(t, c0, c1):
        return T.NU[:, (t - 1) * C + c0:(t - 1) * C + c1]

    def scatter(q, t):
        h = lead(t) if q == "v" else 1 - lead(t)
        buf, r, key, _ = tab[q]
        out, keys = buf[:].indirect(nu(t, 128 * h, 128 * h + 128)), ["NU%d%d" % (t, h), "CS", "CSv", "CSa", key + "0", key + "1"]
        if q == "v":
            cp("v", out, T.CS[:], keys, [key])
        else:
            act(out, T.CS[:], AF.Sigmoid, keys, [key])

    def flags(q, t, by="s"):
        h = lead(t) if q == "v" else 1 - lead(t)
        buf, r, key, i = tab[q]
        dma(by, row(T.W, R_FLAG[h]), row(buf, r), [key, "W", "W2"], ["Wf%d" % h])

    def owners(q, t):
        buf, r, key, i = tab[q]
        dma("s", half(T.TT, i, C), row(buf, r), [key], ["TT%d" % i] + (["Z2"] if i else ["Z0", "Z1"]))
        if t < STEPS:
            clear(q)

    terms, made = [], [0, 0]

    def term_bank(i):
        return (6, 7, 0, 2)[i % 4] if i >= 8 * (STEPS - 1) else (6, 7, 0, 1, 2, 3, 6, 7)[i % 8]

    def term_mm(n=1):
        for _ in range(n):
            t, h, j = terms[made[0]]
            b = term_bank(made[0])
            made[0] += 1
            it, hs = [], (0, 1) if h is None else (h,)
            for kk in range(4):
                k, o = (2 * j + kk // 2 if len(hs) == 2 else 4 * j + kk), half(B[b], kk)
                h = hs[kk % len(hs)]
                it += [(o, T.PB1[:], dn_of(T.D, t, h)[:, k:H:16], True, False), (o, T.PB2[:, 0:128], dn_of(T.NN, t, h)[:, k:H:16], False, False),
                       (o, half(T.SEL, k), half(T.NH, h), False, True)]
            mm(it, ["PB1", "PB2"] + ["SEL%d" % k for k in range(16)]
               + [k for h in hs for k in ["NH%d" % h] + of("D%d_" % (t % 2), h) + of("N%d_" % (t % 2), h)], ["o%d" % b], [b])

    def term_buf(t):
        return (T.W, "XL%d") if t == STEPS else (T.X, "X%d")

    def term_act(n=2):
        t, h, j = terms[made[1]]
        b = term_bank(made[1])
        made[1] += n
        x = j if h is None else 4 * (h != lead(t)) + j
        buf, key = term_buf(t)
        act(buf[:, 512 * x:512 * (x + n)], T["B%d" % (b // 2)][:, 512 * (b % 2):512 * (b % 2 + n)], AF.Sigmoid, ["o%d" % (b + i) for i in range(n)],
            [key % (x + i) for i in range(n)], [b + i for i in range(n)], scale=-1.0 / 64, bias=-FAR - BIG / 64)

    def fold_home(t):
        buf, key = term_buf(t)
        n, dst = (C, half(T.EL, t - 1, C)) if t < STEPS else (128, half(T.EL, 2 * t - 2 + lead(t)))
        keys = [key % j for j in range(n // 32)]
        need("g", keys, [])
        rid, pid, _ = topo.addr(near(core))
        s = lsem()
        g.remote_dma_fused([RemoteDMATransfer(dst_ids=[DstId(rid=rid, pnc=pid)], dma_engine_mask=topo.mask(core, near(core)), remote_sem=T.sem["re%d" % t],
                                              srcs=[half(buf, k, n) for k in range(16)], dsts=[dst], alu_op=1)], local_sem=T.sem[s])
        done((s, len(topo.engines(core, near(core))), "r"), keys, [])

    def totals(us):
        mm([(half(B[4], h), T.PBF[:, 16 * u * h:16 * u * h + 128], half(T.EL, 2 * u - 2 + h), False, u == STEPS)
            for u in us for h in ((0, 1) if u < STEPS else (lead(u),))], ["PBF"] + ["EL%d" % u for u in us], ["e"], [4])

    def summed(h, j):
        mm([(half(B[4], h), T.PBF[:, 64 * h:64 * h + 128], half(T.W, 16 + 4 * j + kk), False, False) for kk in range(4)], ["PBF", "XL%d" % (4 + j)], ["e"], [4])

    def turn(t, *quarters):
        for i in quarters:
            a, sb = rs(t) + H + 1024 * i, vs(t) + 1024 * i
            dma("s", T.P[16:128, a:a + 1024], T.P[0:112, sb:sb + 1024], ["SB%d%d" % (t, i)], ["R%d1%d" % (t, 2 * i)])
            dma("s", T.P[0:16, a:a + 1024], T.P[112:128, sb:sb + 1024], ["SB%d%d" % (t, i)], ["R%d1%d" % (t, 2 * i + 1)])

    for t in range(1, STEPS + 1):
        last = t == STEPS

        def look(q, h, part=(0, 4)):
            c0, c1 = span(h, part)
            cp(q, T.GL[:, 16 * c0:16 * c1], T.W[:].indirect(nu(t, c0, c1)), ["NU%d%d" % (t, h)] + wk_, pieces("GL", c0, c1))

        def pointers():
            di = [half(T.DI, i, C) for i in range(2)]
            at = [vs(t) + H * (lead(t) if i == 0 else 1 - lead(t)) - CODE / 2 for i in range(2)]
            return [lambda: ts(di[1], half(T.TT, 1, C), CODE, at[1], OP.mult, OP.add, ["TT1"], ["DI1", "NIa", "NIb", "NIc"]),
                    lambda: tt(xp, xp, di[1], OP.max, ["xp", "DI1"], ["xp"], [4]),
                    lambda: ts(di[0], half(T.TT, 0, C), CODE, at[0], OP.mult, OP.add, ["TT0"], ["DI0", "DN"]),
                    lambda: tt(xp, xp, di[0], OP.max, ["xp", "DI0"], ["xp"], [4])] + parts(xp, ["xp"], R_PT, ["Wp", "Wq"], [4])

        def lb_(h):
            return 5 if h == lead(t) else 2 + h

        def lists(h):
            for e in range(2):
                if (t > 1, not last)[e]:
                    x = 144 * e + 15
                    mm([(half(B[lb_(h)], e), T.EX[:, x - k:x - k + 128], T.GL[:, H * h + k:H * h + H:16], k == 0, k == 15) for k in range(16)],
                       of("GL", h) + ["EX%d" % e], ["pd"[e] + str(h)], [lb_(h)])

        def offsets(h):
            a, z_ = 128 if t == 1 else 0, 128 if last else C
            cp("v", T.PD[:, C * h + a:C * h + z_], B[lb_(h)][:, a:z_], (["p%d" % h] if t > 1 else []) + ([] if last else ["d%d" % h]), ["PD%d" % h], [lb_(h)])

        def names_f(h):
            cp("v", half(T.NF, h), nu(t, 128 * h, 128 * h + 128), ["NU%d%d" % (t, h)], ["NF%d" % h])

        def stride(h):
            tt(half(T.DS, h), half(B[lb_(h)], 1), half(T.NF, h), OP.subtract, ["d%d" % h, "NF%d" % h], ["DS%d" % h], [lb_(h)])

        def opened(h):
            mm([(B[h][:], half(T.LK, h)[0:3 + t, :], T.RK[0:3 + t, 0:512], True, False)], ["LK", "RKa", "RKc"], ["M%d" % h], [h])

        def own_share(h):
            to_cells(h, 0, T.TW[:, 0:24], rec(t, h), rkeys(t, h) + ["TW0", "TW1", "TW2"], ["M%d" % h])

        def site_share(h, stop=False):
            to_cells(h, 2, T.TW[:, 48 + 16 * h:64 + 16 * h], half(T.GL, h, H), of("GL", h) + ["TW%d" % (6 + 2 * h), "TW%d" % (7 + 2 * h)], ["M%d" % h], False, stop)

        def turned(h, src, key, start):
            mm([(half(B[4], h), T.PBF[:, 112 * h:112 * h + 128], half(src, h), start, not start)], ["PBF", key + str(h)], ["nm%d" % h], [4])

        def taken(q, h, part=(0, 4)):
            c0, c1 = span(h, part)
            need(q, [], ["RS%d" % (2 * h), "RS%d" % (2 * h + 1)])
            cp(q, T.RS[:, 16 * c0:16 * c1], T.W[:].indirect(T.PD[:, 128 * (h + 1) + c0:128 * (h + 1) + c1]), ["PD%d" % h] + wk_, pieces("RQ", c0, c1))

        def taken_mm(h):
            to_cells(2 + h, 2, T.TW[:, 88:96], half(T.RS, h, H), of("RQ", h) + ["TW11"], ["oc%d" % h], True)

        def d_gather(h, part=(0, 4)):
            c0, c1 = span(h, part)
            if t == 1:
                win, keys = T.P[:, Y0:Y0 + K].indirect(nu(t, c0, c1)), ["Y0", "NU1%d" % h]
            else:
                win, keys = pool(t, 0)
                win, keys = win.indirect(T.PD[:, 128 * h + c0:128 * h + c1]), keys + ["PD%d" % h]
            n, q0, q1 = len(rkeys(t, h)) // 2, part[0] // 2, (part[1] - 1) // 2
            a = K * (t % 2)
            tt(T.D[:, a + 16 * c0:a + 16 * c1], win, T.P[:, rs(t) + 16 * c0:rs(t) + 16 * c1], OP.subtract,
               keys + rkeys(t, h)[n * q0:n * q1 + n], pieces("D%d_" % (t % 2), c0, c1))

        def d_pass(h):
            to_cells(2 + h, 3, T.TW[:, 80:88], dn_of(T.D, t, h), of("D%d_" % (t % 2), h) + ["TW10"], ["dd%d" % h], True)

        def n_make(q, h):
            o, i, r, w = dn_of(T.NN, t, h), dn_of(T.D, t, h), of("D%d_" % (t % 2), h), of("N%d_" % (t % 2), h)
            if q == "v":
                ts(o, i, -1.0, 0.0, OP.mult, OP.max, r, w)
            else:
                act(o, i, AF.Relu, r, w, scale=-1.0)

        def n_pass(h, stop=True):
            to_cells(h, 0, T.TW[:, 24:48], dn_of(T.NN, t, h), of("N%d_" % (t % 2), h) + ["TW3", "TW4", "TW5"], ["M%d" % h], False, stop)

        def flip(h, e, src, key):
            mm([(half(B[2 + h], e), half(src, h), T.PB1[:], True, True)], [key + str(h), "PB1"], ["lm"[e] + str(h)], [2 + h])

        def choices(h):
            M, S, mk, n = B[h], B[2 + h], "M%d" % h, half(B[2 + h], 1)
            k = lambda name: name + str(h)
            ob = 6 if h == lead(t) else 5
            O, ok = B[ob], "o%d" % ob
            z1, z2, p1, q2 = half(T.ZZ, 2 * h), half(T.ZZ, 2 * h + 1), half(T.PQ, 2 * h), half(T.PQ, 2 * h + 1)

            def bond():
                ts(half(T.BT, h), half(M, 0), 0.0, None, OP.is_gt, None, [mk], [k("BT")], [h])
                flip(h, 0, T.BT, "BT")

            def excess():
                ts(half(T.RE, h), half(M, 1), -1.0 / 32, 0.0, OP.add, OP.max, [mk], [k("RE")], [h])

            def count():
                cp("v", half(T.BL, h), half(S, 0), [k("l")], [k("BL")], [2 + h])
                mm([(n, half(T.BL, h), T.BD[:], True, True)], [k("BL"), "BD"], [k("m")], [2 + h])

            def weakest():
                tt(half(T.WM, h), half(M, 0), half(T.RE, h), OP.subtract, [mk, k("RE")], [k("WM")], [h])

            def strength():
                tt(n, n, half(T.WM, h), OP.mult, [k("m"), k("WM")], [k("m")], [2 + h])

            def holds():
                tt(half(T.HD, h), n, half(T.FL, 2 * t - 2 + h), OP.is_gt, [k("m"), "F%d" % t], [k("HD")], [2 + h])
                mm([(half(O, 0), half(T.LK, 2 + h)[0:4, :], T.RK[0:4, 512:640], True, False)], ["LK", "RKb"], [ok], [ob])

            def free():
                tt(half(T.BT, h), half(T.HD, h), half(S, 2), OP.is_le, [k("HD"), k("oc")], [k("BT")], [2 + h])
                flip(h, 0, T.BT, "BT")

            def moves():
                tt(half(T.ST, h), half(S, 0), half(T.DS, h), OP.mult, [k("l"), k("DS")], [k("ST")], [2 + h])
                turned(h, T.ST, "ST", False)

            def names_out():
                cp("v", half(T.NS, h), half(B[4], h), [k("nm")], [k("NS")], [4])
                send(half(T.NU, 2 * t + h), half(T.NS, h), peer(1), ("ny%d", "nx%d")[h] % (t + 1), [k("NS")])

            def stays():
                tt(z1, half(T.HD, h), half(M, 2), OP.is_ge, [k("HD"), mk], [k("Za")], [h])

            def takes():
                tt(z2, z1, half(S, 3), OP.is_le, [k("Za"), k("dd")], [k("Zb")], [2 + h])
                mm([(half(O, 0), z1, T.PZ1[:], False, False), (half(O, 0), z2, T.PZ1[:], False, False)], [k("Za"), k("Zb"), "PZ1"], [ok], [ob])

            def keeps():
                tt(q2, half(M, 3), z1, OP.mult, [mk, k("Za")], [k("PQb"), "PQ0", "PQ1"], [h])
                mm([(half(O, 1), half(T.LK, 2 + h)[0:4, :], T.RK[0:4, 640:768], True, False), (half(O, 1), z2, T.PZ0[:], False, False),
                    (half(O, 1), q2, T.PBF[:, 0:128], False, True)], [k("PQb"), k("Zb"), "PZ0", "PBF"], [ok], [ob])

            def reach():
                tt(p1, half(M, 3), z2, OP.mult, [mk, k("Zb")], [k("PQa")], [h])
                mm([(half(O, 0), p1, T.PBF[:, 0:128], False, True)], [k("PQa"), "PBF"], [ok], [ob])

            def rec_lists(a=0, z_=2):
                ts(T.RV[:, C * h + 128 * a:C * h + 128 * z_], O[:, 128 * a:128 * z_], float(2 * K * (t - 1)), None, OP.add, None, [ok],
                   [k("RU"), k("VU")][a:z_], [ob])

            def mask(q):
                flip(h, 1, T.HD, "HD")
                cp(q, half(T.NH, h), n, [k("m")], [k("NH")], [2 + h])
                if last:
                    terms.extend((t, h, j) for j in range(4))
                elif h != lead(t):
                    terms.extend((t, None, j) for j in range(8))
            return [bond, excess, count, weakest, strength, holds], [free, moves, names_out], [stays, takes, reach, keeps, rec_lists], mask

        L_, E_ = lead(t), 1 - lead(t)
        pt = pointers()
        (la, lb, lc, lmask), (ea, eb, ec, emask) = choices(L_), choices(E_)
        if t == 1:
            scatter("v", t)
            scatter("a", t)
            flags("a", t, "a")
            flags("v", t)
            need("g", ["WV", "WA"], [])
            pull_out(1)
            cells_out(0, 1, ["RS0"])
            last_tables()
            owners("a", t)
            owners("v", t)
            opened(L_)
            opened(E_)
            spread(range(5, 16))
            names_f(L_)
            names_f(E_)
            d_gather(L_, (0, 2))
            d_gather(L_, (2, 4))
            own_share(L_)
            d_pass(L_)
            n_make("v", L_)
            n_pass(L_, False)
            look("v", L_, (0, 2))
            look("a", L_, (2, 4))
            lists(L_)
            site_share(L_, True)
            look("v", E_, (0, 2))
            look("a", E_, (2, 4))
            offsets(L_)
            need("g", ["Wf0", "Wf1"], [])
            pull_out(2)
            pull_out(3)
        else:
            turn(t, *((1, 0) if L_ == X_ else (0,)))
            look("a", L_)
            scatter("v", t)
            term_mm(2)
            lists(L_)
            term_act()
            flags("v", t, "a")
            opened(L_)
            opened(E_)
            term_act()
            owners("a", t)
            owners("v", t)
            if E_ == X_:
                turn(t, 1)
            gather_v("v", t - 1, E_, (0, 3))
            offsets(L_)
            term_act()
            need("g", rkeys(t, X_) + ["Wf%d" % L_], [])
            fold_home(t - 1)
            d_gather(L_, (2, 4))
            site_share(L_)
            own_share(L_)
            d_gather(L_, (0, 2))
            d_pass(L_)
            n_make("v", L_)
            n_pass(L_)
            if not last:
                names_f(L_)
                names_f(E_)
            look("a", E_)
        if last:
            pt[0]()
            pt[1]()
        else:
            stride(L_)
            turned(L_, T.NF, "NF", True)
            taken("a", L_)
        for f in la:
            f()
        lists(E_)
        for f in lc[:4] + ([] if last else pt[:2]):
            f()
        offsets(E_)
        if not last:
            taken_mm(L_)
            taken("a", E_)
        lc[4]()
        if last:
            gather_v("a", t, L_)
            mm([(B[4][:, 0:C], T.PB1[:], T.KM[:], True, False)], ["PB1", "KM"], ["e"], [4])
            totals((1, 2))
        d_gather(E_, (0, 1))
        if not last:
            lb[0]()
            stride(E_)
            lb[1]()
        lmask("v")
        if not last:
            lb[2]()
        own_share(E_)
        site_share(E_)
        d_gather(E_, (1, 4))
        if last:
            term_mm(4)
        d_pass(E_)
        n_make("v", E_)
        n_pass(E_)
        if not last:
            pt[2]()
            pt[3]()
            gather_r("a", t, L_)
            cells_out(2 * L_, t + 1)
            scatter("a", t + 1)
            flags("a", t + 1, "a")
            ea[0]()
            ea[1]()
            taken_mm(E_)
            pt[4]()
            ea[2]()
            ea[3]()
            turned(E_, T.NF, "NF", True)
            for f in (ea[4], ea[5], eb[0], ec[0], eb[1], ec[1], ec[2], pt[5], pt[6], eb[2]):
                f()
            ec[4](0, 1)
            ec[3]()
            gather_r("v", t, E_, (0, 2))
            cells_out(2 * E_, t + 1)
            emask("v")
            ec[4](1, 2)
            term_mm(6)
            gather_v("a", t, L_, (3, 4))
            gather_v("a", t, E_)
            term_act()
            gather_r("v", t, E_, (2, 4))
            need("g", ["WA"], [])
            cells_out(2 * E_ + 1, t + 1)
            cells_out(2 * L_ + 1, t + 1)
            continue

        YW, YR = T.WV[:, 0:1024], T.WA[:, 0:1024]
        weights = [(T.PB1, "PB1"), (T.PBM, "PBM"), (T.PB2, "PB2"), (T.PBN, "PBN")]

        def wall(q, c0, c1):
            win, wk = pool(STEPS + 1, 0)
            cp(q, T.GL[:, 16 * c0:16 * c1], win.indirect(T.PD[:, c0:c1]), wk + ["PD0"], pieces("GL", c0, c1))

        def wall_mm(c0, c1):
            for j in range(2):
                b = 1 + 2 * j
                mm([(B[b][:, C * a + c0:C * a + c1], weights[i][0][:, 0:128], T.GL[:, 16 * c0 + 2 * j + a + 4 * i:16 * c1:16], i == 0, i == 3)
                    for a in range(2) for i in range(4)], pieces("GL", c0, c1) + [w[1] for w in weights], ["o%d" % b], [b])

        def cells(h, j):
            mm([(B[2 * j][:], weights[i][0][:, 64 * h:64 * h + 128], half(T.RS, 2 * i + j, 512), i == 0, i == 3) for i in (2 * h, 2 * h + 1)],
               ["RQ%d" % (2 * i + j) for i in (2 * h, 2 * h + 1)] + [w[1] for w in weights], ["o%d" % (2 * j)], [2 * j])

        def store(q, b, out, okey, dst, j):
            cp(q, half(out, j, 512), B[b][:], ["o%d" % b], [okey + str(j)], [b])
            dma("s", half(dst, j, 512), half(out, j, 512), [okey + str(j)], [])

        identities((("PBM", -1.0), ("PBN", -2.0)))
        need("a", [], wk_)
        term_act()
        term_act(1)
        term_act(1)
        fold_home(t)
        gather_r("a", t, L_)
        for f in pt[2:4] + ea:
            f()
        emask("v")
        ec[0]()
        term_mm(1)
        ec[1]()
        ec[2]()
        ec[3]()
        term_mm(3)
        cp("v", T.PD[:, 0:C], xp, ["xp"], ["PD0"], [4])
        ec[4]()
        term_act()
        summed(E_, 0)
        gather_v("v", t, E_, (0, 3))
        gather_v("a", t, E_, (3, 4))
        need("v", [], ["WV", "WA"])
        need("a", [], ["WV", "WA"])
        summed(E_, 1)
        term_act(1)
        term_act(1)
        wall("v", 0, 64)
        cells(L_, 0)
        summed(E_, 2)
        gather_r("a", t, E_)
        wall("v", 64, 128)
        cells(L_, 1)
        wall_mm(0, 64)
        summed(E_, 3)
        wall("v", 128, 192)
        wall_mm(64, 128)
        totals((3,))
        wall("v", 192, 256)
        cells(E_, 0)
        cells(E_, 1)
        wall_mm(128, 192)
        store("a", 0, YR, "YR", T.yr, 0)
        store("a", 2, YR, "YR", T.yr, 1)
        wall_mm(192, 256)
        totals((4,))
        store("v", 1, YW, "YW", T.yw, 0)
        store("a", 3, YW, "YW", T.yw, 1)
        ts(T.NF[:], B[4][:, 0:C], math.exp(FAR), None, OP.mult, None, ["e"], ["NF0", "NF1"], [4])
        dma("s", T.ye[:], T.NF[:], ["NF0", "NF1"], [])

    for s, v in final.items():
        if all(seen[q].get(s, 0) < v for q in Q):
            g.wait_ge(T.sem[s], v)
